import numpy as np
import ml_dtypes


def mxq(x, axis, fmt="e4m3"):
    dtype, down = {"e4m3": (ml_dtypes.float8_e4m3fn, 7), "e5m2": (ml_dtypes.float8_e5m2, 14)}[fmt]
    v = np.moveaxis(np.asarray(x, np.float32).astype(ml_dtypes.bfloat16).astype(np.float64), axis, -1)
    blocks = v.reshape(v.shape[:-1] + (-1, 32))
    amax = np.abs(blocks).max(-1, keepdims=True)
    byte = np.maximum(np.where(amax > 0, np.frexp(amax)[1] - 1 + 127, 0) - down, 1)
    scale = np.exp2(byte - 127.0)
    codes = (blocks / scale).astype(np.float32).astype(dtype).astype(np.float64)
    return np.moveaxis((codes * scale).reshape(v.shape), -1, axis)


WIDE = False


def mx_kscale(k):
    if not WIDE:
        return np.ones(k)
    levels = np.array([24, -24, 12, -12, 0])
    if k % 512:
        return np.exp2(np.random.permutation(np.resize(levels, k // 32))).repeat(32)
    a = np.empty((k // 512, 16))
    for p in range(k // 512):
        a[p, :8] = np.random.permutation(np.resize(levels, 8))
        for g in range(8):
            far = levels[np.abs(levels - a[p, g]) >= 10]
            a[p, g + 8] = far[np.random.randint(len(far))]
    return np.exp2(a.ravel()).repeat(32)


def f64(x):
    return np.asarray(x).astype(np.float64)


def striped(idx):
    return np.tile(idx.reshape(-1, 16).T, (8, 1)).astype(np.uint16)


def unstriped(offs):
    return offs[:16].T.reshape(-1).astype(np.int64)


E2M1 = np.array([0.0, 0.5, 1.0, 1.5, 2.0, 3.0, 4.0, 6.0, -0.0, -0.5, -1.0, -1.5, -2.0, -3.0, -4.0, -6.0])


def pack_weight(w, fmt):
    k, n = w.shape
    w = f64(np.asarray(w, np.float32).astype(ml_dtypes.bfloat16)).reshape(k // 32, 32, n)
    amax = np.abs(w).max(1)
    if fmt == "e4m3":
        byte = np.frexp(amax)[1] - 1 + 127 - 7
    else:
        mant, ex = np.frexp(amax / 6.0)
        byte = np.where(mant > 0.5, ex, ex - 1) + 127
    byte = np.clip(np.where(amax > 0, byte, 1), 1, 254)
    scaled = (w * np.exp2(127.0 - byte)[:, None, :]).reshape(k, n).astype(np.float32)
    by_word = np.ascontiguousarray(scaled.reshape(k // 512, 128, 4, n).transpose(0, 1, 3, 2))
    if fmt == "e4m3":
        words = by_word.astype(ml_dtypes.float8_e4m3fn).view(np.uint8)
    else:
        c = by_word.astype(ml_dtypes.float4_e2m1fn).view(np.uint8) & 0xF
        words = (c[..., 0::2] | (c[..., 1::2] << 4)).reshape(k // 512, 128, 2 * n)
    return np.ascontiguousarray(words), np.ascontiguousarray(byte.astype(np.uint8).reshape(k // 512, 16, n))


def unpack_weight(words, scales, fmt):
    g, _, n = scales.shape
    words = np.ascontiguousarray(words).reshape(g, 128, n, -1)
    if fmt == "e4m3":
        vals = words.view(ml_dtypes.float8_e4m3fn).astype(np.float64)
    else:
        nib = np.empty((g, 128, n, 4), np.uint8)
        nib[..., 0::2] = words & 0xF
        nib[..., 1::2] = words >> 4
        vals = E2M1[nib]
    vals = vals * np.repeat(np.exp2(scales.astype(np.float64) - 127.0), 8, axis=1)[..., None]
    return vals.transpose(0, 1, 3, 2).reshape(g * 512, n)


def split(x):
    m, e = np.frexp(f64(x))
    hi = np.ldexp(np.trunc(16.0 * m) / 16.0, e)
    return hi, f64(x) - hi


K, L, N, T, J = 512, 1024, 512, 1024, 512


def setup_inputs():
    n = np.random.standard_normal
    s = mx_kscale(K)[:, None]
    s2 = mx_kscale(L)[:, None]
    p_tab = pack_weight(n((K, T)) * s, "e4m3")
    p_wx = pack_weight(n((L, N)) / np.sqrt(L) / s2, "e2m1")
    return {
        "tab_words": p_tab[0],
        "tab_scales": p_tab[1],
        "wt": (n((K, N)) / np.sqrt(K) / s).astype(np.float32),
        "x": (n((L, J)) * s2).astype(np.float32),
        "wx_words": p_wx[0],
        "wx_scales": p_wx[1],
        "gT": (n((N, T))).astype(np.float32),
        "offs": striped(np.random.permutation(T)[:J]),
    }


def reference(tab_words, tab_scales, wt, x, wx_words, wx_scales, gT, offs):
    idx = unstriped(offs)
    tab_ = unpack_weight(tab_words, tab_scales, "e4m3")[:, idx]
    wt_hi, wt_lo = split(wt)
    wt_hi_, wt_lo_ = mxq(wt_hi, 0, "e4m3"), mxq(wt_lo, 0, "e4m3")
    x_q_ = mxq(f64(x), 0, "e4m3")
    x_r_ = mxq(f64(x) - x_q_, 0, "e4m3")
    wx_ = unpack_weight(wx_words, wx_scales, "e2m1")
    y = wt_hi_.T @ tab_ + wt_lo_.T @ tab_ + wx_.T @ x_q_ + wx_.T @ x_r_
    return y * f64(gT)[:, idx]

@@ -1,0 +1,251 @@
+from contextlib import ExitStack
+
+import concourse.mybir as mybir
+from concourse.masks import make_identity
+
+K, L, N, T, J = 512, 1024, 512, 1024, 512
+FLOPS = 2 * (2 * K * N * J + 2 * L * N * J + L * 512 * J)
+
+F32 = mybir.dt.float32
+BF16 = mybir.dt.bfloat16
+I32 = mybir.dt.int32
+U32 = mybir.dt.uint32
+U16 = mybir.dt.uint16
+U8 = mybir.dt.uint8
+FP8X4 = mybir.dt.float8_e4m3fn_x4
+FP4X4 = mybir.dt.float4_e2m1fn_x4
+ALU = mybir.AluOpType
+
+P = 128
+PACK = 4
+K_PASS = P * PACK
+X_PASSES = L // K_PASS
+N_TILES = N // P
+J_HALF = J // 2
+HI_MASK = -983056
+
+
+def paired_rows(ap):
+    return ap.rearrange("p t (c i) -> p c t i", i=2)
+
+
+def paired_words(ap):
+    return ap.rearrange("p (c i) t -> p c t i", i=2)
+
+
+def tile_list_tiert_xhl_gate_kernel(
+    tc, tab_words, tab_scales, wt, x, wx_words, wx_scales, gT, offs, out
+):
+    nc = tc.nc
+    with ExitStack() as ctx:
+        keep = ctx.enter_context(tc.tile_pool(name="keep", bufs=1))
+        y_psum = ctx.enter_context(tc.psum_pool(name="y_psum", bufs=1))
+        back_psum = ctx.enter_context(tc.psum_pool(name="back_psum", bufs=4))
+
+        offsets = keep.tile([P, J // 16], U16, name="offsets")
+        nc.sync.dma_start(offsets[:], offs)
+
+        tab_s = keep.tile([P, T], U8, name="tab_s", align_bytes=64)
+        nc.vector.memset(tab_s[:].bitcast(I32), 0)
+        for q in range(4):
+            nc.scalar.dma_start(
+                tab_s[32 * q : 32 * q + 4, :].bitcast(I32), tab_scales[0, 4 * q : 4 * q + 4, :].bitcast(I32)
+            )
+
+        blocks = keep.tile([P, 2 * PACK - 1, P], BF16, name="blocks")
+        nc.gpsimd.memset(blocks[:].rearrange("p b m -> p (b m)"), 0.0)
+        make_identity(nc, blocks[:, PACK - 1, :], nomemset=True)
+        ident = keep.tile([P, PACK, P, PACK], BF16, name="ident", align_bytes=64)
+        ident_flat = ident[:].rearrange("p t m i -> p (t m i)")
+        for t in range(PACK):
+            nc.vector.tensor_copy(
+                ident[:, t].rearrange("p (c e) i -> p c i e", e=4),
+                blocks[:, PACK - 1 - t : 2 * PACK - 1 - t, :].rearrange("p i (c e) -> p c i e", e=4),
+            )
+        wx_s = keep.tile([P, X_PASSES, N], U8, name="wx_s", align_bytes=64)
+        nc.vector.memset(wx_s[:].rearrange("p a n -> p (a n)").bitcast(I32), 0)
+
+        x_raw = {}
+
+        def load_x(a, h):
+            x_raw[a, h] = keep.tile([P, PACK, J_HALF], F32, name=f"x_raw{a}{h}")
+            rows = x[a * K_PASS : (a + 1) * K_PASS, h * J_HALF : (h + 1) * J_HALF]
+            nc.sync.dma_start(x_raw[a, h][:], rows.rearrange("(p t) j -> p t j", t=PACK))
+
+        load_x(0, 0)
+        tab_w = keep.tile([P, T], I32, name="tab_w", align_bytes=64)
+        nc.sync.dma_start(tab_w[:], tab_words[0].rearrange("p t i -> p (t i)").bitcast(I32))
+        load_x(0, 1)
+        load_x(1, 0)
+        load_x(1, 1)
+        for q in range(4):
+            nc.sync.dma_start(
+                wx_s[32 * q : 32 * q + 4, :, :].bitcast(I32),
+                wx_scales[:, 4 * q : 4 * q + 4, :].rearrange("a r n -> r a n").bitcast(I32),
+            )
+        wx_w = keep.tile([P, X_PASSES, 2 * N], U8, name="wx_w", align_bytes=64)
+        nc.sync.dma_start(wx_w[:].bitcast(I32), wx_words.rearrange("a p b -> p a b").bitcast(I32))
+
+        wt_raw = []
+        gates = []
+
+        def load_wt(h):
+            raw = keep.tile([P, PACK, N // 2], F32, name=f"wt_raw{h}")
+            nc.sync.dma_start(raw[:], wt[:, h * (N // 2) : (h + 1) * (N // 2)].rearrange("(p t) n -> p t n", t=PACK))
+            wt_raw.append(raw)
+
+        def load_gate(nt):
+            g = keep.tile([P, T], F32, name=f"gate{nt}")
+            nc.sync.dma_start(g[:], gT[nt * P : (nt + 1) * P, :])
+            gates.append(g)
+
+        load_wt(0)
+        load_gate(0)
+        load_wt(1)
+        load_gate(1)
+        load_gate(2)
+        load_gate(3)
+
+        v_s = keep.tile([P, J], U8, name="v_s", align_bytes=64)
+        nc.vector.tensor_copy(v_s[:], tab_s[:].indirect(offsets[:]))
+        id_w = keep.tile([P, K_PASS], U32, name="id_w", align_bytes=64)
+        id_s = keep.tile([P, K_PASS], U8, name="id_s", align_bytes=64)
+        nc.vector.quantize_mx(out=id_w[:].bitcast(FP8X4), scales=id_s[:], in_=ident_flat)
+        v_w = keep.tile([P, J], U32, name="v_w", align_bytes=64)
+        nc.vector.tensor_copy(v_w[:], tab_w[:].bitcast(U32).indirect(offsets[:]))
+
+        xq_w = [keep.tile([P, J], U32, name=f"xq_w{a}", align_bytes=64) for a in range(X_PASSES)]
+        xq_s = [keep.tile([P, J], U8, name=f"xq_s{a}", align_bytes=64) for a in range(X_PASSES)]
+        xr_w = [keep.tile([P, J], U32, name=f"xr_w{a}", align_bytes=64) for a in range(X_PASSES)]
+        xr_s = [keep.tile([P, J], U8, name=f"xr_s{a}", align_bytes=64) for a in range(X_PASSES)]
+        rest = {}
+
+        def first_tier(a, h):
+            cols = slice(h * J_HALF, (h + 1) * J_HALF)
+            x_bf = keep.tile([P, J_HALF, PACK], BF16, name=f"x_bf{a}{h}", align_bytes=64)
+            nc.scalar.copy(paired_words(x_bf[:]), paired_rows(x_raw[a, h][:]))
+            nc.vector.quantize_mx(
+                out=xq_w[a][:, cols].bitcast(FP8X4), scales=xq_s[a][:, cols], in_=x_bf[:].rearrange("p j t -> p (j t)")
+            )
+
+        def left_over(a, h):
+            rest[a, h] = keep.tile([P, J_HALF, PACK], BF16, name=f"rest{a}{h}", align_bytes=64)
+            for u in range(J_HALF // P):
+                local = slice(u * P, (u + 1) * P)
+                cols = slice(h * J_HALF + u * P, h * J_HALF + (u + 1) * P)
+                back = back_psum.tile([P, PACK, P], F32, name="back")
+                for t in range(PACK):
+                    nc.tensor.matmul_mx(
+                        out=back[:, t, :],
+                        lhsT=id_w[:, t * P : (t + 1) * P].bitcast(FP8X4),
+                        lhsT_scale=id_s[:, t * P : (t + 1) * P],
+                        rhs=xq_w[a][:, cols].bitcast(FP8X4),
+                        rhs_scale=xq_s[a][:, cols],
+                        start=True,
+                        stop=True,
+                    )
+                nc.vector.tensor_tensor(
+                    paired_words(rest[a, h][:, local, :]),
+                    paired_rows(x_raw[a, h][:, :, local]),
+                    paired_rows(back[:]),
+                    ALU.subtract,
+                )
+
+        def second_tier(a, h):
+            cols = slice(h * J_HALF, (h + 1) * J_HALF)
+            nc.vector.quantize_mx(
+                out=xr_w[a][:, cols].bitcast(FP8X4),
+                scales=xr_s[a][:, cols],
+                in_=rest[a, h][:].rearrange("p j t -> p (j t)"),
+            )
+
+        chunks = [(a, h) for a in range(X_PASSES) for h in range(2)]
+        for step in range(len(chunks) + 2):
+            if step < len(chunks):
+                first_tier(*chunks[step])
+            if 2 <= step:
+                second_tier(*chunks[step - 2])
+            if 1 <= step <= len(chunks):
+                left_over(*chunks[step - 1])
+
+        y = [y_psum.tile([P, J], F32, name=f"y{nt}") for nt in range(N_TILES)]
+        for tier, (words, scales) in enumerate(((xq_w, xq_s), (xr_w, xr_s))):
+            for a in range(X_PASSES):
+                for nt in range(N_TILES):
+                    nc.tensor.matmul_mx(
+                        out=y[nt][:],
+                        lhsT=wx_w[:, a, 2 * P * nt : 2 * P * (nt + 1)].bitcast(FP4X4),
+                        lhsT_scale=wx_s[:, a, P * nt : P * (nt + 1)],
+                        rhs=words[a][:].bitcast(FP8X4),
+                        rhs_scale=scales[a][:],
+                        start=(tier == 0 and a == 0),
+                        stop=False,
+                    )
+
+        parts = {}
+
+        def split_hi(nt):
+            raw = wt_raw[nt // 2][:].bitcast(BF16).rearrange("p t (n e) -> p t n e", e=2)
+            local = slice((nt % 2) * P, (nt % 2 + 1) * P)
+            upper = keep.tile([P, P, PACK], BF16, name=f"upper{nt}", align_bytes=64)
+            nc.scalar.copy(paired_words(upper[:]), paired_rows(raw[:, :, local, 1]))
+            parts[nt] = keep.tile([P, 2, P, PACK], BF16, name=f"parts{nt}", align_bytes=64)
+            nc.vector.tensor_scalar(
+                parts[nt][:, 0].rearrange("p n t -> p (n t)").bitcast(I32),
+                upper[:].rearrange("p n t -> p (n t)").bitcast(I32),
+                HI_MASK,
+                None,
+                ALU.bitwise_and,
+            )
+
+        def split_lo(nt):
+            local = slice((nt % 2) * P, (nt % 2 + 1) * P)
+            nc.vector.tensor_tensor(
+                paired_words(parts[nt][:, 1]),
+                paired_rows(wt_raw[nt // 2][:, :, local]),
+                paired_words(parts[nt][:, 0]),
+                ALU.subtract,
+            )
+
+        sums = {}
+
+        def table_passes(nt):
+            w_w = keep.tile([P, 2 * P], U32, name=f"w_w{nt}", align_bytes=64)
+            w_s = keep.tile([P, 2 * P], U8, name=f"w_s{nt}", align_bytes=64)
+            nc.vector.quantize_mx(
+                out=w_w[:].bitcast(FP8X4), scales=w_s[:], in_=parts[nt][:].rearrange("p s n t -> p (s n t)")
+            )
+            for part in range(2):
+                nc.tensor.matmul_mx(
+                    out=y[nt][:],
+                    lhsT=w_w[:, part * P : (part + 1) * P].bitcast(FP8X4),
+                    lhsT_scale=w_s[:, part * P : (part + 1) * P],
+                    rhs=v_w[:].bitcast(FP8X4),
+                    rhs_scale=v_s[:],
+                    start=False,
+                    stop=(part == 1),
+                )
+            sums[nt] = keep.tile([P, J], F32, name=f"sums{nt}")
+            nc.scalar.copy(sums[nt][:], y[nt][:])
+
+        def gate_and_store(nt):
+            result = keep.tile([P, J], F32, name=f"result{nt}")
+            nc.vector.tensor_tensor(result[:], gates[nt][:].indirect(offsets[:]), sums[nt][:], ALU.mult)
+            nc.sync.dma_start(out[nt * P : (nt + 1) * P, :], result[:])
+
+        split_hi(0)
+        split_hi(1)
+        split_lo(0)
+        split_lo(1)
+        table_passes(0)
+        split_hi(2)
+        table_passes(1)
+        split_hi(3)
+        split_lo(2)
+        gate_and_store(0)
+        split_lo(3)
+        table_passes(2)
+        table_passes(3)
+        gate_and_store(1)
+        gate_and_store(2)
+        gate_and_store(3)

@@ -1,7 +1,6 @@
 from contextlib import ExitStack
 
 import concourse.mybir as mybir
-from concourse.masks import make_identity
 
 K, L, N, T, J = 512, 1024, 512, 1024, 512
 FLOPS = 2 * (2 * K * N * J + 2 * L * N * J + L * 512 * J)
@@ -22,6 +21,8 @@ K_PASS = P * PACK
 X_PASSES = L // K_PASS
 N_TILES = N // P
 J_HALF = J // 2
+N_HALF = N // 2
+X_CHUNKS = ((0, 0, P), (0, P, P), (0, J_HALF, J_HALF), (1, 0, J_HALF), (1, J_HALF, J_HALF))
 HI_MASK = -983056
 
 
@@ -39,213 +40,203 @@ def tile_list_tiert_xhl_gate_kernel(
     nc = tc.nc
     with ExitStack() as ctx:
         keep = ctx.enter_context(tc.tile_pool(name="keep", bufs=1))
+        woven = ctx.enter_context(tc.tile_pool(name="woven", bufs=2))
         y_psum = ctx.enter_context(tc.psum_pool(name="y_psum", bufs=1))
         back_psum = ctx.enter_context(tc.psum_pool(name="back_psum", bufs=4))
 
         offsets = keep.tile([P, J // 16], U16, name="offsets")
         nc.sync.dma_start(offsets[:], offs)
 
-        tab_s = keep.tile([P, T], U8, name="tab_s", align_bytes=64)
-        nc.vector.memset(tab_s[:].bitcast(I32), 0)
-        for q in range(4):
-            nc.scalar.dma_start(
-                tab_s[32 * q : 32 * q + 4, :].bitcast(I32), tab_scales[0, 4 * q : 4 * q + 4, :].bitcast(I32)
-            )
-
-        blocks = keep.tile([P, 2 * PACK - 1, P], BF16, name="blocks")
-        nc.gpsimd.memset(blocks[:].rearrange("p b m -> p (b m)"), 0.0)
-        make_identity(nc, blocks[:, PACK - 1, :], nomemset=True)
-        ident = keep.tile([P, PACK, P, PACK], BF16, name="ident", align_bytes=64)
-        ident_flat = ident[:].rearrange("p t m i -> p (t m i)")
-        for t in range(PACK):
-            nc.vector.tensor_copy(
-                ident[:, t].rearrange("p (c e) i -> p c i e", e=4),
-                blocks[:, PACK - 1 - t : 2 * PACK - 1 - t, :].rearrange("p i (c e) -> p c i e", e=4),
-            )
         wx_s = keep.tile([P, X_PASSES, N], U8, name="wx_s", align_bytes=64)
         nc.vector.memset(wx_s[:].rearrange("p a n -> p (a n)").bitcast(I32), 0)
+        tab_s = keep.tile([P, T], U8, name="tab_s", align_bytes=64)
+        nc.vector.memset(tab_s[:].bitcast(I32), 0)
 
-        x_raw = {}
+        ramp = woven.tile([P, K_PASS], BF16, name="ramp", tag="woven", align_bytes=64)
+        nc.gpsimd.iota(
+            ramp[:], pattern=[[1, K_PASS]], base=0, channel_multiplier=-PACK, allow_small_or_imprecise_dtypes=True
+        )
+        id_w = keep.tile([P, K_PASS], U32, name="id_w", align_bytes=64)
+        id_s = keep.tile([P, K_PASS], U8, name="id_s", align_bytes=64)
+        ident = (
+            woven.tile([P, 2, K_PASS], BF16, name="ident0", tag="woven", align_bytes=64),
+            keep.tile([P, 2, K_PASS], BF16, name="ident1", tag="v_w", align_bytes=64),
+        )
+        for t in range(PACK):
+            nc.vector.tensor_scalar(ident[t // 2][:, t % 2, :], ramp[:], float(t), None, ALU.is_equal)
+        for h in range(2):
+            cols = slice(h * 2 * P, (h + 1) * 2 * P)
+            nc.vector.quantize_mx(
+                out=id_w[:, cols].bitcast(FP8X4), scales=id_s[:, cols], in_=ident[h][:].rearrange("p t f -> p (t f)")
+            )
 
-        def load_x(a, h):
-            x_raw[a, h] = keep.tile([P, PACK, J_HALF], F32, name=f"x_raw{a}{h}")
-            rows = x[a * K_PASS : (a + 1) * K_PASS, h * J_HALF : (h + 1) * J_HALF]
-            nc.sync.dma_start(x_raw[a, h][:], rows.rearrange("(p t) j -> p t j", t=PACK))
-
-        load_x(0, 0)
         tab_w = keep.tile([P, T], I32, name="tab_w", align_bytes=64)
         nc.sync.dma_start(tab_w[:], tab_words[0].rearrange("p t i -> p (t i)").bitcast(I32))
-        load_x(0, 1)
-        load_x(1, 0)
-        load_x(1, 1)
+
+        x_raw = []
+        for c, (a, first, width) in enumerate(X_CHUNKS):
+            raw = keep.tile([P, PACK, width], F32, name=f"x_raw{c}")
+            rows = x[a * K_PASS : (a + 1) * K_PASS, first : first + width]
+            nc.sync.dma_start(raw[:], rows.rearrange("(p t) j -> p t j", t=PACK))
+            x_raw.append(raw)
+
+        wx_w = keep.tile([P, X_PASSES, 2 * N], U8, name="wx_w", align_bytes=64)
+        nc.sync.dma_start(wx_w[:].bitcast(I32), wx_words.rearrange("a p b -> p a b").bitcast(I32))
         for q in range(4):
             nc.sync.dma_start(
                 wx_s[32 * q : 32 * q + 4, :, :].bitcast(I32),
                 wx_scales[:, 4 * q : 4 * q + 4, :].rearrange("a r n -> r a n").bitcast(I32),
             )
-        wx_w = keep.tile([P, X_PASSES, 2 * N], U8, name="wx_w", align_bytes=64)
-        nc.sync.dma_start(wx_w[:].bitcast(I32), wx_words.rearrange("a p b -> p a b").bitcast(I32))
-
         wt_raw = []
-        gates = []
-
-        def load_wt(h):
-            raw = keep.tile([P, PACK, N // 2], F32, name=f"wt_raw{h}")
-            nc.sync.dma_start(raw[:], wt[:, h * (N // 2) : (h + 1) * (N // 2)].rearrange("(p t) n -> p t n", t=PACK))
+        for h in range(2):
+            raw = keep.tile([P, PACK, N_HALF], F32, name=f"wt_raw{h}")
+            nc.sync.dma_start(raw[:], wt[:, h * N_HALF : (h + 1) * N_HALF].rearrange("(p t) n -> p t n", t=PACK))
             wt_raw.append(raw)
+        gates = []
 
         def load_gate(nt):
             g = keep.tile([P, T], F32, name=f"gate{nt}")
             nc.sync.dma_start(g[:], gT[nt * P : (nt + 1) * P, :])
             gates.append(g)
 
-        load_wt(0)
         load_gate(0)
-        load_wt(1)
-        load_gate(1)
-        load_gate(2)
-        load_gate(3)
+        for q in range(4):
+            nc.sync.dma_start(
+                tab_s[32 * q : 32 * q + 4, :].bitcast(I32), tab_scales[0, 4 * q : 4 * q + 4, :].bitcast(I32)
+            )
+        for nt in range(1, N_TILES):
+            load_gate(nt)
 
-        v_s = keep.tile([P, J], U8, name="v_s", align_bytes=64)
-        nc.vector.tensor_copy(v_s[:], tab_s[:].indirect(offsets[:]))
-        id_w = keep.tile([P, K_PASS], U32, name="id_w", align_bytes=64)
-        id_s = keep.tile([P, K_PASS], U8, name="id_s", align_bytes=64)
-        nc.vector.quantize_mx(out=id_w[:].bitcast(FP8X4), scales=id_s[:], in_=ident_flat)
-        v_w = keep.tile([P, J], U32, name="v_w", align_bytes=64)
+        v_w = keep.tile([P, J], U32, name="v_w", tag="v_w", align_bytes=64)
         nc.vector.tensor_copy(v_w[:], tab_w[:].bitcast(U32).indirect(offsets[:]))
 
         xq_w = [keep.tile([P, J], U32, name=f"xq_w{a}", align_bytes=64) for a in range(X_PASSES)]
         xq_s = [keep.tile([P, J], U8, name=f"xq_s{a}", align_bytes=64) for a in range(X_PASSES)]
         xr_w = [keep.tile([P, J], U32, name=f"xr_w{a}", align_bytes=64) for a in range(X_PASSES)]
         xr_s = [keep.tile([P, J], U8, name=f"xr_s{a}", align_bytes=64) for a in range(X_PASSES)]
-        rest = {}
+        rest = [keep.tile([P, J, PACK], BF16, name=f"rest{a}", tag=f"rest{a}", align_bytes=64) for a in range(X_PASSES)]
+        back = {}
 
-        def first_tier(a, h):
-            cols = slice(h * J_HALF, (h + 1) * J_HALF)
-            x_bf = keep.tile([P, J_HALF, PACK], BF16, name=f"x_bf{a}{h}", align_bytes=64)
-            nc.scalar.copy(paired_words(x_bf[:]), paired_rows(x_raw[a, h][:]))
+        def quantize(words, scales, first, values):
+            cols = slice(first, first + values.shape[1])
             nc.vector.quantize_mx(
-                out=xq_w[a][:, cols].bitcast(FP8X4), scales=xq_s[a][:, cols], in_=x_bf[:].rearrange("p j t -> p (j t)")
+                out=words[:, cols].bitcast(FP8X4), scales=scales[:, cols], in_=values.rearrange("p j t -> p (j t)")
             )
 
-        def left_over(a, h):
-            rest[a, h] = keep.tile([P, J_HALF, PACK], BF16, name=f"rest{a}{h}", align_bytes=64)
-            for u in range(J_HALF // P):
-                local = slice(u * P, (u + 1) * P)
-                cols = slice(h * J_HALF + u * P, h * J_HALF + (u + 1) * P)
-                back = back_psum.tile([P, PACK, P], F32, name="back")
+        def first_tier(c):
+            a, first, width = X_CHUNKS[c]
+            x_bf = woven.tile([P, width, PACK], BF16, name=f"x_bf{c}", tag="woven", align_bytes=64)
+            nc.scalar.copy(paired_words(x_bf[:]), paired_rows(x_raw[c][:]))
+            quantize(xq_w[a], xq_s[a], first, x_bf[:])
+            for j0 in range(first, first + width, P):
+                back[a, j0] = back_psum.tile([P, PACK, P], F32, name="back")
                 for t in range(PACK):
                     nc.tensor.matmul_mx(
-                        out=back[:, t, :],
+                        out=back[a, j0][:, t, :],
                         lhsT=id_w[:, t * P : (t + 1) * P].bitcast(FP8X4),
                         lhsT_scale=id_s[:, t * P : (t + 1) * P],
-                        rhs=xq_w[a][:, cols].bitcast(FP8X4),
-                        rhs_scale=xq_s[a][:, cols],
+                        rhs=xq_w[a][:, j0 : j0 + P].bitcast(FP8X4),
+                        rhs_scale=xq_s[a][:, j0 : j0 + P],
                         start=True,
                         stop=True,
                     )
+
+        def left_over(c):
+            a, first, width = X_CHUNKS[c]
+            for j0 in range(first, first + width, P):
                 nc.vector.tensor_tensor(
-                    paired_words(rest[a, h][:, local, :]),
-                    paired_rows(x_raw[a, h][:, :, local]),
-                    paired_rows(back[:]),
+                    paired_words(rest[a][:, j0 : j0 + P, :]),
+                    paired_rows(x_raw[c][:, :, j0 - first : j0 - first + P]),
+                    paired_rows(back[a, j0][:]),
                     ALU.subtract,
                 )
 
-        def second_tier(a, h):
-            cols = slice(h * J_HALF, (h + 1) * J_HALF)
-            nc.vector.quantize_mx(
-                out=xr_w[a][:, cols].bitcast(FP8X4),
-                scales=xr_s[a][:, cols],
-                in_=rest[a, h][:].rearrange("p j t -> p (j t)"),
-            )
+        def second_tier(a, first, width):
+            quantize(xr_w[a], xr_s[a], first, rest[a][:, first : first + width, :])
 
-        chunks = [(a, h) for a in range(X_PASSES) for h in range(2)]
-        for step in range(len(chunks) + 2):
-            if step < len(chunks):
-                first_tier(*chunks[step])
-            if 2 <= step:
-                second_tier(*chunks[step - 2])
-            if 1 <= step <= len(chunks):
-                left_over(*chunks[step - 1])
-
-        y = [y_psum.tile([P, J], F32, name=f"y{nt}") for nt in range(N_TILES)]
-        for tier, (words, scales) in enumerate(((xq_w, xq_s), (xr_w, xr_s))):
-            for a in range(X_PASSES):
-                for nt in range(N_TILES):
-                    nc.tensor.matmul_mx(
-                        out=y[nt][:],
-                        lhsT=wx_w[:, a, 2 * P * nt : 2 * P * (nt + 1)].bitcast(FP4X4),
-                        lhsT_scale=wx_s[:, a, P * nt : P * (nt + 1)],
-                        rhs=words[a][:].bitcast(FP8X4),
-                        rhs_scale=scales[a][:],
-                        start=(tier == 0 and a == 0),
-                        stop=False,
-                    )
+        first_tier(0)
+        first_tier(1)
+        left_over(0)
+        left_over(1)
+        first_tier(2)
+        second_tier(0, 0, J_HALF)
+        left_over(2)
+        first_tier(3)
+        first_tier(4)
+        second_tier(0, J_HALF, J_HALF)
+        left_over(3)
+        left_over(4)
 
         parts = {}
 
-        def split_hi(nt):
-            raw = wt_raw[nt // 2][:].bitcast(BF16).rearrange("p t (n e) -> p t n e", e=2)
-            local = slice((nt % 2) * P, (nt % 2 + 1) * P)
-            upper = keep.tile([P, P, PACK], BF16, name=f"upper{nt}", align_bytes=64)
-            nc.scalar.copy(paired_words(upper[:]), paired_rows(raw[:, :, local, 1]))
-            parts[nt] = keep.tile([P, 2, P, PACK], BF16, name=f"parts{nt}", align_bytes=64)
+        def split_hi(h):
+            halves = wt_raw[h][:].bitcast(BF16).rearrange("p t (n e) -> p t n e", e=2)
+            upper = woven.tile([P, N_HALF, PACK], BF16, name=f"upper{h}", tag="woven", align_bytes=64)
+            nc.scalar.copy(paired_words(upper[:]), paired_rows(halves[:, :, :, 1]))
+            parts[h] = keep.tile([P, 2, N_HALF, PACK], BF16, name=f"parts{h}", align_bytes=64)
             nc.vector.tensor_scalar(
-                parts[nt][:, 0].rearrange("p n t -> p (n t)").bitcast(I32),
+                parts[h][:, 0].rearrange("p n t -> p (n t)").bitcast(I32),
                 upper[:].rearrange("p n t -> p (n t)").bitcast(I32),
                 HI_MASK,
                 None,
                 ALU.bitwise_and,
             )
 
-        def split_lo(nt):
-            local = slice((nt % 2) * P, (nt % 2 + 1) * P)
+        def split_lo(h):
             nc.vector.tensor_tensor(
-                paired_words(parts[nt][:, 1]),
-                paired_rows(wt_raw[nt // 2][:, :, local]),
-                paired_words(parts[nt][:, 0]),
-                ALU.subtract,
+                paired_words(parts[h][:, 1]), paired_rows(wt_raw[h][:]), paired_words(parts[h][:, 0]), ALU.subtract
             )
+
+        split_hi(0)
+        second_tier(1, 0, J)
+
+        y = [y_psum.tile([P, J], F32, name=f"y{nt}") for nt in range(N_TILES)]
+        x_operands = ((1, xq_w, xq_s), (0, xq_w, xq_s), (0, xr_w, xr_s), (1, xr_w, xr_s))
+        for i, (a, words, scales) in enumerate(x_operands):
+            for nt in range(N_TILES):
+                nc.tensor.matmul_mx(
+                    out=y[nt][:],
+                    lhsT=wx_w[:, a, 2 * P * nt : 2 * P * (nt + 1)].bitcast(FP4X4),
+                    lhsT_scale=wx_s[:, a, P * nt : P * (nt + 1)],
+                    rhs=words[a][:].bitcast(FP8X4),
+                    rhs_scale=scales[a][:],
+                    start=(i == 0),
+                    stop=False,
+                )
 
         sums = {}
 
-        def table_passes(nt):
-            w_w = keep.tile([P, 2 * P], U32, name=f"w_w{nt}", align_bytes=64)
-            w_s = keep.tile([P, 2 * P], U8, name=f"w_s{nt}", align_bytes=64)
+        def table_passes(h):
+            w_w = keep.tile([P, 2, N_HALF], U32, name=f"w_w{h}", align_bytes=64)
+            w_s = keep.tile([P, 2, N_HALF], U8, name=f"w_s{h}", align_bytes=64)
             nc.vector.quantize_mx(
-                out=w_w[:].bitcast(FP8X4), scales=w_s[:], in_=parts[nt][:].rearrange("p s n t -> p (s n t)")
+                out=w_w[:].rearrange("p s n -> p (s n)").bitcast(FP8X4),
+                scales=w_s[:].rearrange("p s n -> p (s n)"),
+                in_=parts[h][:].rearrange("p s n t -> p (s n t)"),
             )
-            for part in range(2):
-                nc.tensor.matmul_mx(
-                    out=y[nt][:],
-                    lhsT=w_w[:, part * P : (part + 1) * P].bitcast(FP8X4),
-                    lhsT_scale=w_s[:, part * P : (part + 1) * P],
-                    rhs=v_w[:].bitcast(FP8X4),
-                    rhs_scale=v_s[:],
-                    start=False,
-                    stop=(part == 1),
-                )
-            sums[nt] = keep.tile([P, J], F32, name=f"sums{nt}")
-            nc.scalar.copy(sums[nt][:], y[nt][:])
+            for u in range(N_HALF // P):
+                nt = h * (N_HALF // P) + u
+                for part in range(2):
+                    nc.tensor.matmul_mx(
+                        out=y[nt][:],
+                        lhsT=w_w[:, part, u * P : (u + 1) * P].bitcast(FP8X4),
+                        lhsT_scale=w_s[:, part, u * P : (u + 1) * P],
+                        rhs=v_w[:].bitcast(FP8X4),
+                        rhs_scale=v_s[:],
+                        start=False,
+                        stop=(part == 1),
+                    )
+                sums[nt] = keep.tile([P, J], F32, name=f"sums{nt}")
+                nc.scalar.copy(sums[nt][:], y[nt][:])
 
-        def gate_and_store(nt):
+        split_lo(0)
+        v_s = keep.tile([P, J], U8, name="v_s", tag="rest1", align_bytes=64)
+        nc.vector.tensor_copy(v_s[:], tab_s[:].indirect(offsets[:]))
+        table_passes(0)
+        split_hi(1)
+        split_lo(1)
+        table_passes(1)
+        for nt in range(N_TILES):
             result = keep.tile([P, J], F32, name=f"result{nt}")
             nc.vector.tensor_tensor(result[:], gates[nt][:].indirect(offsets[:]), sums[nt][:], ALU.mult)
             nc.sync.dma_start(out[nt * P : (nt + 1) * P, :], result[:])
-
-        split_hi(0)
-        split_hi(1)
-        split_lo(0)
-        split_lo(1)
-        table_passes(0)
-        split_hi(2)
-        table_passes(1)
-        split_hi(3)
-        split_lo(2)
-        gate_and_store(0)
-        split_lo(3)
-        table_passes(2)
-        table_passes(3)
-        gate_and_store(1)
-        gate_and_store(2)
-        gate_and_store(3)

@@ -52,10 +52,12 @@ def tile_list_tiert_xhl_gate_kernel(
         tab_s = keep.tile([P, T], U8, name="tab_s", align_bytes=64)
         nc.vector.memset(tab_s[:].bitcast(I32), 0)
 
-        ramp = woven.tile([P, K_PASS], BF16, name="ramp", tag="woven", align_bytes=64)
+        ramp_f32 = keep.tile([P, K_PASS], F32, name="ramp_f32")
         nc.gpsimd.iota(
-            ramp[:], pattern=[[1, K_PASS]], base=0, channel_multiplier=-PACK, allow_small_or_imprecise_dtypes=True
+            ramp_f32[:], pattern=[[1, K_PASS]], base=0, channel_multiplier=-PACK, allow_small_or_imprecise_dtypes=True
         )
+        ramp = woven.tile([P, K_PASS], BF16, name="ramp", tag="woven", align_bytes=64)
+        nc.scalar.copy(ramp[:], ramp_f32[:])
         id_w = keep.tile([P, K_PASS], U32, name="id_w", align_bytes=64)
         id_s = keep.tile([P, K_PASS], U8, name="id_s", align_bytes=64)
         ident = (
@@ -70,15 +72,21 @@ def tile_list_tiert_xhl_gate_kernel(
                 out=id_w[:, cols].bitcast(FP8X4), scales=id_s[:, cols], in_=ident[h][:].rearrange("p t f -> p (t f)")
             )
 
-        tab_w = keep.tile([P, T], I32, name="tab_w", align_bytes=64)
-        nc.sync.dma_start(tab_w[:], tab_words[0].rearrange("p t i -> p (t i)").bitcast(I32))
-
         x_raw = []
-        for c, (a, first, width) in enumerate(X_CHUNKS):
+
+        def load_x(c):
+            a, first, width = X_CHUNKS[c]
             raw = keep.tile([P, PACK, width], F32, name=f"x_raw{c}")
             rows = x[a * K_PASS : (a + 1) * K_PASS, first : first + width]
             nc.sync.dma_start(raw[:], rows.rearrange("(p t) j -> p t j", t=PACK))
             x_raw.append(raw)
+
+        for c in range(3):
+            load_x(c)
+        tab_w = keep.tile([P, T], I32, name="tab_w", align_bytes=64)
+        nc.sync.dma_start(tab_w[:], tab_words[0].rearrange("p t i -> p (t i)").bitcast(I32))
+        for c in range(3, 5):
+            load_x(c)
 
         wx_w = keep.tile([P, X_PASSES, 2 * N], U8, name="wx_w", align_bytes=64)
         nc.sync.dma_start(wx_w[:].bitcast(I32), wx_words.rearrange("a p b -> p a b").bitcast(I32))
@@ -107,9 +115,6 @@ def tile_list_tiert_xhl_gate_kernel(
         for nt in range(1, N_TILES):
             load_gate(nt)
 
-        v_w = keep.tile([P, J], U32, name="v_w", tag="v_w", align_bytes=64)
-        nc.vector.tensor_copy(v_w[:], tab_w[:].bitcast(U32).indirect(offsets[:]))
-
         xq_w = [keep.tile([P, J], U32, name=f"xq_w{a}", align_bytes=64) for a in range(X_PASSES)]
         xq_s = [keep.tile([P, J], U8, name=f"xq_s{a}", align_bytes=64) for a in range(X_PASSES)]
         xr_w = [keep.tile([P, J], U32, name=f"xr_w{a}", align_bytes=64) for a in range(X_PASSES)]
@@ -125,7 +130,8 @@ def tile_list_tiert_xhl_gate_kernel(
 
         def first_tier(c):
             a, first, width = X_CHUNKS[c]
-            x_bf = woven.tile([P, width, PACK], BF16, name=f"x_bf{c}", tag="woven", align_bytes=64)
+            pool, tag = (keep, "v_w") if c == 2 else (woven, "woven")
+            x_bf = pool.tile([P, width, PACK], BF16, name=f"x_bf{c}", tag=tag, align_bytes=64)
             nc.scalar.copy(paired_words(x_bf[:]), paired_rows(x_raw[c][:]))
             quantize(xq_w[a], xq_s[a], first, x_bf[:])
             for j0 in range(first, first + width, P):
@@ -160,6 +166,8 @@ def tile_list_tiert_xhl_gate_kernel(
         left_over(1)
         first_tier(2)
         second_tier(0, 0, J_HALF)
+        v_w = keep.tile([P, J], U32, name="v_w", tag="v_w", align_bytes=64)
+        nc.vector.tensor_copy(v_w[:], tab_w[:].bitcast(U32).indirect(offsets[:]))
         left_over(2)
         first_tier(3)
         first_tier(4)
@@ -189,6 +197,7 @@ def tile_list_tiert_xhl_gate_kernel(
 
         split_hi(0)
         second_tier(1, 0, J)
+        split_hi(1)
 
         y = [y_psum.tile([P, J], F32, name=f"y{nt}") for nt in range(N_TILES)]
         x_operands = ((1, xq_w, xq_s), (0, xq_w, xq_s), (0, xr_w, xr_s), (1, xr_w, xr_s))
@@ -233,10 +242,19 @@ def tile_list_tiert_xhl_gate_kernel(
         v_s = keep.tile([P, J], U8, name="v_s", tag="rest1", align_bytes=64)
         nc.vector.tensor_copy(v_s[:], tab_s[:].indirect(offsets[:]))
         table_passes(0)
-        split_hi(1)
         split_lo(1)
+
+        def gate_and_store(nt, first, width):
+            result = keep.tile([P, width], F32, name=f"result{nt}_{first}")
+            picks = offsets[:, first // 16 : (first + width) // 16]
+            nc.vector.tensor_tensor(
+                result[:], gates[nt][:].indirect(picks), sums[nt][:, first : first + width], ALU.mult
+            )
+            nc.sync.dma_start(out[nt * P : (nt + 1) * P, first : first + width], result[:])
+
+        gate_and_store(0, 0, J)
         table_passes(1)
-        for nt in range(N_TILES):
-            result = keep.tile([P, J], F32, name=f"result{nt}")
-            nc.vector.tensor_tensor(result[:], gates[nt][:].indirect(offsets[:]), sums[nt][:], ALU.mult)
-            nc.sync.dma_start(out[nt * P : (nt + 1) * P, :], result[:])
+        gate_and_store(1, 0, J)
+        gate_and_store(2, 0, J)
+        gate_and_store(3, 0, J_HALF)
+        gate_and_store(3, J_HALF, J_HALF)

@@ -3,7 +3,6 @@ from contextlib import ExitStack
 import concourse.mybir as mybir
 
 K, L, N, T, J = 512, 1024, 512, 1024, 512
-FLOPS = 2 * (2 * K * N * J + 2 * L * N * J + L * 512 * J)
 
 F32 = mybir.dt.float32
 BF16 = mybir.dt.bfloat16
@@ -18,11 +17,17 @@ ALU = mybir.AluOpType
 P = 128
 PACK = 4
 K_PASS = P * PACK
+QUADRANTS = 4
 X_PASSES = L // K_PASS
 N_TILES = N // P
 J_HALF = J // 2
 N_HALF = N // 2
+LIST_ROWS = 16
+
+FLOPS = 2 * J * (2 * K * N + 2 * L * N + L * K_PASS)
+
 X_CHUNKS = ((0, 0, P), (0, P, P), (0, J_HALF, J_HALF), (1, 0, J_HALF), (1, J_HALF, J_HALF))
+
 HI_MASK = -983056
 
 
@@ -40,29 +45,28 @@ def tile_list_tiert_xhl_gate_kernel(
     nc = tc.nc
     with ExitStack() as ctx:
         keep = ctx.enter_context(tc.tile_pool(name="keep", bufs=1))
-        woven = ctx.enter_context(tc.tile_pool(name="woven", bufs=2))
         y_psum = ctx.enter_context(tc.psum_pool(name="y_psum", bufs=1))
         back_psum = ctx.enter_context(tc.psum_pool(name="back_psum", bufs=4))
 
-        offsets = keep.tile([P, J // 16], U16, name="offsets")
+        offsets = keep.tile([P, J // LIST_ROWS], U16, name="offsets")
         nc.sync.dma_start(offsets[:], offs)
 
         wx_s = keep.tile([P, X_PASSES, N], U8, name="wx_s", align_bytes=64)
         nc.vector.memset(wx_s[:].rearrange("p a n -> p (a n)").bitcast(I32), 0)
-        tab_s = keep.tile([P, T], U8, name="tab_s", align_bytes=64)
+        tab_s = keep.tile([P, T], U8, name="tab_s", tag="tab_s", align_bytes=64)
         nc.vector.memset(tab_s[:].bitcast(I32), 0)
 
-        ramp_f32 = keep.tile([P, K_PASS], F32, name="ramp_f32")
+        ramp = keep.tile([P, K_PASS], BF16, name="ramp", tag="ramp", align_bytes=64)
         nc.gpsimd.iota(
-            ramp_f32[:], pattern=[[1, K_PASS]], base=0, channel_multiplier=-PACK, allow_small_or_imprecise_dtypes=True
+            ramp[:], pattern=[[1, K_PASS]], base=0, channel_multiplier=-PACK, allow_small_or_imprecise_dtypes=True
         )
-        ramp = woven.tile([P, K_PASS], BF16, name="ramp", tag="woven", align_bytes=64)
-        nc.scalar.copy(ramp[:], ramp_f32[:])
+        warm = keep.tile([P, 2], BF16, name="warm")
+        nc.scalar.copy(warm[:], ramp[:, 0:2])
         id_w = keep.tile([P, K_PASS], U32, name="id_w", align_bytes=64)
         id_s = keep.tile([P, K_PASS], U8, name="id_s", align_bytes=64)
         ident = (
-            woven.tile([P, 2, K_PASS], BF16, name="ident0", tag="woven", align_bytes=64),
-            keep.tile([P, 2, K_PASS], BF16, name="ident1", tag="v_w", align_bytes=64),
+            keep.tile([P, 2, K_PASS], BF16, name="ident0", tag="ident0", align_bytes=64),
+            keep.tile([P, 2, K_PASS], BF16, name="ident1", align_bytes=64),
         )
         for t in range(PACK):
             nc.vector.tensor_scalar(ident[t // 2][:, t % 2, :], ramp[:], float(t), None, ALU.is_equal)
@@ -76,30 +80,35 @@ def tile_list_tiert_xhl_gate_kernel(
 
         def load_x(c):
             a, first, width = X_CHUNKS[c]
-            raw = keep.tile([P, PACK, width], F32, name=f"x_raw{c}")
+            raw = keep.tile([P, PACK, width], F32, name=f"x_raw{c}", tag=f"x_raw{c}", align_bytes=64)
             rows = x[a * K_PASS : (a + 1) * K_PASS, first : first + width]
             nc.sync.dma_start(raw[:], rows.rearrange("(p t) j -> p t j", t=PACK))
             x_raw.append(raw)
 
-        for c in range(3):
+        first_pass_chunks = [c for c, chunk in enumerate(X_CHUNKS) if chunk[0] == 0]
+        for c in first_pass_chunks:
             load_x(c)
         tab_w = keep.tile([P, T], I32, name="tab_w", align_bytes=64)
         nc.sync.dma_start(tab_w[:], tab_words[0].rearrange("p t i -> p (t i)").bitcast(I32))
-        for c in range(3, 5):
+        for c in range(len(first_pass_chunks), len(X_CHUNKS)):
             load_x(c)
 
+        wt_raw = []
+
+        def load_wt(h):
+            raw = keep.tile([P, PACK, N_HALF], F32, name=f"wt_raw{h}")
+            nc.sync.dma_start(raw[:], wt[:, h * N_HALF : (h + 1) * N_HALF].rearrange("(p t) n -> p t n", t=PACK))
+            wt_raw.append(raw)
+
+        load_wt(0)
         wx_w = keep.tile([P, X_PASSES, 2 * N], U8, name="wx_w", align_bytes=64)
         nc.sync.dma_start(wx_w[:].bitcast(I32), wx_words.rearrange("a p b -> p a b").bitcast(I32))
-        for q in range(4):
+        for q in range(QUADRANTS):
             nc.sync.dma_start(
                 wx_s[32 * q : 32 * q + 4, :, :].bitcast(I32),
                 wx_scales[:, 4 * q : 4 * q + 4, :].rearrange("a r n -> r a n").bitcast(I32),
             )
-        wt_raw = []
-        for h in range(2):
-            raw = keep.tile([P, PACK, N_HALF], F32, name=f"wt_raw{h}")
-            nc.sync.dma_start(raw[:], wt[:, h * N_HALF : (h + 1) * N_HALF].rearrange("(p t) n -> p t n", t=PACK))
-            wt_raw.append(raw)
+        load_wt(1)
         gates = []
 
         def load_gate(nt):
@@ -108,7 +117,7 @@ def tile_list_tiert_xhl_gate_kernel(
             gates.append(g)
 
         load_gate(0)
-        for q in range(4):
+        for q in range(QUADRANTS):
             nc.sync.dma_start(
                 tab_s[32 * q : 32 * q + 4, :].bitcast(I32), tab_scales[0, 4 * q : 4 * q + 4, :].bitcast(I32)
             )
@@ -119,7 +128,7 @@ def tile_list_tiert_xhl_gate_kernel(
         xq_s = [keep.tile([P, J], U8, name=f"xq_s{a}", align_bytes=64) for a in range(X_PASSES)]
         xr_w = [keep.tile([P, J], U32, name=f"xr_w{a}", align_bytes=64) for a in range(X_PASSES)]
         xr_s = [keep.tile([P, J], U8, name=f"xr_s{a}", align_bytes=64) for a in range(X_PASSES)]
-        rest = [keep.tile([P, J, PACK], BF16, name=f"rest{a}", tag=f"rest{a}", align_bytes=64) for a in range(X_PASSES)]
+        rest = [keep.tile([P, J, PACK], BF16, name=f"rest{a}", align_bytes=64) for a in range(X_PASSES)]
         back = {}
 
         def quantize(words, scales, first, values):
@@ -128,12 +137,10 @@ def tile_list_tiert_xhl_gate_kernel(
                 out=words[:, cols].bitcast(FP8X4), scales=scales[:, cols], in_=values.rearrange("p j t -> p (j t)")
             )
 
-        def first_tier(c):
+        def first_tier(c, x_bf, weave):
             a, first, width = X_CHUNKS[c]
-            pool, tag = (keep, "v_w") if c == 2 else (woven, "woven")
-            x_bf = pool.tile([P, width, PACK], BF16, name=f"x_bf{c}", tag=tag, align_bytes=64)
-            nc.scalar.copy(paired_words(x_bf[:]), paired_rows(x_raw[c][:]))
-            quantize(xq_w[a], xq_s[a], first, x_bf[:])
+            weave(paired_words(x_bf), paired_rows(x_raw[c][:]))
+            quantize(xq_w[a], xq_s[a], first, x_bf)
             for j0 in range(first, first + width, P):
                 back[a, j0] = back_psum.tile([P, PACK, P], F32, name="back")
                 for t in range(PACK):
@@ -160,28 +167,30 @@ def tile_list_tiert_xhl_gate_kernel(
         def second_tier(a, first, width):
             quantize(xr_w[a], xr_s[a], first, rest[a][:, first : first + width, :])
 
-        first_tier(0)
-        first_tier(1)
+        def woven(name, width, tag):
+            return keep.tile([P, width, PACK], BF16, name=name, tag=tag, align_bytes=64)
+
+        first_tier(0, woven("x_bf0", P, "ramp")[:], nc.vector.tensor_copy)
+        first_tier(1, woven("x_bf1", P, "ident0")[:], nc.scalar.copy)
         left_over(0)
         left_over(1)
-        first_tier(2)
+        first_tier(2, woven("x_bf2", J_HALF, "ident0")[:], nc.scalar.copy)
         second_tier(0, 0, J_HALF)
-        v_w = keep.tile([P, J], U32, name="v_w", tag="v_w", align_bytes=64)
+        v_w = keep.tile([P, J], U32, name="v_w", tag="ident0", align_bytes=64)
         nc.vector.tensor_copy(v_w[:], tab_w[:].bitcast(U32).indirect(offsets[:]))
         left_over(2)
-        first_tier(3)
-        first_tier(4)
+        x_bf_last = woven("x_bf_last", J, "x_raw1")
+        first_tier(3, x_bf_last[:, :J_HALF, :], nc.scalar.copy)
+        first_tier(4, x_bf_last[:, J_HALF:, :], nc.scalar.copy)
         second_tier(0, J_HALF, J_HALF)
-        left_over(3)
-        left_over(4)
 
         parts = {}
 
-        def split_hi(h):
+        def split_hi(h, upper_tag, parts_tag):
             halves = wt_raw[h][:].bitcast(BF16).rearrange("p t (n e) -> p t n e", e=2)
-            upper = woven.tile([P, N_HALF, PACK], BF16, name=f"upper{h}", tag="woven", align_bytes=64)
+            upper = woven(f"upper{h}", N_HALF, upper_tag)
             nc.scalar.copy(paired_words(upper[:]), paired_rows(halves[:, :, :, 1]))
-            parts[h] = keep.tile([P, 2, N_HALF, PACK], BF16, name=f"parts{h}", align_bytes=64)
+            parts[h] = keep.tile([P, 2, N_HALF, PACK], BF16, name=f"parts{h}", tag=parts_tag, align_bytes=64)
             nc.vector.tensor_scalar(
                 parts[h][:, 0].rearrange("p n t -> p (n t)").bitcast(I32),
                 upper[:].rearrange("p n t -> p (n t)").bitcast(I32),
@@ -190,14 +199,21 @@ def tile_list_tiert_xhl_gate_kernel(
                 ALU.bitwise_and,
             )
 
-        def split_lo(h):
-            nc.vector.tensor_tensor(
-                paired_words(parts[h][:, 1]), paired_rows(wt_raw[h][:]), paired_words(parts[h][:, 0]), ALU.subtract
+        split_hi(0, "x_raw2", "parts0")
+        for n0 in range(0, N_HALF, P):
+            cols = slice(n0, n0 + P)
+            nc.gpsimd.tensor_tensor(
+                parts[0][:, 1, cols, :],
+                wt_raw[0][:, :, cols].rearrange("p t n -> p n t"),
+                parts[0][:, 0, cols, :],
+                ALU.subtract,
             )
-
-        split_hi(0)
+        left_over(3)
+        left_over(4)
+        v_s = keep.tile([P, J], U8, name="v_s", tag="x_raw4", align_bytes=64)
+        nc.vector.tensor_copy(v_s[:], tab_s[:].indirect(offsets[:]))
         second_tier(1, 0, J)
-        split_hi(1)
+        split_hi(1, "x_raw3", "tab_s")
 
         y = [y_psum.tile([P, J], F32, name=f"y{nt}") for nt in range(N_TILES)]
         x_operands = ((1, xq_w, xq_s), (0, xq_w, xq_s), (0, xr_w, xr_s), (1, xr_w, xr_s))
@@ -238,15 +254,14 @@ def tile_list_tiert_xhl_gate_kernel(
                 sums[nt] = keep.tile([P, J], F32, name=f"sums{nt}")
                 nc.scalar.copy(sums[nt][:], y[nt][:])
 
-        split_lo(0)
-        v_s = keep.tile([P, J], U8, name="v_s", tag="rest1", align_bytes=64)
-        nc.vector.tensor_copy(v_s[:], tab_s[:].indirect(offsets[:]))
         table_passes(0)
-        split_lo(1)
+        nc.vector.tensor_tensor(
+            paired_words(parts[1][:, 1]), paired_rows(wt_raw[1][:]), paired_words(parts[1][:, 0]), ALU.subtract
+        )
 
         def gate_and_store(nt, first, width):
             result = keep.tile([P, width], F32, name=f"result{nt}_{first}")
-            picks = offsets[:, first // 16 : (first + width) // 16]
+            picks = offsets[:, first // LIST_ROWS : (first + width) // LIST_ROWS]
             nc.vector.tensor_tensor(
                 result[:], gates[nt][:].indirect(picks), sums[nt][:, first : first + width], ALU.mult
             )
@@ -254,7 +269,7 @@ def tile_list_tiert_xhl_gate_kernel(
 
         gate_and_store(0, 0, J)
         table_passes(1)
-        gate_and_store(1, 0, J)
-        gate_and_store(2, 0, J)
-        gate_and_store(3, 0, J_HALF)
-        gate_and_store(3, J_HALF, J_HALF)
+        for nt in range(1, N_TILES - 1):
+            gate_and_store(nt, 0, J)
+        gate_and_store(N_TILES - 1, 0, J_HALF)
+        gate_and_store(N_TILES - 1, J_HALF, J_HALF)

@@ -53,7 +53,7 @@ def tile_list_tiert_xhl_gate_kernel(
 
         wx_s = keep.tile([P, X_PASSES, N], U8, name="wx_s", align_bytes=64)
         nc.vector.memset(wx_s[:].rearrange("p a n -> p (a n)").bitcast(I32), 0)
-        tab_s = keep.tile([P, T], U8, name="tab_s", tag="tab_s", align_bytes=64)
+        tab_s = keep.tile([P, T], U8, name="tab_s", align_bytes=64)
         nc.vector.memset(tab_s[:].bitcast(I32), 0)
 
         ramp = keep.tile([P, K_PASS], BF16, name="ramp", tag="ramp", align_bytes=64)
@@ -128,7 +128,7 @@ def tile_list_tiert_xhl_gate_kernel(
         xq_s = [keep.tile([P, J], U8, name=f"xq_s{a}", align_bytes=64) for a in range(X_PASSES)]
         xr_w = [keep.tile([P, J], U32, name=f"xr_w{a}", align_bytes=64) for a in range(X_PASSES)]
         xr_s = [keep.tile([P, J], U8, name=f"xr_s{a}", align_bytes=64) for a in range(X_PASSES)]
-        rest = [keep.tile([P, J, PACK], BF16, name=f"rest{a}", align_bytes=64) for a in range(X_PASSES)]
+        rest = [keep.tile([P, J, PACK], BF16, name=f"rest{a}", tag=f"rest{a}", align_bytes=64) for a in range(X_PASSES)]
         back = {}
 
         def quantize(words, scales, first, values):
@@ -186,11 +186,11 @@ def tile_list_tiert_xhl_gate_kernel(
 
         parts = {}
 
-        def split_hi(h, upper_tag, parts_tag):
+        def split_hi(h, upper_tag):
             halves = wt_raw[h][:].bitcast(BF16).rearrange("p t (n e) -> p t n e", e=2)
             upper = woven(f"upper{h}", N_HALF, upper_tag)
             nc.scalar.copy(paired_words(upper[:]), paired_rows(halves[:, :, :, 1]))
-            parts[h] = keep.tile([P, 2, N_HALF, PACK], BF16, name=f"parts{h}", tag=parts_tag, align_bytes=64)
+            parts[h] = keep.tile([P, 2, N_HALF, PACK], BF16, name=f"parts{h}", align_bytes=64)
             nc.vector.tensor_scalar(
                 parts[h][:, 0].rearrange("p n t -> p (n t)").bitcast(I32),
                 upper[:].rearrange("p n t -> p (n t)").bitcast(I32),
@@ -199,21 +199,19 @@ def tile_list_tiert_xhl_gate_kernel(
                 ALU.bitwise_and,
             )
 
-        split_hi(0, "x_raw2", "parts0")
-        for n0 in range(0, N_HALF, P):
-            cols = slice(n0, n0 + P)
-            nc.gpsimd.tensor_tensor(
-                parts[0][:, 1, cols, :],
-                wt_raw[0][:, :, cols].rearrange("p t n -> p n t"),
-                parts[0][:, 0, cols, :],
-                ALU.subtract,
+        def split_lo(h):
+            nc.vector.tensor_tensor(
+                paired_words(parts[h][:, 1]), paired_rows(wt_raw[h][:]), paired_words(parts[h][:, 0]), ALU.subtract
             )
+
+        split_hi(0, "x_raw2")
         left_over(3)
         left_over(4)
-        v_s = keep.tile([P, J], U8, name="v_s", tag="x_raw4", align_bytes=64)
-        nc.vector.tensor_copy(v_s[:], tab_s[:].indirect(offsets[:]))
+        split_lo(0)
         second_tier(1, 0, J)
-        split_hi(1, "x_raw3", "tab_s")
+        split_hi(1, "x_raw3")
+        v_s = keep.tile([P, J], U8, name="v_s", tag="rest1", align_bytes=64)
+        nc.vector.tensor_copy(v_s[:], tab_s[:].indirect(offsets[:]))
 
         y = [y_psum.tile([P, J], F32, name=f"y{nt}") for nt in range(N_TILES)]
         x_operands = ((1, xq_w, xq_s), (0, xq_w, xq_s), (0, xr_w, xr_s), (1, xr_w, xr_s))
@@ -255,9 +253,7 @@ def tile_list_tiert_xhl_gate_kernel(
                 nc.scalar.copy(sums[nt][:], y[nt][:])
 
         table_passes(0)
-        nc.vector.tensor_tensor(
-            paired_words(parts[1][:, 1]), paired_rows(wt_raw[1][:]), paired_words(parts[1][:, 0]), ALU.subtract
-        )
+        split_lo(1)
 
         def gate_and_store(nt, first, width):
             result = keep.tile([P, width], F32, name=f"result{nt}_{first}")

@@ -22,6 +22,7 @@ X_PASSES = L // K_PASS
 N_TILES = N // P
 J_HALF = J // 2
 N_HALF = N // 2
+SCALE_ROWS = K_PASS // 32
 LIST_ROWS = 16
 
 FLOPS = 2 * J * (2 * K * N + 2 * L * N + L * K_PASS)
@@ -29,6 +30,7 @@ FLOPS = 2 * J * (2 * K * N + 2 * L * N + L * K_PASS)
 X_CHUNKS = ((0, 0, P), (0, P, P), (0, J_HALF, J_HALF), (1, 0, J_HALF), (1, J_HALF, J_HALF))
 
 HI_MASK = -983056
+BF16_ONE = 0x3F80
 
 
 def paired_rows(ap):
@@ -48,32 +50,33 @@ def tile_list_tiert_xhl_gate_kernel(
         y_psum = ctx.enter_context(tc.psum_pool(name="y_psum", bufs=1))
         back_psum = ctx.enter_context(tc.psum_pool(name="back_psum", bufs=4))
 
-        offsets = keep.tile([P, J // LIST_ROWS], U16, name="offsets")
-        nc.sync.dma_start(offsets[:], offs)
-
+        tab_s = keep.tile([P, T], U8, name="tab_s", align_bytes=64)
+        nc.vector.memset(tab_s[: P - SCALE_ROWS, :].bitcast(I32), 0)
+        v_s = keep.tile([P, J], U8, name="v_s", align_bytes=64)
+        nc.vector.memset(v_s[:].bitcast(I32), 0)
         wx_s = keep.tile([P, X_PASSES, N], U8, name="wx_s", align_bytes=64)
         nc.vector.memset(wx_s[:].rearrange("p a n -> p (a n)").bitcast(I32), 0)
-        tab_s = keep.tile([P, T], U8, name="tab_s", align_bytes=64)
-        nc.vector.memset(tab_s[:].bitcast(I32), 0)
 
-        ramp = keep.tile([P, K_PASS], BF16, name="ramp", tag="ramp", align_bytes=64)
-        nc.gpsimd.iota(
-            ramp[:], pattern=[[1, K_PASS]], base=0, channel_multiplier=-PACK, allow_small_or_imprecise_dtypes=True
-        )
+        ramp = keep.tile([P, 2 * P], BF16, name="ramp", tag="ramp", align_bytes=64)
+        nc.gpsimd.iota(ramp[:], pattern=[[1, 2 * P]], base=0, channel_multiplier=-2, allow_small_or_imprecise_dtypes=True)
         warm = keep.tile([P, 2], BF16, name="warm")
         nc.scalar.copy(warm[:], ramp[:, 0:2])
         id_w = keep.tile([P, K_PASS], U32, name="id_w", align_bytes=64)
         id_s = keep.tile([P, K_PASS], U8, name="id_s", align_bytes=64)
         ident = (
-            keep.tile([P, 2, K_PASS], BF16, name="ident0", tag="ident0", align_bytes=64),
-            keep.tile([P, 2, K_PASS], BF16, name="ident1", align_bytes=64),
+            keep.tile([P, 2, 2 * P], I32, name="ident0", tag="ident0", align_bytes=64),
+            keep.tile([P, 2, 2 * P], I32, name="ident1", tag="ident1", align_bytes=64),
         )
         for t in range(PACK):
-            nc.vector.tensor_scalar(ident[t // 2][:, t % 2, :], ramp[:], float(t), None, ALU.is_equal)
+            nc.vector.tensor_scalar(
+                ident[t // 2][:, t % 2, :], ramp[:], float(t // 2), float(BF16_ONE << (16 * (t % 2))), ALU.is_equal, ALU.mult
+            )
         for h in range(2):
             cols = slice(h * 2 * P, (h + 1) * 2 * P)
             nc.vector.quantize_mx(
-                out=id_w[:, cols].bitcast(FP8X4), scales=id_s[:, cols], in_=ident[h][:].rearrange("p t f -> p (t f)")
+                out=id_w[:, cols].bitcast(FP8X4),
+                scales=id_s[:, cols],
+                in_=ident[h][:].rearrange("p t f -> p (t f)").bitcast(BF16),
             )
 
         x_raw = []
@@ -86,10 +89,21 @@ def tile_list_tiert_xhl_gate_kernel(
             x_raw.append(raw)
 
         first_pass_chunks = [c for c, chunk in enumerate(X_CHUNKS) if chunk[0] == 0]
-        for c in first_pass_chunks:
+        load_x(0)
+        offsets = keep.tile([P, J // LIST_ROWS], U16, name="offsets")
+        nc.sync.dma_start(offsets[:], offs)
+        nc.sync.dma_start(tab_s[P - SCALE_ROWS :, :].bitcast(I32), tab_scales[0].bitcast(I32))
+        for c in first_pass_chunks[1:]:
             load_x(c)
         tab_w = keep.tile([P, T], I32, name="tab_w", align_bytes=64)
         nc.sync.dma_start(tab_w[:], tab_words[0].rearrange("p t i -> p (t i)").bitcast(I32))
+        wx_w = keep.tile([P, X_PASSES, 2 * N], U8, name="wx_w", align_bytes=64)
+        nc.sync.dma_start(wx_w[:].bitcast(I32), wx_words.rearrange("a p b -> p a b").bitcast(I32))
+        for q in range(QUADRANTS):
+            nc.sync.dma_start(
+                wx_s[32 * q : 32 * q + 4, :, :].bitcast(I32),
+                wx_scales[:, 4 * q : 4 * q + 4, :].rearrange("a r n -> r a n").bitcast(I32),
+            )
         for c in range(len(first_pass_chunks), len(X_CHUNKS)):
             load_x(c)
 
@@ -101,13 +115,6 @@ def tile_list_tiert_xhl_gate_kernel(
             wt_raw.append(raw)
 
         load_wt(0)
-        wx_w = keep.tile([P, X_PASSES, 2 * N], U8, name="wx_w", align_bytes=64)
-        nc.sync.dma_start(wx_w[:].bitcast(I32), wx_words.rearrange("a p b -> p a b").bitcast(I32))
-        for q in range(QUADRANTS):
-            nc.sync.dma_start(
-                wx_s[32 * q : 32 * q + 4, :, :].bitcast(I32),
-                wx_scales[:, 4 * q : 4 * q + 4, :].rearrange("a r n -> r a n").bitcast(I32),
-            )
         load_wt(1)
         gates = []
 
@@ -117,18 +124,12 @@ def tile_list_tiert_xhl_gate_kernel(
             gates.append(g)
 
         load_gate(0)
-        for q in range(QUADRANTS):
-            nc.sync.dma_start(
-                tab_s[32 * q : 32 * q + 4, :].bitcast(I32), tab_scales[0, 4 * q : 4 * q + 4, :].bitcast(I32)
-            )
-        for nt in range(1, N_TILES):
-            load_gate(nt)
 
         xq_w = [keep.tile([P, J], U32, name=f"xq_w{a}", align_bytes=64) for a in range(X_PASSES)]
         xq_s = [keep.tile([P, J], U8, name=f"xq_s{a}", align_bytes=64) for a in range(X_PASSES)]
         xr_w = [keep.tile([P, J], U32, name=f"xr_w{a}", align_bytes=64) for a in range(X_PASSES)]
         xr_s = [keep.tile([P, J], U8, name=f"xr_s{a}", align_bytes=64) for a in range(X_PASSES)]
-        rest = [keep.tile([P, J, PACK], BF16, name=f"rest{a}", tag=f"rest{a}", align_bytes=64) for a in range(X_PASSES)]
+        rest = [keep.tile([P, J, PACK], BF16, name="rest0", align_bytes=64)]
         back = {}
 
         def quantize(words, scales, first, values):
@@ -171,26 +172,37 @@ def tile_list_tiert_xhl_gate_kernel(
             return keep.tile([P, width, PACK], BF16, name=name, tag=tag, align_bytes=64)
 
         first_tier(0, woven("x_bf0", P, "ramp")[:], nc.vector.tensor_copy)
+        v_rows = keep.tile([P, J], U8, name="v_rows", tag="ramp", align_bytes=64)
+        half = J_HALF // LIST_ROWS
+        nc.vector.tensor_copy(v_rows[:, :J_HALF], tab_s[:].indirect(offsets[:, :half]))
         first_tier(1, woven("x_bf1", P, "ident0")[:], nc.scalar.copy)
+        nc.vector.tensor_copy(v_rows[:, J_HALF:], tab_s[:].indirect(offsets[:, half:]))
+        for q in range(QUADRANTS):
+            first_row = P - SCALE_ROWS + 4 * q
+            nc.sync.dma_start(v_s[32 * q : 32 * q + 4, :].bitcast(I32), v_rows[first_row : first_row + 4, :].bitcast(I32))
+        for nt in range(1, N_TILES):
+            load_gate(nt)
         left_over(0)
         left_over(1)
-        first_tier(2, woven("x_bf2", J_HALF, "ident0")[:], nc.scalar.copy)
+        first_tier(2, woven("x_bf2", J_HALF, "ident1")[:], nc.scalar.copy)
         second_tier(0, 0, J_HALF)
-        v_w = keep.tile([P, J], U32, name="v_w", tag="ident0", align_bytes=64)
+        v_w = keep.tile([P, J], U32, name="v_w", tag="ident1", align_bytes=64)
         nc.vector.tensor_copy(v_w[:], tab_w[:].bitcast(U32).indirect(offsets[:]))
         left_over(2)
         x_bf_last = woven("x_bf_last", J, "x_raw1")
         first_tier(3, x_bf_last[:, :J_HALF, :], nc.scalar.copy)
         first_tier(4, x_bf_last[:, J_HALF:, :], nc.scalar.copy)
         second_tier(0, J_HALF, J_HALF)
+        rest.append(woven("rest1", J, "x_raw1"))
 
-        parts = {}
+        parts = [
+            keep.tile([P, 2, N_HALF, PACK], BF16, name=f"parts{h}", align_bytes=64)[:] for h in range(2)
+        ]
 
         def split_hi(h, upper_tag):
             halves = wt_raw[h][:].bitcast(BF16).rearrange("p t (n e) -> p t n e", e=2)
             upper = woven(f"upper{h}", N_HALF, upper_tag)
             nc.scalar.copy(paired_words(upper[:]), paired_rows(halves[:, :, :, 1]))
-            parts[h] = keep.tile([P, 2, N_HALF, PACK], BF16, name=f"parts{h}", align_bytes=64)
             nc.vector.tensor_scalar(
                 parts[h][:, 0].rearrange("p n t -> p (n t)").bitcast(I32),
                 upper[:].rearrange("p n t -> p (n t)").bitcast(I32),
@@ -210,22 +222,25 @@ def tile_list_tiert_xhl_gate_kernel(
         split_lo(0)
         second_tier(1, 0, J)
         split_hi(1, "x_raw3")
-        v_s = keep.tile([P, J], U8, name="v_s", tag="rest1", align_bytes=64)
-        nc.vector.tensor_copy(v_s[:], tab_s[:].indirect(offsets[:]))
 
         y = [y_psum.tile([P, J], F32, name=f"y{nt}") for nt in range(N_TILES)]
-        x_operands = ((1, xq_w, xq_s), (0, xq_w, xq_s), (0, xr_w, xr_s), (1, xr_w, xr_s))
-        for i, (a, words, scales) in enumerate(x_operands):
+        x_operands = ((0, xq_w, xq_s), (0, xr_w, xr_s), (1, xq_w, xq_s), (1, xr_w, xr_s))
+
+        def wx_pass(i, nt):
+            a, words, scales = x_operands[i]
+            nc.tensor.matmul_mx(
+                out=y[nt][:],
+                lhsT=wx_w[:, a, 2 * P * nt : 2 * P * (nt + 1)].bitcast(FP4X4),
+                lhsT_scale=wx_s[:, a, P * nt : P * (nt + 1)],
+                rhs=words[a][:].bitcast(FP8X4),
+                rhs_scale=scales[a][:],
+                start=(i == 0),
+                stop=False,
+            )
+
+        for i in range(len(x_operands) - 1):
             for nt in range(N_TILES):
-                nc.tensor.matmul_mx(
-                    out=y[nt][:],
-                    lhsT=wx_w[:, a, 2 * P * nt : 2 * P * (nt + 1)].bitcast(FP4X4),
-                    lhsT_scale=wx_s[:, a, P * nt : P * (nt + 1)],
-                    rhs=words[a][:].bitcast(FP8X4),
-                    rhs_scale=scales[a][:],
-                    start=(i == 0),
-                    stop=False,
-                )
+                wx_pass(i, nt)
 
         sums = {}
 
@@ -235,10 +250,11 @@ def tile_list_tiert_xhl_gate_kernel(
             nc.vector.quantize_mx(
                 out=w_w[:].rearrange("p s n -> p (s n)").bitcast(FP8X4),
                 scales=w_s[:].rearrange("p s n -> p (s n)"),
-                in_=parts[h][:].rearrange("p s n t -> p (s n t)"),
+                in_=parts[h].rearrange("p s n t -> p (s n t)"),
             )
             for u in range(N_HALF // P):
                 nt = h * (N_HALF // P) + u
+                wx_pass(len(x_operands) - 1, nt)
                 for part in range(2):
                     nc.tensor.matmul_mx(
                         out=y[nt][:],

@@ -59,8 +59,6 @@ def tile_list_tiert_xhl_gate_kernel(
 
         ramp = keep.tile([P, 2 * P], BF16, name="ramp", tag="ramp", align_bytes=64)
         nc.gpsimd.iota(ramp[:], pattern=[[1, 2 * P]], base=0, channel_multiplier=-2, allow_small_or_imprecise_dtypes=True)
-        warm = keep.tile([P, 2], BF16, name="warm")
-        nc.scalar.copy(warm[:], ramp[:, 0:2])
         id_w = keep.tile([P, K_PASS], U32, name="id_w", align_bytes=64)
         id_s = keep.tile([P, K_PASS], U8, name="id_s", align_bytes=64)
         ident = (
@@ -71,13 +69,18 @@ def tile_list_tiert_xhl_gate_kernel(
             nc.vector.tensor_scalar(
                 ident[t // 2][:, t % 2, :], ramp[:], float(t // 2), float(BF16_ONE << (16 * (t % 2))), ALU.is_equal, ALU.mult
             )
-        for h in range(2):
+        warm = keep.tile([P, 2], BF16, name="warm")
+        nc.scalar.copy(warm[:], ident[1][:, 0, 0:1].bitcast(BF16))
+
+        def quantize_identity(h):
             cols = slice(h * 2 * P, (h + 1) * 2 * P)
             nc.vector.quantize_mx(
                 out=id_w[:, cols].bitcast(FP8X4),
                 scales=id_s[:, cols],
                 in_=ident[h][:].rearrange("p t f -> p (t f)").bitcast(BF16),
             )
+
+        quantize_identity(0)
 
         x_raw = []
 
@@ -88,24 +91,13 @@ def tile_list_tiert_xhl_gate_kernel(
             nc.sync.dma_start(raw[:], rows.rearrange("(p t) j -> p t j", t=PACK))
             x_raw.append(raw)
 
-        first_pass_chunks = [c for c, chunk in enumerate(X_CHUNKS) if chunk[0] == 0]
-        load_x(0)
         offsets = keep.tile([P, J // LIST_ROWS], U16, name="offsets")
         nc.sync.dma_start(offsets[:], offs)
         nc.sync.dma_start(tab_s[P - SCALE_ROWS :, :].bitcast(I32), tab_scales[0].bitcast(I32))
-        for c in first_pass_chunks[1:]:
+        for c in range(len(X_CHUNKS)):
             load_x(c)
         tab_w = keep.tile([P, T], I32, name="tab_w", align_bytes=64)
         nc.sync.dma_start(tab_w[:], tab_words[0].rearrange("p t i -> p (t i)").bitcast(I32))
-        wx_w = keep.tile([P, X_PASSES, 2 * N], U8, name="wx_w", align_bytes=64)
-        nc.sync.dma_start(wx_w[:].bitcast(I32), wx_words.rearrange("a p b -> p a b").bitcast(I32))
-        for q in range(QUADRANTS):
-            nc.sync.dma_start(
-                wx_s[32 * q : 32 * q + 4, :, :].bitcast(I32),
-                wx_scales[:, 4 * q : 4 * q + 4, :].rearrange("a r n -> r a n").bitcast(I32),
-            )
-        for c in range(len(first_pass_chunks), len(X_CHUNKS)):
-            load_x(c)
 
         wt_raw = []
 
@@ -115,6 +107,13 @@ def tile_list_tiert_xhl_gate_kernel(
             wt_raw.append(raw)
 
         load_wt(0)
+        wx_w = keep.tile([P, X_PASSES, 2 * N], U8, name="wx_w", align_bytes=64)
+        nc.sync.dma_start(wx_w[:].bitcast(I32), wx_words.rearrange("a p b -> p a b").bitcast(I32))
+        for q in range(QUADRANTS):
+            nc.sync.dma_start(
+                wx_s[32 * q : 32 * q + 4, :, :].bitcast(I32),
+                wx_scales[:, 4 * q : 4 * q + 4, :].rearrange("a r n -> r a n").bitcast(I32),
+            )
         load_wt(1)
         gates = []
 
@@ -129,7 +128,7 @@ def tile_list_tiert_xhl_gate_kernel(
         xq_s = [keep.tile([P, J], U8, name=f"xq_s{a}", align_bytes=64) for a in range(X_PASSES)]
         xr_w = [keep.tile([P, J], U32, name=f"xr_w{a}", align_bytes=64) for a in range(X_PASSES)]
         xr_s = [keep.tile([P, J], U8, name=f"xr_s{a}", align_bytes=64) for a in range(X_PASSES)]
-        rest = [keep.tile([P, J, PACK], BF16, name="rest0", align_bytes=64)]
+        rest = []
         back = {}
 
         def quantize(words, scales, first, values):
@@ -138,9 +137,11 @@ def tile_list_tiert_xhl_gate_kernel(
                 out=words[:, cols].bitcast(FP8X4), scales=scales[:, cols], in_=values.rearrange("p j t -> p (j t)")
             )
 
-        def first_tier(c, x_bf, weave):
+        def weave(c, x_bf, copy):
+            copy(paired_words(x_bf), paired_rows(x_raw[c][:]))
+
+        def first_tier(c, x_bf):
             a, first, width = X_CHUNKS[c]
-            weave(paired_words(x_bf), paired_rows(x_raw[c][:]))
             quantize(xq_w[a], xq_s[a], first, x_bf)
             for j0 in range(first, first + width, P):
                 back[a, j0] = back_psum.tile([P, PACK, P], F32, name="back")
@@ -171,32 +172,42 @@ def tile_list_tiert_xhl_gate_kernel(
         def woven(name, width, tag):
             return keep.tile([P, width, PACK], BF16, name=name, tag=tag, align_bytes=64)
 
-        first_tier(0, woven("x_bf0", P, "ramp")[:], nc.vector.tensor_copy)
         v_rows = keep.tile([P, J], U8, name="v_rows", tag="ramp", align_bytes=64)
         half = J_HALF // LIST_ROWS
         nc.vector.tensor_copy(v_rows[:, :J_HALF], tab_s[:].indirect(offsets[:, :half]))
-        first_tier(1, woven("x_bf1", P, "ident0")[:], nc.scalar.copy)
+        x_bf_first = woven("x_bf_first", J_HALF, "ident0")
+        weave(0, x_bf_first[:, :P, :], nc.vector.tensor_copy)
+        quantize_identity(1)
+        first_tier(0, x_bf_first[:, :P, :])
         nc.vector.tensor_copy(v_rows[:, J_HALF:], tab_s[:].indirect(offsets[:, half:]))
+        weave(1, x_bf_first[:, P:, :], nc.scalar.copy)
+        first_tier(1, x_bf_first[:, P:, :])
         for q in range(QUADRANTS):
             first_row = P - SCALE_ROWS + 4 * q
             nc.sync.dma_start(v_s[32 * q : 32 * q + 4, :].bitcast(I32), v_rows[first_row : first_row + 4, :].bitcast(I32))
         for nt in range(1, N_TILES):
             load_gate(nt)
+        rest.append(woven("rest0", J, "ident0"))
         left_over(0)
         left_over(1)
-        first_tier(2, woven("x_bf2", J_HALF, "ident1")[:], nc.scalar.copy)
+        x_bf2 = woven("x_bf2", J_HALF, "ident1")
+        weave(2, x_bf2[:], nc.scalar.copy)
+        first_tier(2, x_bf2[:])
         second_tier(0, 0, J_HALF)
-        v_w = keep.tile([P, J], U32, name="v_w", tag="ident1", align_bytes=64)
-        nc.vector.tensor_copy(v_w[:], tab_w[:].bitcast(U32).indirect(offsets[:]))
         left_over(2)
         x_bf_last = woven("x_bf_last", J, "x_raw1")
-        first_tier(3, x_bf_last[:, :J_HALF, :], nc.scalar.copy)
-        first_tier(4, x_bf_last[:, J_HALF:, :], nc.scalar.copy)
+        weave(3, x_bf_last[:, :J_HALF, :], nc.scalar.copy)
+        first_tier(3, x_bf_last[:, :J_HALF, :])
+        weave(4, x_bf_last[:, J_HALF:, :], nc.scalar.copy)
+        first_tier(4, x_bf_last[:, J_HALF:, :])
         second_tier(0, J_HALF, J_HALF)
         rest.append(woven("rest1", J, "x_raw1"))
+        v_w = keep.tile([P, J], U32, name="v_w", tag="ident0", align_bytes=64)
+        nc.vector.tensor_copy(v_w[:], tab_w[:].bitcast(U32).indirect(offsets[:]))
 
         parts = [
-            keep.tile([P, 2, N_HALF, PACK], BF16, name=f"parts{h}", align_bytes=64)[:] for h in range(2)
+            keep.tile([P, 2, N_HALF, PACK], BF16, name=f"parts{h}", tag=tag, align_bytes=64)[:]
+            for h, tag in enumerate(("x_raw3", "parts1"))
         ]
 
         def split_hi(h, upper_tag):
@@ -216,15 +227,15 @@ def tile_list_tiert_xhl_gate_kernel(
                 paired_words(parts[h][:, 1]), paired_rows(wt_raw[h][:]), paired_words(parts[h][:, 0]), ALU.subtract
             )
 
-        split_hi(0, "x_raw2")
         left_over(3)
         left_over(4)
-        split_lo(0)
+        split_hi(0, "x_raw2")
         second_tier(1, 0, J)
-        split_hi(1, "x_raw3")
+        split_lo(0)
+        split_hi(1, "x_raw4")
 
         y = [y_psum.tile([P, J], F32, name=f"y{nt}") for nt in range(N_TILES)]
-        x_operands = ((0, xq_w, xq_s), (0, xr_w, xr_s), (1, xq_w, xq_s), (1, xr_w, xr_s))
+        x_operands = ((1, xq_w, xq_s), (0, xq_w, xq_s), (0, xr_w, xr_s), (1, xr_w, xr_s))
 
         def wx_pass(i, nt):
             a, words, scales = x_operands[i]

@@ -106,7 +106,6 @@ def tile_list_tiert_xhl_gate_kernel(
             nc.sync.dma_start(raw[:], wt[:, h * N_HALF : (h + 1) * N_HALF].rearrange("(p t) n -> p t n", t=PACK))
             wt_raw.append(raw)
 
-        load_wt(0)
         wx_w = keep.tile([P, X_PASSES, 2 * N], U8, name="wx_w", align_bytes=64)
         nc.sync.dma_start(wx_w[:].bitcast(I32), wx_words.rearrange("a p b -> p a b").bitcast(I32))
         for q in range(QUADRANTS):
@@ -114,6 +113,7 @@ def tile_list_tiert_xhl_gate_kernel(
                 wx_s[32 * q : 32 * q + 4, :, :].bitcast(I32),
                 wx_scales[:, 4 * q : 4 * q + 4, :].rearrange("a r n -> r a n").bitcast(I32),
             )
+        load_wt(0)
         load_wt(1)
         gates = []
 
@@ -137,12 +137,14 @@ def tile_list_tiert_xhl_gate_kernel(
                 out=words[:, cols].bitcast(FP8X4), scales=scales[:, cols], in_=values.rearrange("p j t -> p (j t)")
             )
 
-        def weave(c, x_bf, copy):
-            copy(paired_words(x_bf), paired_rows(x_raw[c][:]))
+        def weave(c, x_bf, copy, skip=0, take=J_HALF):
+            cols = slice(skip, min(skip + take, X_CHUNKS[c][2]))
+            copy(paired_words(x_bf[:, cols, :]), paired_rows(x_raw[c][:, :, cols]))
 
-        def first_tier(c, x_bf):
+        def first_tier(c, x_bf, skip=0, take=J_HALF):
             a, first, width = X_CHUNKS[c]
-            quantize(xq_w[a], xq_s[a], first, x_bf)
+            first, width = first + skip, min(take, width)
+            quantize(xq_w[a], xq_s[a], first, x_bf[:, skip : skip + width, :])
             for j0 in range(first, first + width, P):
                 back[a, j0] = back_psum.tile([P, PACK, P], F32, name="back")
                 for t in range(PACK):
@@ -191,8 +193,9 @@ def tile_list_tiert_xhl_gate_kernel(
         left_over(0)
         left_over(1)
         x_bf2 = woven("x_bf2", J_HALF, "ident1")
-        weave(2, x_bf2[:], nc.scalar.copy)
-        first_tier(2, x_bf2[:])
+        for j0 in range(0, J_HALF, P):
+            weave(2, x_bf2[:], nc.scalar.copy, j0, P)
+            first_tier(2, x_bf2[:], j0, P)
         second_tier(0, 0, J_HALF)
         left_over(2)
         x_bf_last = woven("x_bf_last", J, "x_raw1")
@@ -201,12 +204,12 @@ def tile_list_tiert_xhl_gate_kernel(
         weave(4, x_bf_last[:, J_HALF:, :], nc.scalar.copy)
         first_tier(4, x_bf_last[:, J_HALF:, :])
         second_tier(0, J_HALF, J_HALF)
-        rest.append(woven("rest1", J, "x_raw1"))
+        rest.append(woven("rest1", J, "rest1"))
         v_w = keep.tile([P, J], U32, name="v_w", tag="ident0", align_bytes=64)
         nc.vector.tensor_copy(v_w[:], tab_w[:].bitcast(U32).indirect(offsets[:]))
 
         parts = [
-            keep.tile([P, 2, N_HALF, PACK], BF16, name=f"parts{h}", tag=tag, align_bytes=64)[:]
+            keep.tile([P, 2, 2, P, PACK], BF16, name=f"parts{h}", tag=tag, align_bytes=64)[:]
             for h, tag in enumerate(("x_raw3", "parts1"))
         ]
 
@@ -215,17 +218,21 @@ def tile_list_tiert_xhl_gate_kernel(
             upper = woven(f"upper{h}", N_HALF, upper_tag)
             nc.scalar.copy(paired_words(upper[:]), paired_rows(halves[:, :, :, 1]))
             nc.vector.tensor_scalar(
-                parts[h][:, 0].rearrange("p n t -> p (n t)").bitcast(I32),
-                upper[:].rearrange("p n t -> p (n t)").bitcast(I32),
+                parts[h][:, :, 0].rearrange("p u n t -> p u (n t)").bitcast(I32),
+                upper[:].rearrange("p (u n) t -> p u (n t)", u=2).bitcast(I32),
                 HI_MASK,
                 None,
                 ALU.bitwise_and,
             )
 
         def split_lo(h):
-            nc.vector.tensor_tensor(
-                paired_words(parts[h][:, 1]), paired_rows(wt_raw[h][:]), paired_words(parts[h][:, 0]), ALU.subtract
-            )
+            for u in range(N_HALF // P):
+                nc.vector.tensor_tensor(
+                    paired_words(parts[h][:, u, 1]),
+                    paired_rows(wt_raw[h][:, :, u * P : (u + 1) * P]),
+                    paired_words(parts[h][:, u, 0]),
+                    ALU.subtract,
+                )
 
         left_over(3)
         left_over(4)
@@ -256,21 +263,21 @@ def tile_list_tiert_xhl_gate_kernel(
         sums = {}
 
         def table_passes(h):
-            w_w = keep.tile([P, 2, N_HALF], U32, name=f"w_w{h}", align_bytes=64)
-            w_s = keep.tile([P, 2, N_HALF], U8, name=f"w_s{h}", align_bytes=64)
-            nc.vector.quantize_mx(
-                out=w_w[:].rearrange("p s n -> p (s n)").bitcast(FP8X4),
-                scales=w_s[:].rearrange("p s n -> p (s n)"),
-                in_=parts[h].rearrange("p s n t -> p (s n t)"),
-            )
             for u in range(N_HALF // P):
                 nt = h * (N_HALF // P) + u
+                w_w = keep.tile([P, 2, P], U32, name=f"w_w{nt}", align_bytes=64)
+                w_s = keep.tile([P, 2, P], U8, name=f"w_s{nt}", align_bytes=64)
+                nc.vector.quantize_mx(
+                    out=w_w[:].rearrange("p s n -> p (s n)").bitcast(FP8X4),
+                    scales=w_s[:].rearrange("p s n -> p (s n)"),
+                    in_=parts[h][:, u].rearrange("p s n t -> p (s n t)"),
+                )
                 wx_pass(len(x_operands) - 1, nt)
                 for part in range(2):
                     nc.tensor.matmul_mx(
                         out=y[nt][:],
-                        lhsT=w_w[:, part, u * P : (u + 1) * P].bitcast(FP8X4),
-                        lhsT_scale=w_s[:, part, u * P : (u + 1) * P],
+                        lhsT=w_w[:, part, :].bitcast(FP8X4),
+                        lhsT_scale=w_s[:, part, :],
                         rhs=v_w[:].bitcast(FP8X4),
                         rhs_scale=v_s[:],
                         start=False,
@@ -290,9 +297,8 @@ def tile_list_tiert_xhl_gate_kernel(
             )
             nc.sync.dma_start(out[nt * P : (nt + 1) * P, first : first + width], result[:])
 
-        gate_and_store(0, 0, J)
         table_passes(1)
-        for nt in range(1, N_TILES - 1):
+        for nt in range(N_TILES - 1):
             gate_and_store(nt, 0, J)
         gate_and_store(N_TILES - 1, 0, J_HALF)
         gate_and_store(N_TILES - 1, J_HALF, J_HALF)

@@ -81,6 +81,7 @@ def tile_list_tiert_xhl_gate_kernel(
             )
 
         quantize_identity(0)
+        quantize_identity(1)
 
         x_raw = []
 
@@ -106,6 +107,7 @@ def tile_list_tiert_xhl_gate_kernel(
             nc.sync.dma_start(raw[:], wt[:, h * N_HALF : (h + 1) * N_HALF].rearrange("(p t) n -> p t n", t=PACK))
             wt_raw.append(raw)
 
+        load_wt(0)
         wx_w = keep.tile([P, X_PASSES, 2 * N], U8, name="wx_w", align_bytes=64)
         nc.sync.dma_start(wx_w[:].bitcast(I32), wx_words.rearrange("a p b -> p a b").bitcast(I32))
         for q in range(QUADRANTS):
@@ -113,7 +115,6 @@ def tile_list_tiert_xhl_gate_kernel(
                 wx_s[32 * q : 32 * q + 4, :, :].bitcast(I32),
                 wx_scales[:, 4 * q : 4 * q + 4, :].rearrange("a r n -> r a n").bitcast(I32),
             )
-        load_wt(0)
         load_wt(1)
         gates = []
 
@@ -174,14 +175,11 @@ def tile_list_tiert_xhl_gate_kernel(
         def woven(name, width, tag):
             return keep.tile([P, width, PACK], BF16, name=name, tag=tag, align_bytes=64)
 
-        v_rows = keep.tile([P, J], U8, name="v_rows", tag="ramp", align_bytes=64)
-        half = J_HALF // LIST_ROWS
-        nc.vector.tensor_copy(v_rows[:, :J_HALF], tab_s[:].indirect(offsets[:, :half]))
-        x_bf_first = woven("x_bf_first", J_HALF, "ident0")
-        weave(0, x_bf_first[:, :P, :], nc.vector.tensor_copy)
-        quantize_identity(1)
+        v_rows = keep.tile([P, J], U8, name="v_rows", tag="ident0", align_bytes=64)
+        nc.vector.tensor_copy(v_rows[:], tab_s[:].indirect(offsets[:]))
+        x_bf_first = woven("x_bf_first", J_HALF, "ramp")
+        weave(0, x_bf_first[:, :P, :], nc.scalar.copy)
         first_tier(0, x_bf_first[:, :P, :])
-        nc.vector.tensor_copy(v_rows[:, J_HALF:], tab_s[:].indirect(offsets[:, half:]))
         weave(1, x_bf_first[:, P:, :], nc.scalar.copy)
         first_tier(1, x_bf_first[:, P:, :])
         for q in range(QUADRANTS):
@@ -189,7 +187,7 @@ def tile_list_tiert_xhl_gate_kernel(
             nc.sync.dma_start(v_s[32 * q : 32 * q + 4, :].bitcast(I32), v_rows[first_row : first_row + 4, :].bitcast(I32))
         for nt in range(1, N_TILES):
             load_gate(nt)
-        rest.append(woven("rest0", J, "ident0"))
+        rest.append(woven("rest0", J, "ramp"))
         left_over(0)
         left_over(1)
         x_bf2 = woven("x_bf2", J_HALF, "ident1")
@@ -205,7 +203,7 @@ def tile_list_tiert_xhl_gate_kernel(
         first_tier(4, x_bf_last[:, J_HALF:, :])
         second_tier(0, J_HALF, J_HALF)
         rest.append(woven("rest1", J, "rest1"))
-        v_w = keep.tile([P, J], U32, name="v_w", tag="ident0", align_bytes=64)
+        v_w = keep.tile([P, J], U32, name="v_w", tag="ramp", align_bytes=64)
         nc.vector.tensor_copy(v_w[:], tab_w[:].bitcast(U32).indirect(offsets[:]))
 
         parts = [

@@ -22,6 +22,7 @@ X_PASSES = L // K_PASS
 N_TILES = N // P
 J_HALF = J // 2
 N_HALF = N // 2
+TILES_IN_HALF = N_HALF // P
 SCALE_ROWS = K_PASS // 32
 LIST_ROWS = 16
 
@@ -58,30 +59,24 @@ def tile_list_tiert_xhl_gate_kernel(
         nc.vector.memset(wx_s[:].rearrange("p a n -> p (a n)").bitcast(I32), 0)
 
         ramp = keep.tile([P, 2 * P], BF16, name="ramp", tag="ramp", align_bytes=64)
-        nc.gpsimd.iota(ramp[:], pattern=[[1, 2 * P]], base=0, channel_multiplier=-2, allow_small_or_imprecise_dtypes=True)
+        nc.gpsimd.iota(
+            ramp[:], pattern=[[1, 2 * P]], base=0, channel_multiplier=-2, allow_small_or_imprecise_dtypes=True
+        )
         id_w = keep.tile([P, K_PASS], U32, name="id_w", align_bytes=64)
         id_s = keep.tile([P, K_PASS], U8, name="id_s", align_bytes=64)
-        ident = (
-            keep.tile([P, 2, 2 * P], I32, name="ident0", tag="ident0", align_bytes=64),
-            keep.tile([P, 2, 2 * P], I32, name="ident1", tag="ident1", align_bytes=64),
-        )
+        ident = [keep.tile([P, 2, 2 * P], I32, name=f"ident{h}", tag=f"ident{h}", align_bytes=64) for h in range(2)]
         for t in range(PACK):
-            nc.vector.tensor_scalar(
-                ident[t // 2][:, t % 2, :], ramp[:], float(t // 2), float(BF16_ONE << (16 * (t % 2))), ALU.is_equal, ALU.mult
-            )
+            one = float(BF16_ONE << (16 * (t % 2)))
+            nc.vector.tensor_scalar(ident[t // 2][:, t % 2, :], ramp[:], float(t // 2), one, ALU.is_equal, ALU.mult)
         warm = keep.tile([P, 2], BF16, name="warm")
         nc.scalar.copy(warm[:], ident[1][:, 0, 0:1].bitcast(BF16))
-
-        def quantize_identity(h):
+        for h in range(2):
             cols = slice(h * 2 * P, (h + 1) * 2 * P)
             nc.vector.quantize_mx(
                 out=id_w[:, cols].bitcast(FP8X4),
                 scales=id_s[:, cols],
                 in_=ident[h][:].rearrange("p t f -> p (t f)").bitcast(BF16),
             )
-
-        quantize_identity(0)
-        quantize_identity(1)
 
         x_raw = []
 
@@ -123,8 +118,6 @@ def tile_list_tiert_xhl_gate_kernel(
             nc.sync.dma_start(g[:], gT[nt * P : (nt + 1) * P, :])
             gates.append(g)
 
-        load_gate(0)
-
         xq_w = [keep.tile([P, J], U32, name=f"xq_w{a}", align_bytes=64) for a in range(X_PASSES)]
         xq_s = [keep.tile([P, J], U8, name=f"xq_s{a}", align_bytes=64) for a in range(X_PASSES)]
         xr_w = [keep.tile([P, J], U32, name=f"xr_w{a}", align_bytes=64) for a in range(X_PASSES)]
@@ -138,14 +131,11 @@ def tile_list_tiert_xhl_gate_kernel(
                 out=words[:, cols].bitcast(FP8X4), scales=scales[:, cols], in_=values.rearrange("p j t -> p (j t)")
             )
 
-        def weave(c, x_bf, copy, skip=0, take=J_HALF):
-            cols = slice(skip, min(skip + take, X_CHUNKS[c][2]))
-            copy(paired_words(x_bf[:, cols, :]), paired_rows(x_raw[c][:, :, cols]))
-
-        def first_tier(c, x_bf, skip=0, take=J_HALF):
-            a, first, width = X_CHUNKS[c]
-            first, width = first + skip, min(take, width)
-            quantize(xq_w[a], xq_s[a], first, x_bf[:, skip : skip + width, :])
+        def first_tier(c, x_bf, skip=0):
+            a = X_CHUNKS[c][0]
+            first, width = X_CHUNKS[c][1] + skip, x_bf.shape[1]
+            nc.scalar.copy(paired_words(x_bf), paired_rows(x_raw[c][:, :, skip : skip + width]))
+            quantize(xq_w[a], xq_s[a], first, x_bf)
             for j0 in range(first, first + width, P):
                 back[a, j0] = back_psum.tile([P, PACK, P], F32, name="back")
                 for t in range(PACK):
@@ -178,28 +168,23 @@ def tile_list_tiert_xhl_gate_kernel(
         v_rows = keep.tile([P, J], U8, name="v_rows", tag="ident0", align_bytes=64)
         nc.vector.tensor_copy(v_rows[:], tab_s[:].indirect(offsets[:]))
         x_bf_first = woven("x_bf_first", J_HALF, "ramp")
-        weave(0, x_bf_first[:, :P, :], nc.scalar.copy)
         first_tier(0, x_bf_first[:, :P, :])
-        weave(1, x_bf_first[:, P:, :], nc.scalar.copy)
         first_tier(1, x_bf_first[:, P:, :])
         for q in range(QUADRANTS):
-            first_row = P - SCALE_ROWS + 4 * q
-            nc.sync.dma_start(v_s[32 * q : 32 * q + 4, :].bitcast(I32), v_rows[first_row : first_row + 4, :].bitcast(I32))
-        for nt in range(1, N_TILES):
+            gathered = slice(P - SCALE_ROWS + 4 * q, P - SCALE_ROWS + 4 * q + 4)
+            nc.sync.dma_start(v_s[32 * q : 32 * q + 4, :].bitcast(I32), v_rows[gathered, :].bitcast(I32))
+        for nt in range(N_TILES):
             load_gate(nt)
         rest.append(woven("rest0", J, "ramp"))
         left_over(0)
         left_over(1)
         x_bf2 = woven("x_bf2", J_HALF, "ident1")
         for j0 in range(0, J_HALF, P):
-            weave(2, x_bf2[:], nc.scalar.copy, j0, P)
-            first_tier(2, x_bf2[:], j0, P)
+            first_tier(2, x_bf2[:, j0 : j0 + P, :], j0)
         second_tier(0, 0, J_HALF)
         left_over(2)
         x_bf_last = woven("x_bf_last", J, "x_raw1")
-        weave(3, x_bf_last[:, :J_HALF, :], nc.scalar.copy)
         first_tier(3, x_bf_last[:, :J_HALF, :])
-        weave(4, x_bf_last[:, J_HALF:, :], nc.scalar.copy)
         first_tier(4, x_bf_last[:, J_HALF:, :])
         second_tier(0, J_HALF, J_HALF)
         rest.append(woven("rest1", J, "rest1"))
@@ -207,7 +192,7 @@ def tile_list_tiert_xhl_gate_kernel(
         nc.vector.tensor_copy(v_w[:], tab_w[:].bitcast(U32).indirect(offsets[:]))
 
         parts = [
-            keep.tile([P, 2, 2, P, PACK], BF16, name=f"parts{h}", tag=tag, align_bytes=64)[:]
+            keep.tile([P, TILES_IN_HALF, 2, P, PACK], BF16, name=f"parts{h}", tag=tag, align_bytes=64)[:]
             for h, tag in enumerate(("x_raw3", "parts1"))
         ]
 
@@ -217,14 +202,14 @@ def tile_list_tiert_xhl_gate_kernel(
             nc.scalar.copy(paired_words(upper[:]), paired_rows(halves[:, :, :, 1]))
             nc.vector.tensor_scalar(
                 parts[h][:, :, 0].rearrange("p u n t -> p u (n t)").bitcast(I32),
-                upper[:].rearrange("p (u n) t -> p u (n t)", u=2).bitcast(I32),
+                upper[:].rearrange("p (u n) t -> p u (n t)", u=TILES_IN_HALF).bitcast(I32),
                 HI_MASK,
                 None,
                 ALU.bitwise_and,
             )
 
         def split_lo(h):
-            for u in range(N_HALF // P):
+            for u in range(TILES_IN_HALF):
                 nc.vector.tensor_tensor(
                     paired_words(parts[h][:, u, 1]),
                     paired_rows(wt_raw[h][:, :, u * P : (u + 1) * P]),
@@ -237,10 +222,10 @@ def tile_list_tiert_xhl_gate_kernel(
         split_hi(0, "x_raw2")
         second_tier(1, 0, J)
         split_lo(0)
-        split_hi(1, "x_raw4")
 
         y = [y_psum.tile([P, J], F32, name=f"y{nt}") for nt in range(N_TILES)]
         x_operands = ((1, xq_w, xq_s), (0, xq_w, xq_s), (0, xr_w, xr_s), (1, xr_w, xr_s))
+        last_tile = N_TILES - 1
 
         def wx_pass(i, nt):
             a, words, scales = x_operands[i]
@@ -250,42 +235,49 @@ def tile_list_tiert_xhl_gate_kernel(
                 lhsT_scale=wx_s[:, a, P * nt : P * (nt + 1)],
                 rhs=words[a][:].bitcast(FP8X4),
                 rhs_scale=scales[a][:],
-                start=(i == 0),
-                stop=False,
+                start=(i == 0 and nt != last_tile),
+                stop=(i == len(x_operands) - 1 and nt == last_tile),
             )
 
         for i in range(len(x_operands) - 1):
-            for nt in range(N_TILES):
+            for nt in range(last_tile):
                 wx_pass(i, nt)
 
         sums = {}
 
-        def table_passes(h):
-            for u in range(N_HALF // P):
-                nt = h * (N_HALF // P) + u
-                w_w = keep.tile([P, 2, P], U32, name=f"w_w{nt}", align_bytes=64)
-                w_s = keep.tile([P, 2, P], U8, name=f"w_s{nt}", align_bytes=64)
-                nc.vector.quantize_mx(
-                    out=w_w[:].rearrange("p s n -> p (s n)").bitcast(FP8X4),
-                    scales=w_s[:].rearrange("p s n -> p (s n)"),
-                    in_=parts[h][:, u].rearrange("p s n t -> p (s n t)"),
-                )
+        def close_tile(nt):
+            h, u = divmod(nt, TILES_IN_HALF)
+            w_w = keep.tile([P, 2, P], U32, name=f"w_w{nt}", align_bytes=64)
+            w_s = keep.tile([P, 2, P], U8, name=f"w_s{nt}", align_bytes=64)
+            nc.vector.quantize_mx(
+                out=w_w[:].rearrange("p s n -> p (s n)").bitcast(FP8X4),
+                scales=w_s[:].rearrange("p s n -> p (s n)"),
+                in_=parts[h][:, u].rearrange("p s n t -> p (s n t)"),
+            )
+            if nt != last_tile:
                 wx_pass(len(x_operands) - 1, nt)
-                for part in range(2):
-                    nc.tensor.matmul_mx(
-                        out=y[nt][:],
-                        lhsT=w_w[:, part, :].bitcast(FP8X4),
-                        lhsT_scale=w_s[:, part, :],
-                        rhs=v_w[:].bitcast(FP8X4),
-                        rhs_scale=v_s[:],
-                        start=False,
-                        stop=(part == 1),
-                    )
-                sums[nt] = keep.tile([P, J], F32, name=f"sums{nt}")
-                nc.scalar.copy(sums[nt][:], y[nt][:])
+            for part in range(2):
+                nc.tensor.matmul_mx(
+                    out=y[nt][:],
+                    lhsT=w_w[:, part, :].bitcast(FP8X4),
+                    lhsT_scale=w_s[:, part, :],
+                    rhs=v_w[:].bitcast(FP8X4),
+                    rhs_scale=v_s[:],
+                    start=(part == 0 and nt == last_tile),
+                    stop=(part == 1 and nt != last_tile),
+                )
+            if nt == last_tile:
+                for i in range(len(x_operands)):
+                    wx_pass(i, nt)
+            sums[nt] = keep.tile([P, J], F32, name=f"sums{nt}")
+            nc.scalar.copy(sums[nt][:], y[nt][:])
 
-        table_passes(0)
+        close_tile(0)
+        split_hi(1, "x_raw4")
+        close_tile(1)
         split_lo(1)
+        close_tile(2)
+        close_tile(3)
 
         def gate_and_store(nt, first, width):
             result = keep.tile([P, width], F32, name=f"result{nt}_{first}")
@@ -295,7 +287,6 @@ def tile_list_tiert_xhl_gate_kernel(
             )
             nc.sync.dma_start(out[nt * P : (nt + 1) * P, first : first + width], result[:])
 
-        table_passes(1)
         for nt in range(N_TILES - 1):
             gate_and_store(nt, 0, J)
         gate_and_store(N_TILES - 1, 0, J_HALF)

@@ -102,7 +102,6 @@ def tile_list_tiert_xhl_gate_kernel(
             nc.sync.dma_start(raw[:], wt[:, h * N_HALF : (h + 1) * N_HALF].rearrange("(p t) n -> p t n", t=PACK))
             wt_raw.append(raw)
 
-        load_wt(0)
         wx_w = keep.tile([P, X_PASSES, 2 * N], U8, name="wx_w", align_bytes=64)
         nc.sync.dma_start(wx_w[:].bitcast(I32), wx_words.rearrange("a p b -> p a b").bitcast(I32))
         for q in range(QUADRANTS):
@@ -110,6 +109,7 @@ def tile_list_tiert_xhl_gate_kernel(
                 wx_s[32 * q : 32 * q + 4, :, :].bitcast(I32),
                 wx_scales[:, 4 * q : 4 * q + 4, :].rearrange("a r n -> r a n").bitcast(I32),
             )
+        load_wt(0)
         load_wt(1)
         gates = []
 
@@ -193,7 +193,7 @@ def tile_list_tiert_xhl_gate_kernel(
 
         parts = [
             keep.tile([P, TILES_IN_HALF, 2, P, PACK], BF16, name=f"parts{h}", tag=tag, align_bytes=64)[:]
-            for h, tag in enumerate(("x_raw3", "parts1"))
+            for h, tag in enumerate(("x_raw4", "rest1"))
         ]
 
         def split_hi(h, upper_tag):
@@ -219,13 +219,13 @@ def tile_list_tiert_xhl_gate_kernel(
 
         left_over(3)
         left_over(4)
+        second_tier(1, 0, J_HALF)
         split_hi(0, "x_raw2")
-        second_tier(1, 0, J)
+        second_tier(1, J_HALF, J_HALF)
         split_lo(0)
 
         y = [y_psum.tile([P, J], F32, name=f"y{nt}") for nt in range(N_TILES)]
         x_operands = ((1, xq_w, xq_s), (0, xq_w, xq_s), (0, xr_w, xr_s), (1, xr_w, xr_s))
-        last_tile = N_TILES - 1
 
         def wx_pass(i, nt):
             a, words, scales = x_operands[i]
@@ -235,12 +235,12 @@ def tile_list_tiert_xhl_gate_kernel(
                 lhsT_scale=wx_s[:, a, P * nt : P * (nt + 1)],
                 rhs=words[a][:].bitcast(FP8X4),
                 rhs_scale=scales[a][:],
-                start=(i == 0 and nt != last_tile),
-                stop=(i == len(x_operands) - 1 and nt == last_tile),
+                start=(i == 0),
+                stop=False,
             )
 
         for i in range(len(x_operands) - 1):
-            for nt in range(last_tile):
+            for nt in range(N_TILES):
                 wx_pass(i, nt)
 
         sums = {}
@@ -254,8 +254,7 @@ def tile_list_tiert_xhl_gate_kernel(
                 scales=w_s[:].rearrange("p s n -> p (s n)"),
                 in_=parts[h][:, u].rearrange("p s n t -> p (s n t)"),
             )
-            if nt != last_tile:
-                wx_pass(len(x_operands) - 1, nt)
+            wx_pass(len(x_operands) - 1, nt)
             for part in range(2):
                 nc.tensor.matmul_mx(
                     out=y[nt][:],
@@ -263,17 +262,14 @@ def tile_list_tiert_xhl_gate_kernel(
                     lhsT_scale=w_s[:, part, :],
                     rhs=v_w[:].bitcast(FP8X4),
                     rhs_scale=v_s[:],
-                    start=(part == 0 and nt == last_tile),
-                    stop=(part == 1 and nt != last_tile),
+                    start=False,
+                    stop=(part == 1),
                 )
-            if nt == last_tile:
-                for i in range(len(x_operands)):
-                    wx_pass(i, nt)
             sums[nt] = keep.tile([P, J], F32, name=f"sums{nt}")
             nc.scalar.copy(sums[nt][:], y[nt][:])
 
         close_tile(0)
-        split_hi(1, "x_raw4")
+        split_hi(1, "x_raw3")
         close_tile(1)
         split_lo(1)
         close_tile(2)

@@ -78,6 +78,18 @@ def tile_list_tiert_xhl_gate_kernel(
                 in_=ident[h][:].rearrange("p t f -> p (t f)").bitcast(BF16),
             )
 
+        warm_sum = y_psum.tile([P, 2 * P], F32, name="warm_sum", tag="y3")
+        for i in range(4):
+            nc.tensor.matmul_mx(
+                out=warm_sum[:],
+                lhsT=id_w[:, :P].bitcast(FP8X4),
+                lhsT_scale=id_s[:, :P],
+                rhs=id_w[:, : 2 * P].bitcast(FP8X4),
+                rhs_scale=id_s[:, : 2 * P],
+                start=True,
+                stop=True,
+            )
+
         x_raw = []
 
         def load_x(c):
@@ -188,7 +200,7 @@ def tile_list_tiert_xhl_gate_kernel(
         first_tier(4, x_bf_last[:, J_HALF:, :])
         second_tier(0, J_HALF, J_HALF)
         rest.append(woven("rest1", J, "rest1"))
-        v_w = keep.tile([P, J], U32, name="v_w", tag="ramp", align_bytes=64)
+        v_w = keep.tile([P, J], U32, name="v_w", tag="x_raw2", align_bytes=64)
         nc.vector.tensor_copy(v_w[:], tab_w[:].bitcast(U32).indirect(offsets[:]))
 
         parts = [
@@ -220,11 +232,11 @@ def tile_list_tiert_xhl_gate_kernel(
         left_over(3)
         left_over(4)
         second_tier(1, 0, J_HALF)
-        split_hi(0, "x_raw2")
+        split_hi(0, "ramp")
         second_tier(1, J_HALF, J_HALF)
         split_lo(0)
 
-        y = [y_psum.tile([P, J], F32, name=f"y{nt}") for nt in range(N_TILES)]
+        y = [y_psum.tile([P, J], F32, name=f"y{nt}", tag=f"y{nt}") for nt in range(N_TILES)]
         x_operands = ((1, xq_w, xq_s), (0, xq_w, xq_s), (0, xr_w, xr_s), (1, xr_w, xr_s))
 
         def wx_pass(i, nt):
@@ -285,5 +297,5 @@ def tile_list_tiert_xhl_gate_kernel(
 
         for nt in range(N_TILES - 1):
             gate_and_store(nt, 0, J)
-        gate_and_store(N_TILES - 1, 0, J_HALF)
-        gate_and_store(N_TILES - 1, J_HALF, J_HALF)
+        gate_and_store(N_TILES - 1, 0, J - P)
+        gate_and_store(N_TILES - 1, J - P, P)

@@ -28,9 +28,12 @@ LIST_ROWS = 16
 
 FLOPS = 2 * J * (2 * K * N + 2 * L * N + L * K_PASS)
 
-X_CHUNKS = ((0, 0, P), (0, P, P), (0, J_HALF, J_HALF), (1, 0, J_HALF), (1, J_HALF, J_HALF))
+X_CHUNKS = ((0, 0, P), (0, P, P), (0, J_HALF, J_HALF), (1, 0, J))
 
-HI_MASK = -983056
+POOL_COLS = 192
+
+HI_MASK = -1048576
+HI_MASK_PAIR = -983056
 BF16_ONE = 0x3F80
 
 
@@ -104,16 +107,15 @@ def tile_list_tiert_xhl_gate_kernel(
         nc.sync.dma_start(tab_s[P - SCALE_ROWS :, :].bitcast(I32), tab_scales[0].bitcast(I32))
         for c in range(len(X_CHUNKS)):
             load_x(c)
-        tab_w = keep.tile([P, T], I32, name="tab_w", align_bytes=64)
+        tab_w = keep.tile([P, T], I32, name="tab_w", tag="tab_w", align_bytes=64)
         nc.sync.dma_start(tab_w[:], tab_words[0].rearrange("p t i -> p (t i)").bitcast(I32))
 
-        wt_raw = []
+        def load_wt(name, first, width):
+            raw = keep.tile([P, PACK, width], F32, name=name)
+            nc.sync.dma_start(raw[:], wt[:, first : first + width].rearrange("(p t) n -> p t n", t=PACK))
+            return raw
 
-        def load_wt(h):
-            raw = keep.tile([P, PACK, N_HALF], F32, name=f"wt_raw{h}")
-            nc.sync.dma_start(raw[:], wt[:, h * N_HALF : (h + 1) * N_HALF].rearrange("(p t) n -> p t n", t=PACK))
-            wt_raw.append(raw)
-
+        wt_pool = load_wt("wt_pool", 0, POOL_COLS)
         wx_w = keep.tile([P, X_PASSES, 2 * N], U8, name="wx_w", align_bytes=64)
         nc.sync.dma_start(wx_w[:].bitcast(I32), wx_words.rearrange("a p b -> p a b").bitcast(I32))
         for q in range(QUADRANTS):
@@ -121,8 +123,7 @@ def tile_list_tiert_xhl_gate_kernel(
                 wx_s[32 * q : 32 * q + 4, :, :].bitcast(I32),
                 wx_scales[:, 4 * q : 4 * q + 4, :].rearrange("a r n -> r a n").bitcast(I32),
             )
-        load_wt(0)
-        load_wt(1)
+        wt_rest = load_wt("wt_rest", POOL_COLS, N - POOL_COLS)
         gates = []
 
         def load_gate(nt):
@@ -195,46 +196,65 @@ def tile_list_tiert_xhl_gate_kernel(
             first_tier(2, x_bf2[:, j0 : j0 + P, :], j0)
         second_tier(0, 0, J_HALF)
         left_over(2)
-        x_bf_last = woven("x_bf_last", J, "x_raw1")
-        first_tier(3, x_bf_last[:, :J_HALF, :])
-        first_tier(4, x_bf_last[:, J_HALF:, :])
         second_tier(0, J_HALF, J_HALF)
-        rest.append(woven("rest1", J, "rest1"))
         v_w = keep.tile([P, J], U32, name="v_w", tag="x_raw2", align_bytes=64)
         nc.vector.tensor_copy(v_w[:], tab_w[:].bitcast(U32).indirect(offsets[:]))
+        x_bf_last = woven("x_bf_last", J, "x_raw0")
+        first_tier(3, x_bf_last[:, :J_HALF, :])
+        first_tier(3, x_bf_last[:, J_HALF:, :], J_HALF)
+        hi_rows = keep.tile([P, PACK, POOL_COLS], I32, name="hi_rows", tag="tab_w", align_bytes=64)
+        nc.vector.tensor_scalar(hi_rows[:], wt_pool[:].bitcast(I32), HI_MASK, None, ALU.bitwise_and)
 
-        parts = [
-            keep.tile([P, TILES_IN_HALF, 2, P, PACK], BF16, name=f"parts{h}", tag=tag, align_bytes=64)[:]
-            for h, tag in enumerate(("x_raw4", "rest1"))
-        ]
+        late = woven("late", J + POOL_COLS, "x_raw0")
+        rest.append(late[:, :J, :])
+        lo_rows = late[:, J:, :].rearrange("p n t -> p (n t)")
+        nc.gpsimd.tensor_tensor(
+            lo_rows,
+            wt_pool[:].rearrange("p t n -> p (t n)"),
+            hi_rows[:].bitcast(F32).rearrange("p t n -> p (t n)"),
+            ALU.subtract,
+        )
+        lo_rows = lo_rows.rearrange("p (t n) -> p t n", t=PACK)
+        left_over(3)
 
-        def split_hi(h, upper_tag):
-            halves = wt_raw[h][:].bitcast(BF16).rearrange("p t (n e) -> p t n e", e=2)
-            upper = woven(f"upper{h}", N_HALF, upper_tag)
-            nc.scalar.copy(paired_words(upper[:]), paired_rows(halves[:, :, :, 1]))
-            nc.vector.tensor_scalar(
-                parts[h][:, :, 0].rearrange("p u n t -> p u (n t)").bitcast(I32),
-                upper[:].rearrange("p (u n) t -> p u (n t)", u=TILES_IN_HALF).bitcast(I32),
-                HI_MASK,
-                None,
-                ALU.bitwise_and,
+        hi = woven("hi", N, "hi")
+        lo = woven("lo", N, "lo")
+        nc.scalar.copy(paired_words(hi[:, :POOL_COLS, :]), paired_rows(hi_rows[:].bitcast(F32)))
+        halves = wt_rest[:].bitcast(BF16).rearrange("p t (n e) -> p t n e", e=2)
+        upper = woven("upper", N - POOL_COLS, "ident1")
+        nc.scalar.copy(paired_words(upper[:]), paired_rows(halves[:, :, :, 1]))
+        nc.scalar.copy(paired_words(lo[:, :POOL_COLS, :]), paired_rows(lo_rows))
+
+        hi_w = keep.tile([P, N], U32, name="hi_w", tag="x_raw3", align_bytes=64)
+        hi_s = keep.tile([P, N], U8, name="hi_s", align_bytes=64)
+        lo_w = keep.tile([P, N], U32, name="lo_w", align_bytes=64)
+        lo_s = keep.tile([P, N], U8, name="lo_s", align_bytes=64)
+
+        def split_lo(first, last):
+            nc.vector.tensor_tensor(
+                paired_words(lo[:, first:last, :]),
+                paired_rows(wt_rest[:, :, first - POOL_COLS : last - POOL_COLS]),
+                paired_words(hi[:, first:last, :]),
+                ALU.subtract,
             )
 
-        def split_lo(h):
-            for u in range(TILES_IN_HALF):
-                nc.vector.tensor_tensor(
-                    paired_words(parts[h][:, u, 1]),
-                    paired_rows(wt_raw[h][:, :, u * P : (u + 1) * P]),
-                    paired_words(parts[h][:, u, 0]),
-                    ALU.subtract,
-                )
-
-        left_over(3)
-        left_over(4)
         second_tier(1, 0, J_HALF)
-        split_hi(0, "ramp")
+        nc.vector.tensor_scalar(
+            hi[:, POOL_COLS:, :].rearrange("p n t -> p (n t)").bitcast(I32),
+            upper[:].rearrange("p n t -> p (n t)").bitcast(I32),
+            HI_MASK_PAIR,
+            None,
+            ALU.bitwise_and,
+        )
         second_tier(1, J_HALF, J_HALF)
-        split_lo(0)
+        quantize(hi_w, hi_s, 0, hi[:, :N_HALF, :])
+        split_lo(POOL_COLS, N_HALF)
+        quantize(lo_w, lo_s, 0, lo[:, :P, :])
+        split_lo(N_HALF, N_HALF + P)
+        quantize(lo_w, lo_s, P, lo[:, P:N_HALF, :])
+        split_lo(N_HALF + P, N)
+        quantize(hi_w, hi_s, N_HALF, hi[:, N_HALF:, :])
+        quantize(lo_w, lo_s, N_HALF, lo[:, N_HALF:, :])
 
         y = [y_psum.tile([P, J], F32, name=f"y{nt}", tag=f"y{nt}") for nt in range(N_TILES)]
         x_operands = ((1, xq_w, xq_s), (0, xq_w, xq_s), (0, xr_w, xr_s), (1, xr_w, xr_s))
@@ -256,36 +276,20 @@ def tile_list_tiert_xhl_gate_kernel(
                 wx_pass(i, nt)
 
         sums = {}
-
-        def close_tile(nt):
-            h, u = divmod(nt, TILES_IN_HALF)
-            w_w = keep.tile([P, 2, P], U32, name=f"w_w{nt}", align_bytes=64)
-            w_s = keep.tile([P, 2, P], U8, name=f"w_s{nt}", align_bytes=64)
-            nc.vector.quantize_mx(
-                out=w_w[:].rearrange("p s n -> p (s n)").bitcast(FP8X4),
-                scales=w_s[:].rearrange("p s n -> p (s n)"),
-                in_=parts[h][:, u].rearrange("p s n t -> p (s n t)"),
-            )
+        for nt in range(N_TILES):
             wx_pass(len(x_operands) - 1, nt)
-            for part in range(2):
+            for words, scales in ((hi_w, hi_s), (lo_w, lo_s)):
                 nc.tensor.matmul_mx(
                     out=y[nt][:],
-                    lhsT=w_w[:, part, :].bitcast(FP8X4),
-                    lhsT_scale=w_s[:, part, :],
+                    lhsT=words[:, P * nt : P * (nt + 1)].bitcast(FP8X4),
+                    lhsT_scale=scales[:, P * nt : P * (nt + 1)],
                     rhs=v_w[:].bitcast(FP8X4),
                     rhs_scale=v_s[:],
                     start=False,
-                    stop=(part == 1),
+                    stop=(words is lo_w),
                 )
             sums[nt] = keep.tile([P, J], F32, name=f"sums{nt}")
             nc.scalar.copy(sums[nt][:], y[nt][:])
-
-        close_tile(0)
-        split_hi(1, "x_raw3")
-        close_tile(1)
-        split_lo(1)
-        close_tile(2)
-        close_tile(3)
 
         def gate_and_store(nt, first, width):
             result = keep.tile([P, width], F32, name=f"result{nt}_{first}")

@@ -72,7 +72,7 @@ def tile_list_tiert_xhl_gate_kernel(
             one = float(BF16_ONE << (16 * (t % 2)))
             nc.vector.tensor_scalar(ident[t // 2][:, t % 2, :], ramp[:], float(t // 2), one, ALU.is_equal, ALU.mult)
         warm = keep.tile([P, 2], BF16, name="warm")
-        nc.scalar.copy(warm[:], ident[1][:, 0, 0:1].bitcast(BF16))
+        nc.scalar.copy(warm[:], ramp[:, 0:2])
         for h in range(2):
             cols = slice(h * 2 * P, (h + 1) * 2 * P)
             nc.vector.quantize_mx(
@@ -102,10 +102,11 @@ def tile_list_tiert_xhl_gate_kernel(
             nc.sync.dma_start(raw[:], rows.rearrange("(p t) j -> p t j", t=PACK))
             x_raw.append(raw)
 
+        load_x(0)
         offsets = keep.tile([P, J // LIST_ROWS], U16, name="offsets")
         nc.sync.dma_start(offsets[:], offs)
         nc.sync.dma_start(tab_s[P - SCALE_ROWS :, :].bitcast(I32), tab_scales[0].bitcast(I32))
-        for c in range(len(X_CHUNKS)):
+        for c in range(1, len(X_CHUNKS)):
             load_x(c)
         tab_w = keep.tile([P, T], I32, name="tab_w", tag="tab_w", align_bytes=64)
         nc.sync.dma_start(tab_w[:], tab_words[0].rearrange("p t i -> p (t i)").bitcast(I32))
@@ -178,20 +179,20 @@ def tile_list_tiert_xhl_gate_kernel(
         def woven(name, width, tag):
             return keep.tile([P, width, PACK], BF16, name=name, tag=tag, align_bytes=64)
 
-        v_rows = keep.tile([P, J], U8, name="v_rows", tag="ident0", align_bytes=64)
+        v_rows = keep.tile([P, J], U8, name="v_rows", tag="ident1", align_bytes=64)
         nc.vector.tensor_copy(v_rows[:], tab_s[:].indirect(offsets[:]))
-        x_bf_first = woven("x_bf_first", J_HALF, "ramp")
+        x_bf_first = woven("x_bf_first", J, "ramp")
         first_tier(0, x_bf_first[:, :P, :])
-        first_tier(1, x_bf_first[:, P:, :])
+        first_tier(1, x_bf_first[:, P:J_HALF, :])
         for q in range(QUADRANTS):
             gathered = slice(P - SCALE_ROWS + 4 * q, P - SCALE_ROWS + 4 * q + 4)
             nc.sync.dma_start(v_s[32 * q : 32 * q + 4, :].bitcast(I32), v_rows[gathered, :].bitcast(I32))
         for nt in range(N_TILES):
             load_gate(nt)
-        rest.append(woven("rest0", J, "ramp"))
+        rest.append(woven("rest0", J, "rest0"))
         left_over(0)
         left_over(1)
-        x_bf2 = woven("x_bf2", J_HALF, "ident1")
+        x_bf2 = x_bf_first[:, J_HALF:, :]
         for j0 in range(0, J_HALF, P):
             first_tier(2, x_bf2[:, j0 : j0 + P, :], j0)
         second_tier(0, 0, J_HALF)
@@ -221,9 +222,20 @@ def tile_list_tiert_xhl_gate_kernel(
         lo = woven("lo", N, "lo")
         nc.scalar.copy(paired_words(hi[:, :POOL_COLS, :]), paired_rows(hi_rows[:].bitcast(F32)))
         halves = wt_rest[:].bitcast(BF16).rearrange("p t (n e) -> p t n e", e=2)
-        upper = woven("upper", N - POOL_COLS, "ident1")
-        nc.scalar.copy(paired_words(upper[:]), paired_rows(halves[:, :, :, 1]))
-        nc.scalar.copy(paired_words(lo[:, :POOL_COLS, :]), paired_rows(lo_rows))
+        upper = woven("upper", N - POOL_COLS, "ramp")
+        last_tile = N - P
+
+        def weave_upper(first, last):
+            cols = slice(first - POOL_COLS, last - POOL_COLS)
+            nc.scalar.copy(paired_words(upper[:, cols, :]), paired_rows(halves[:, :, cols, 1]))
+
+        def weave_lo(first, last):
+            nc.scalar.copy(paired_words(lo[:, first:last, :]), paired_rows(lo_rows[:, :, first:last]))
+
+        weave_upper(POOL_COLS, last_tile)
+        weave_lo(0, P)
+        weave_upper(last_tile, N)
+        weave_lo(P, POOL_COLS)
 
         hi_w = keep.tile([P, N], U32, name="hi_w", tag="x_raw3", align_bytes=64)
         hi_s = keep.tile([P, N], U8, name="hi_s", align_bytes=64)
@@ -238,28 +250,32 @@ def tile_list_tiert_xhl_gate_kernel(
                 ALU.subtract,
             )
 
+        def split_hi(first, last):
+            nc.vector.tensor_scalar(
+                hi[:, first:last, :].rearrange("p n t -> p (n t)").bitcast(I32),
+                upper[:, first - POOL_COLS : last - POOL_COLS, :].rearrange("p n t -> p (n t)").bitcast(I32),
+                HI_MASK_PAIR,
+                None,
+                ALU.bitwise_and,
+            )
+
         second_tier(1, 0, J_HALF)
-        nc.vector.tensor_scalar(
-            hi[:, POOL_COLS:, :].rearrange("p n t -> p (n t)").bitcast(I32),
-            upper[:].rearrange("p n t -> p (n t)").bitcast(I32),
-            HI_MASK_PAIR,
-            None,
-            ALU.bitwise_and,
-        )
+        split_hi(POOL_COLS, last_tile)
         second_tier(1, J_HALF, J_HALF)
         quantize(hi_w, hi_s, 0, hi[:, :N_HALF, :])
-        split_lo(POOL_COLS, N_HALF)
         quantize(lo_w, lo_s, 0, lo[:, :P, :])
-        split_lo(N_HALF, N_HALF + P)
+        split_lo(POOL_COLS, N_HALF)
+        split_hi(last_tile, N)
+        split_lo(N_HALF, last_tile)
         quantize(lo_w, lo_s, P, lo[:, P:N_HALF, :])
-        split_lo(N_HALF + P, N)
+        split_lo(last_tile, N)
         quantize(hi_w, hi_s, N_HALF, hi[:, N_HALF:, :])
         quantize(lo_w, lo_s, N_HALF, lo[:, N_HALF:, :])
 
         y = [y_psum.tile([P, J], F32, name=f"y{nt}", tag=f"y{nt}") for nt in range(N_TILES)]
         x_operands = ((1, xq_w, xq_s), (0, xq_w, xq_s), (0, xr_w, xr_s), (1, xr_w, xr_s))
 
-        def wx_pass(i, nt):
+        def wx_pass(i, nt, start=False):
             a, words, scales = x_operands[i]
             nc.tensor.matmul_mx(
                 out=y[nt][:],
@@ -267,17 +283,20 @@ def tile_list_tiert_xhl_gate_kernel(
                 lhsT_scale=wx_s[:, a, P * nt : P * (nt + 1)],
                 rhs=words[a][:].bitcast(FP8X4),
                 rhs_scale=scales[a][:],
-                start=(i == 0),
+                start=start,
                 stop=False,
             )
 
         for i in range(len(x_operands) - 1):
-            for nt in range(N_TILES):
-                wx_pass(i, nt)
+            for nt in range(N_TILES - 1):
+                wx_pass(i, nt, start=(i == 0))
 
         sums = {}
         for nt in range(N_TILES):
-            wx_pass(len(x_operands) - 1, nt)
+            wx_pass(len(x_operands) - 1, nt, start=(nt == N_TILES - 1))
+            if nt == N_TILES - 1:
+                for i in range(len(x_operands) - 1):
+                    wx_pass(i, nt)
             for words, scales in ((hi_w, hi_s), (lo_w, lo_s)):
                 nc.tensor.matmul_mx(
                     out=y[nt][:],

@@ -20,9 +20,9 @@ K_PASS = P * PACK
 QUADRANTS = 4
 X_PASSES = L // K_PASS
 N_TILES = N // P
+LAST_TILE = N - P
 J_HALF = J // 2
 N_HALF = N // 2
-TILES_IN_HALF = N_HALF // P
 SCALE_ROWS = K_PASS // 32
 LIST_ROWS = 16
 
@@ -31,6 +31,7 @@ FLOPS = 2 * J * (2 * K * N + 2 * L * N + L * K_PASS)
 X_CHUNKS = ((0, 0, P), (0, P, P), (0, J_HALF, J_HALF), (1, 0, J))
 
 POOL_COLS = 192
+WARM_PASSES = 4
 
 HI_MASK = -1048576
 HI_MASK_PAIR = -983056
@@ -81,8 +82,8 @@ def tile_list_tiert_xhl_gate_kernel(
                 in_=ident[h][:].rearrange("p t f -> p (t f)").bitcast(BF16),
             )
 
-        warm_sum = y_psum.tile([P, 2 * P], F32, name="warm_sum", tag="y3")
-        for i in range(4):
+        warm_sum = y_psum.tile([P, 2 * P], F32, name="warm_sum", tag=f"y{N_TILES - 1}")
+        for i in range(WARM_PASSES):
             nc.tensor.matmul_mx(
                 out=warm_sum[:],
                 lhsT=id_w[:, :P].bitcast(FP8X4),
@@ -116,15 +117,15 @@ def tile_list_tiert_xhl_gate_kernel(
             nc.sync.dma_start(raw[:], wt[:, first : first + width].rearrange("(p t) n -> p t n", t=PACK))
             return raw
 
-        wt_pool = load_wt("wt_pool", 0, POOL_COLS)
-        wx_w = keep.tile([P, X_PASSES, 2 * N], U8, name="wx_w", align_bytes=64)
-        nc.sync.dma_start(wx_w[:].bitcast(I32), wx_words.rearrange("a p b -> p a b").bitcast(I32))
+        wt_most = load_wt("wt_most", 0, LAST_TILE)
         for q in range(QUADRANTS):
             nc.sync.dma_start(
                 wx_s[32 * q : 32 * q + 4, :, :].bitcast(I32),
                 wx_scales[:, 4 * q : 4 * q + 4, :].rearrange("a r n -> r a n").bitcast(I32),
             )
-        wt_rest = load_wt("wt_rest", POOL_COLS, N - POOL_COLS)
+        wx_w = keep.tile([P, X_PASSES, 2 * N], U8, name="wx_w", align_bytes=64)
+        nc.sync.dma_start(wx_w[:].bitcast(I32), wx_words.rearrange("a p b -> p a b").bitcast(I32))
+        wt_last = load_wt("wt_last", LAST_TILE, P)
         gates = []
 
         def load_gate(nt):
@@ -192,9 +193,8 @@ def tile_list_tiert_xhl_gate_kernel(
         rest.append(woven("rest0", J, "rest0"))
         left_over(0)
         left_over(1)
-        x_bf2 = x_bf_first[:, J_HALF:, :]
         for j0 in range(0, J_HALF, P):
-            first_tier(2, x_bf2[:, j0 : j0 + P, :], j0)
+            first_tier(2, x_bf_first[:, J_HALF + j0 : J_HALF + j0 + P, :], j0)
         second_tier(0, 0, J_HALF)
         left_over(2)
         second_tier(0, J_HALF, J_HALF)
@@ -204,37 +204,31 @@ def tile_list_tiert_xhl_gate_kernel(
         first_tier(3, x_bf_last[:, :J_HALF, :])
         first_tier(3, x_bf_last[:, J_HALF:, :], J_HALF)
         hi_rows = keep.tile([P, PACK, POOL_COLS], I32, name="hi_rows", tag="tab_w", align_bytes=64)
-        nc.vector.tensor_scalar(hi_rows[:], wt_pool[:].bitcast(I32), HI_MASK, None, ALU.bitwise_and)
+        wt_pool = wt_most[:, :, :POOL_COLS]
+        nc.vector.tensor_scalar(hi_rows[:], wt_pool.bitcast(I32), HI_MASK, None, ALU.bitwise_and)
 
         late = woven("late", J + POOL_COLS, "x_raw0")
         rest.append(late[:, :J, :])
-        lo_rows = late[:, J:, :].rearrange("p n t -> p (n t)")
-        nc.gpsimd.tensor_tensor(
-            lo_rows,
-            wt_pool[:].rearrange("p t n -> p (t n)"),
-            hi_rows[:].bitcast(F32).rearrange("p t n -> p (t n)"),
-            ALU.subtract,
-        )
-        lo_rows = lo_rows.rearrange("p (t n) -> p t n", t=PACK)
+        lo_rows = late[:, J:, :].rearrange("p n t -> p (n t)").rearrange("p (t n) -> p t n", t=PACK)
+        nc.gpsimd.tensor_tensor(lo_rows, wt_pool, hi_rows[:].bitcast(F32), ALU.subtract)
         left_over(3)
 
         hi = woven("hi", N, "hi")
         lo = woven("lo", N, "lo")
         nc.scalar.copy(paired_words(hi[:, :POOL_COLS, :]), paired_rows(hi_rows[:].bitcast(F32)))
-        halves = wt_rest[:].bitcast(BF16).rearrange("p t (n e) -> p t n e", e=2)
-        upper = woven("upper", N - POOL_COLS, "ramp")
-        last_tile = N - P
 
-        def weave_upper(first, last):
-            cols = slice(first - POOL_COLS, last - POOL_COLS)
-            nc.scalar.copy(paired_words(upper[:, cols, :]), paired_rows(halves[:, :, cols, 1]))
+        def upper_halves(name, rows, tag):
+            upper = woven(name, rows.shape[2], tag)
+            halves = rows.bitcast(BF16).rearrange("p t (n e) -> p t n e", e=2)
+            nc.scalar.copy(paired_words(upper[:]), paired_rows(halves[:, :, :, 1]))
+            return upper
 
         def weave_lo(first, last):
             nc.scalar.copy(paired_words(lo[:, first:last, :]), paired_rows(lo_rows[:, :, first:last]))
 
-        weave_upper(POOL_COLS, last_tile)
+        upper_mid = upper_halves("upper_mid", wt_most[:, :, POOL_COLS:], "ramp")
         weave_lo(0, P)
-        weave_upper(last_tile, N)
+        upper_last = upper_halves("upper_last", wt_last[:], "tab_w")
         weave_lo(P, POOL_COLS)
 
         hi_w = keep.tile([P, N], U32, name="hi_w", tag="x_raw3", align_bytes=64)
@@ -242,33 +236,31 @@ def tile_list_tiert_xhl_gate_kernel(
         lo_w = keep.tile([P, N], U32, name="lo_w", align_bytes=64)
         lo_s = keep.tile([P, N], U8, name="lo_s", align_bytes=64)
 
-        def split_lo(first, last):
-            nc.vector.tensor_tensor(
-                paired_words(lo[:, first:last, :]),
-                paired_rows(wt_rest[:, :, first - POOL_COLS : last - POOL_COLS]),
-                paired_words(hi[:, first:last, :]),
-                ALU.subtract,
-            )
-
-        def split_hi(first, last):
+        def split_hi(first, upper):
             nc.vector.tensor_scalar(
-                hi[:, first:last, :].rearrange("p n t -> p (n t)").bitcast(I32),
-                upper[:, first - POOL_COLS : last - POOL_COLS, :].rearrange("p n t -> p (n t)").bitcast(I32),
+                hi[:, first : first + upper.shape[1], :].rearrange("p n t -> p (n t)").bitcast(I32),
+                upper[:].rearrange("p n t -> p (n t)").bitcast(I32),
                 HI_MASK_PAIR,
                 None,
                 ALU.bitwise_and,
             )
 
+        def split_lo(first, rows):
+            cols = slice(first, first + rows.shape[2])
+            nc.vector.tensor_tensor(
+                paired_words(lo[:, cols, :]), paired_rows(rows), paired_words(hi[:, cols, :]), ALU.subtract
+            )
+
         second_tier(1, 0, J_HALF)
-        split_hi(POOL_COLS, last_tile)
+        split_hi(POOL_COLS, upper_mid)
         second_tier(1, J_HALF, J_HALF)
         quantize(hi_w, hi_s, 0, hi[:, :N_HALF, :])
         quantize(lo_w, lo_s, 0, lo[:, :P, :])
-        split_lo(POOL_COLS, N_HALF)
-        split_hi(last_tile, N)
-        split_lo(N_HALF, last_tile)
+        split_lo(POOL_COLS, wt_most[:, :, POOL_COLS:N_HALF])
+        split_hi(LAST_TILE, upper_last)
+        split_lo(N_HALF, wt_most[:, :, N_HALF:])
         quantize(lo_w, lo_s, P, lo[:, P:N_HALF, :])
-        split_lo(last_tile, N)
+        split_lo(LAST_TILE, wt_last[:])
         quantize(hi_w, hi_s, N_HALF, hi[:, N_HALF:, :])
         quantize(lo_w, lo_s, N_HALF, lo[:, N_HALF:, :])
 

@@ -20,7 +20,6 @@ K_PASS = P * PACK
 QUADRANTS = 4
 X_PASSES = L // K_PASS
 N_TILES = N // P
-LAST_TILE = N - P
 J_HALF = J // 2
 N_HALF = N // 2
 SCALE_ROWS = K_PASS // 32
@@ -28,9 +27,7 @@ LIST_ROWS = 16
 
 FLOPS = 2 * J * (2 * K * N + 2 * L * N + L * K_PASS)
 
-X_CHUNKS = ((0, 0, P), (0, P, P), (0, J_HALF, J_HALF), (1, 0, J))
-
-POOL_COLS = 192
+POOL_COLS = N_HALF
 WARM_PASSES = 4
 
 HI_MASK = -1048576
@@ -68,7 +65,10 @@ def tile_list_tiert_xhl_gate_kernel(
         )
         id_w = keep.tile([P, K_PASS], U32, name="id_w", align_bytes=64)
         id_s = keep.tile([P, K_PASS], U8, name="id_s", align_bytes=64)
-        ident = [keep.tile([P, 2, 2 * P], I32, name=f"ident{h}", tag=f"ident{h}", align_bytes=64) for h in range(2)]
+        ident = [
+            keep.tile([P, 2, 2 * P], I32, name="ident0", tag="ident0", align_bytes=64),
+            keep.tile([P, 2, 2 * P], I32, name="ident1", tag="ident1", align_bytes=64),
+        ]
         for t in range(PACK):
             one = float(BF16_ONE << (16 * (t % 2)))
             nc.vector.tensor_scalar(ident[t // 2][:, t % 2, :], ramp[:], float(t // 2), one, ALU.is_equal, ALU.mult)
@@ -94,30 +94,18 @@ def tile_list_tiert_xhl_gate_kernel(
                 stop=True,
             )
 
-        x_raw = []
+        def load_rows(name, source, first, width):
+            raw = keep.tile([P, PACK, width], F32, name=name, tag=name, align_bytes=64)
+            nc.sync.dma_start(raw[:], source[:, first : first + width].rearrange("(p t) j -> p t j", t=PACK))
+            return raw
 
-        def load_x(c):
-            a, first, width = X_CHUNKS[c]
-            raw = keep.tile([P, PACK, width], F32, name=f"x_raw{c}", tag=f"x_raw{c}", align_bytes=64)
-            rows = x[a * K_PASS : (a + 1) * K_PASS, first : first + width]
-            nc.sync.dma_start(raw[:], rows.rearrange("(p t) j -> p t j", t=PACK))
-            x_raw.append(raw)
-
-        load_x(0)
         offsets = keep.tile([P, J // LIST_ROWS], U16, name="offsets")
         nc.sync.dma_start(offsets[:], offs)
         nc.sync.dma_start(tab_s[P - SCALE_ROWS :, :].bitcast(I32), tab_scales[0].bitcast(I32))
-        for c in range(1, len(X_CHUNKS)):
-            load_x(c)
-        tab_w = keep.tile([P, T], I32, name="tab_w", tag="tab_w", align_bytes=64)
-        nc.sync.dma_start(tab_w[:], tab_words[0].rearrange("p t i -> p (t i)").bitcast(I32))
-
-        def load_wt(name, first, width):
-            raw = keep.tile([P, PACK, width], F32, name=name)
-            nc.sync.dma_start(raw[:], wt[:, first : first + width].rearrange("(p t) n -> p t n", t=PACK))
-            return raw
-
-        wt_most = load_wt("wt_most", 0, LAST_TILE)
+        x_left = load_rows("x_left", x[:K_PASS, :], 0, J_HALF)
+        x_right = load_rows("x_right", x[:K_PASS, :], J_HALF, J_HALF)
+        x_last = load_rows("x_last", x[K_PASS:, :], 0, J)
+        wt_pool = load_rows("wt_pool", wt, 0, POOL_COLS)
         for q in range(QUADRANTS):
             nc.sync.dma_start(
                 wx_s[32 * q : 32 * q + 4, :, :].bitcast(I32),
@@ -125,19 +113,14 @@ def tile_list_tiert_xhl_gate_kernel(
             )
         wx_w = keep.tile([P, X_PASSES, 2 * N], U8, name="wx_w", align_bytes=64)
         nc.sync.dma_start(wx_w[:].bitcast(I32), wx_words.rearrange("a p b -> p a b").bitcast(I32))
-        wt_last = load_wt("wt_last", LAST_TILE, P)
-        gates = []
-
-        def load_gate(nt):
-            g = keep.tile([P, T], F32, name=f"gate{nt}")
-            nc.sync.dma_start(g[:], gT[nt * P : (nt + 1) * P, :])
-            gates.append(g)
+        tab_w = keep.tile([P, T], I32, name="tab_w", align_bytes=64)
+        nc.sync.dma_start(tab_w[:], tab_words[0].rearrange("p t i -> p (t i)").bitcast(I32))
+        wt_rest = load_rows("wt_rest", wt, POOL_COLS, N - POOL_COLS)
 
         xq_w = [keep.tile([P, J], U32, name=f"xq_w{a}", align_bytes=64) for a in range(X_PASSES)]
         xq_s = [keep.tile([P, J], U8, name=f"xq_s{a}", align_bytes=64) for a in range(X_PASSES)]
         xr_w = [keep.tile([P, J], U32, name=f"xr_w{a}", align_bytes=64) for a in range(X_PASSES)]
         xr_s = [keep.tile([P, J], U8, name=f"xr_s{a}", align_bytes=64) for a in range(X_PASSES)]
-        rest = []
         back = {}
 
         def quantize(words, scales, first, values):
@@ -146,12 +129,10 @@ def tile_list_tiert_xhl_gate_kernel(
                 out=words[:, cols].bitcast(FP8X4), scales=scales[:, cols], in_=values.rearrange("p j t -> p (j t)")
             )
 
-        def first_tier(c, x_bf, skip=0):
-            a = X_CHUNKS[c][0]
-            first, width = X_CHUNKS[c][1] + skip, x_bf.shape[1]
-            nc.scalar.copy(paired_words(x_bf), paired_rows(x_raw[c][:, :, skip : skip + width]))
+        def first_tier(a, first, rows, x_bf):
+            nc.scalar.copy(paired_words(x_bf), paired_rows(rows))
             quantize(xq_w[a], xq_s[a], first, x_bf)
-            for j0 in range(first, first + width, P):
+            for j0 in range(first, first + x_bf.shape[1], P):
                 back[a, j0] = back_psum.tile([P, PACK, P], F32, name="back")
                 for t in range(PACK):
                     nc.tensor.matmul_mx(
@@ -164,110 +145,104 @@ def tile_list_tiert_xhl_gate_kernel(
                         stop=True,
                     )
 
-        def left_over(c):
-            a, first, width = X_CHUNKS[c]
-            for j0 in range(first, first + width, P):
-                nc.vector.tensor_tensor(
-                    paired_words(rest[a][:, j0 : j0 + P, :]),
-                    paired_rows(x_raw[c][:, :, j0 - first : j0 - first + P]),
-                    paired_rows(back[a, j0][:]),
-                    ALU.subtract,
-                )
-
-        def second_tier(a, first, width):
-            quantize(xr_w[a], xr_s[a], first, rest[a][:, first : first + width, :])
+        def left_over(a, j0, rows, rest):
+            nc.vector.tensor_tensor(
+                paired_words(rest), paired_rows(rows), paired_rows(back[a, j0][:]), ALU.subtract
+            )
 
         def woven(name, width, tag):
             return keep.tile([P, width, PACK], BF16, name=name, tag=tag, align_bytes=64)
 
         v_rows = keep.tile([P, J], U8, name="v_rows", tag="ident1", align_bytes=64)
         nc.vector.tensor_copy(v_rows[:], tab_s[:].indirect(offsets[:]))
-        x_bf_first = woven("x_bf_first", J, "ramp")
-        first_tier(0, x_bf_first[:, :P, :])
-        first_tier(1, x_bf_first[:, P:J_HALF, :])
         for q in range(QUADRANTS):
             gathered = slice(P - SCALE_ROWS + 4 * q, P - SCALE_ROWS + 4 * q + 4)
             nc.sync.dma_start(v_s[32 * q : 32 * q + 4, :].bitcast(I32), v_rows[gathered, :].bitcast(I32))
+        gates = []
         for nt in range(N_TILES):
-            load_gate(nt)
-        rest.append(woven("rest0", J, "rest0"))
-        left_over(0)
-        left_over(1)
-        for j0 in range(0, J_HALF, P):
-            first_tier(2, x_bf_first[:, J_HALF + j0 : J_HALF + j0 + P, :], j0)
-        second_tier(0, 0, J_HALF)
-        left_over(2)
-        second_tier(0, J_HALF, J_HALF)
-        v_w = keep.tile([P, J], U32, name="v_w", tag="x_raw2", align_bytes=64)
-        nc.vector.tensor_copy(v_w[:], tab_w[:].bitcast(U32).indirect(offsets[:]))
-        x_bf_last = woven("x_bf_last", J, "x_raw0")
-        first_tier(3, x_bf_last[:, :J_HALF, :])
-        first_tier(3, x_bf_last[:, J_HALF:, :], J_HALF)
-        hi_rows = keep.tile([P, PACK, POOL_COLS], I32, name="hi_rows", tag="tab_w", align_bytes=64)
-        wt_pool = wt_most[:, :, :POOL_COLS]
-        nc.vector.tensor_scalar(hi_rows[:], wt_pool.bitcast(I32), HI_MASK, None, ALU.bitwise_and)
+            g = keep.tile([P, T], F32, name=f"gate{nt}")
+            nc.sync.dma_start(g[:], gT[nt * P : (nt + 1) * P, :])
+            gates.append(g)
 
-        late = woven("late", J + POOL_COLS, "x_raw0")
-        rest.append(late[:, :J, :])
-        lo_rows = late[:, J:, :].rearrange("p n t -> p (n t)").rearrange("p (t n) -> p t n", t=PACK)
-        nc.gpsimd.tensor_tensor(lo_rows, wt_pool, hi_rows[:].bitcast(F32), ALU.subtract)
-        left_over(3)
+        x_bf_first = woven("x_bf_first", J, "ramp")
+        rest_left = woven("rest_left", J_HALF, "rest_left")
+        rest_right = woven("rest_right", J_HALF, "rest_right")
+
+        def first_rows(j0):
+            half = x_left if j0 < J_HALF else x_right
+            return half[:, :, j0 % J_HALF : j0 % J_HALF + P]
+
+        def first_rest(j0):
+            half = rest_left if j0 < J_HALF else rest_right
+            return half[:, j0 % J_HALF : j0 % J_HALF + P, :]
+
+        first_tier(0, 0, first_rows(0), x_bf_first[:, :P, :])
+        for j0 in range(0, J - P, P):
+            first_tier(0, j0 + P, first_rows(j0 + P), x_bf_first[:, j0 + P : j0 + 2 * P, :])
+            left_over(0, j0, first_rows(j0), first_rest(j0))
+        quantize(xr_w[0], xr_s[0], 0, rest_left[:])
+        left_over(0, J - P, first_rows(J - P), first_rest(J - P))
+
+        x_bf_left = woven("x_bf_left", J_HALF, "x_left")
+        x_bf_third = woven("x_bf_third", P, "ramp")
+        x_bf_fourth = woven("x_bf_fourth", P, "rest_left")
+        first_tier(1, 0, x_last[:, :, :J_HALF], x_bf_left[:])
+        quantize(xr_w[0], xr_s[0], J_HALF, rest_right[:])
+        hi_rows = keep.tile([P, PACK, POOL_COLS], I32, name="hi_rows", tag="x_right", align_bytes=64)
+        nc.vector.tensor_scalar(hi_rows[:], wt_pool[:].bitcast(I32), HI_MASK, None, ALU.bitwise_and)
+        first_tier(1, J_HALF, x_last[:, :, J_HALF : J - P], x_bf_third[:])
+        first_tier(1, J - P, x_last[:, :, J - P :], x_bf_fourth[:])
+
+        rest_last = woven("rest_last", J, "x_left")
+        late = woven("late", N, "rest_left")
+        lo_rows = late[:, :POOL_COLS, :].rearrange("p n t -> p (n t)").rearrange("p (t n) -> p t n", t=PACK)
+        upper = late[:, POOL_COLS:, :]
+        nc.gpsimd.tensor_tensor(lo_rows, wt_pool[:], hi_rows[:].bitcast(F32), ALU.subtract)
+        for j0 in range(0, J, P):
+            left_over(1, j0, x_last[:, :, j0 : j0 + P], rest_last[:, j0 : j0 + P, :])
+        v_w = keep.tile([P, J], U32, name="v_w", tag="ramp", align_bytes=64)
+        nc.vector.tensor_copy(v_w[:], tab_w[:].bitcast(U32).indirect(offsets[:]))
 
         hi = woven("hi", N, "hi")
         lo = woven("lo", N, "lo")
         nc.scalar.copy(paired_words(hi[:, :POOL_COLS, :]), paired_rows(hi_rows[:].bitcast(F32)))
+        halves = wt_rest[:].bitcast(BF16).rearrange("p t (n e) -> p t n e", e=2)
+        nc.scalar.copy(paired_words(upper), paired_rows(halves[:, :, :, 1]))
+        for first in range(0, POOL_COLS, P):
+            nc.scalar.copy(paired_words(lo[:, first : first + P, :]), paired_rows(lo_rows[:, :, first : first + P]))
 
-        def upper_halves(name, rows, tag):
-            upper = woven(name, rows.shape[2], tag)
-            halves = rows.bitcast(BF16).rearrange("p t (n e) -> p t n e", e=2)
-            nc.scalar.copy(paired_words(upper[:]), paired_rows(halves[:, :, :, 1]))
-            return upper
-
-        def weave_lo(first, last):
-            nc.scalar.copy(paired_words(lo[:, first:last, :]), paired_rows(lo_rows[:, :, first:last]))
-
-        upper_mid = upper_halves("upper_mid", wt_most[:, :, POOL_COLS:], "ramp")
-        weave_lo(0, P)
-        upper_last = upper_halves("upper_last", wt_last[:], "tab_w")
-        weave_lo(P, POOL_COLS)
-
-        hi_w = keep.tile([P, N], U32, name="hi_w", tag="x_raw3", align_bytes=64)
+        hi_w = keep.tile([P, N], U32, name="hi_w", tag="x_last", align_bytes=64)
         hi_s = keep.tile([P, N], U8, name="hi_s", align_bytes=64)
         lo_w = keep.tile([P, N], U32, name="lo_w", align_bytes=64)
         lo_s = keep.tile([P, N], U8, name="lo_s", align_bytes=64)
 
-        def split_hi(first, upper):
-            nc.vector.tensor_scalar(
-                hi[:, first : first + upper.shape[1], :].rearrange("p n t -> p (n t)").bitcast(I32),
-                upper[:].rearrange("p n t -> p (n t)").bitcast(I32),
-                HI_MASK_PAIR,
-                None,
-                ALU.bitwise_and,
-            )
-
-        def split_lo(first, rows):
-            cols = slice(first, first + rows.shape[2])
-            nc.vector.tensor_tensor(
-                paired_words(lo[:, cols, :]), paired_rows(rows), paired_words(hi[:, cols, :]), ALU.subtract
-            )
-
-        second_tier(1, 0, J_HALF)
-        split_hi(POOL_COLS, upper_mid)
-        second_tier(1, J_HALF, J_HALF)
-        quantize(hi_w, hi_s, 0, hi[:, :N_HALF, :])
+        quantize(xr_w[1], xr_s[1], 0, rest_last[:, :J_HALF, :])
+        quantize(hi_w, hi_s, 0, hi[:, :POOL_COLS, :])
+        quantize(xr_w[1], xr_s[1], J_HALF, rest_last[:, J_HALF:, :])
         quantize(lo_w, lo_s, 0, lo[:, :P, :])
-        split_lo(POOL_COLS, wt_most[:, :, POOL_COLS:N_HALF])
-        split_hi(LAST_TILE, upper_last)
-        split_lo(N_HALF, wt_most[:, :, N_HALF:])
-        quantize(lo_w, lo_s, P, lo[:, P:N_HALF, :])
-        split_lo(LAST_TILE, wt_last[:])
-        quantize(hi_w, hi_s, N_HALF, hi[:, N_HALF:, :])
-        quantize(lo_w, lo_s, N_HALF, lo[:, N_HALF:, :])
+        nc.vector.tensor_scalar(
+            hi[:, POOL_COLS:, :].rearrange("p n t -> p (n t)").bitcast(I32),
+            upper.rearrange("p n t -> p (n t)").bitcast(I32),
+            HI_MASK_PAIR,
+            None,
+            ALU.bitwise_and,
+        )
+        quantize(lo_w, lo_s, P, lo[:, P:POOL_COLS, :])
+        for first in range(POOL_COLS, N, P):
+            cols = slice(first, first + P)
+            nc.vector.tensor_tensor(
+                paired_words(lo[:, cols, :]),
+                paired_rows(wt_rest[:, :, first - POOL_COLS : first - POOL_COLS + P]),
+                paired_words(hi[:, cols, :]),
+                ALU.subtract,
+            )
+        quantize(hi_w, hi_s, POOL_COLS, hi[:, POOL_COLS:, :])
+        quantize(lo_w, lo_s, POOL_COLS, lo[:, POOL_COLS:, :])
 
         y = [y_psum.tile([P, J], F32, name=f"y{nt}", tag=f"y{nt}") for nt in range(N_TILES)]
         x_operands = ((1, xq_w, xq_s), (0, xq_w, xq_s), (0, xr_w, xr_s), (1, xr_w, xr_s))
 
-        def wx_pass(i, nt, start=False):
+        def wx_pass(i, nt):
             a, words, scales = x_operands[i]
             nc.tensor.matmul_mx(
                 out=y[nt][:],
@@ -275,20 +250,17 @@ def tile_list_tiert_xhl_gate_kernel(
                 lhsT_scale=wx_s[:, a, P * nt : P * (nt + 1)],
                 rhs=words[a][:].bitcast(FP8X4),
                 rhs_scale=scales[a][:],
-                start=start,
+                start=(i == 0),
                 stop=False,
             )
 
-        for i in range(len(x_operands) - 1):
-            for nt in range(N_TILES - 1):
-                wx_pass(i, nt, start=(i == 0))
+        for nt in range(N_TILES):
+            for i in range(len(x_operands) - 1):
+                wx_pass(i, nt)
 
         sums = {}
         for nt in range(N_TILES):
-            wx_pass(len(x_operands) - 1, nt, start=(nt == N_TILES - 1))
-            if nt == N_TILES - 1:
-                for i in range(len(x_operands) - 1):
-                    wx_pass(i, nt)
+            wx_pass(len(x_operands) - 1, nt)
             for words, scales in ((hi_w, hi_s), (lo_w, lo_s)):
                 nc.tensor.matmul_mx(
                     out=y[nt][:],

@@ -99,10 +99,11 @@ def tile_list_tiert_xhl_gate_kernel(
             nc.sync.dma_start(raw[:], source[:, first : first + width].rearrange("(p t) j -> p t j", t=PACK))
             return raw
 
+        x_first = load_rows("x_first", x[:K_PASS, :], 0, P)
         offsets = keep.tile([P, J // LIST_ROWS], U16, name="offsets")
         nc.sync.dma_start(offsets[:], offs)
         nc.sync.dma_start(tab_s[P - SCALE_ROWS :, :].bitcast(I32), tab_scales[0].bitcast(I32))
-        x_left = load_rows("x_left", x[:K_PASS, :], 0, J_HALF)
+        x_second = load_rows("x_second", x[:K_PASS, :], P, P)
         x_right = load_rows("x_right", x[:K_PASS, :], J_HALF, J_HALF)
         x_last = load_rows("x_last", x[K_PASS:, :], 0, J)
         wt_pool = load_rows("wt_pool", wt, 0, POOL_COLS)
@@ -169,8 +170,9 @@ def tile_list_tiert_xhl_gate_kernel(
         rest_right = woven("rest_right", J_HALF, "rest_right")
 
         def first_rows(j0):
-            half = x_left if j0 < J_HALF else x_right
-            return half[:, :, j0 % J_HALF : j0 % J_HALF + P]
+            if j0 < J_HALF:
+                return (x_first, x_second)[j0 // P][:]
+            return x_right[:, :, j0 - J_HALF : j0 - J_HALF + P]
 
         def first_rest(j0):
             half = rest_left if j0 < J_HALF else rest_right
@@ -183,7 +185,7 @@ def tile_list_tiert_xhl_gate_kernel(
         quantize(xr_w[0], xr_s[0], 0, rest_left[:])
         left_over(0, J - P, first_rows(J - P), first_rest(J - P))
 
-        x_bf_left = woven("x_bf_left", J_HALF, "x_left")
+        x_bf_left = woven("x_bf_left", J_HALF, "x_second")
         x_bf_third = woven("x_bf_third", P, "ramp")
         x_bf_fourth = woven("x_bf_fourth", P, "rest_left")
         first_tier(1, 0, x_last[:, :, :J_HALF], x_bf_left[:])
@@ -193,7 +195,7 @@ def tile_list_tiert_xhl_gate_kernel(
         first_tier(1, J_HALF, x_last[:, :, J_HALF : J - P], x_bf_third[:])
         first_tier(1, J - P, x_last[:, :, J - P :], x_bf_fourth[:])
 
-        rest_last = woven("rest_last", J, "x_left")
+        rest_last = woven("rest_last", J, "x_second")
         late = woven("late", N, "rest_left")
         lo_rows = late[:, :POOL_COLS, :].rearrange("p n t -> p (n t)").rearrange("p (t n) -> p t n", t=PACK)
         upper = late[:, POOL_COLS:, :]

@@ -27,7 +27,7 @@ LIST_ROWS = 16
 
 FLOPS = 2 * J * (2 * K * N + 2 * L * N + L * K_PASS)
 
-POOL_COLS = N_HALF
+POOL_COLS = 320
 WARM_PASSES = 4
 
 HI_MASK = -1048576
@@ -189,17 +189,20 @@ def tile_list_tiert_xhl_gate_kernel(
         x_bf_third = woven("x_bf_third", P, "ramp")
         x_bf_fourth = woven("x_bf_fourth", P, "rest_left")
         first_tier(1, 0, x_last[:, :, :J_HALF], x_bf_left[:])
-        quantize(xr_w[0], xr_s[0], J_HALF, rest_right[:])
         hi_rows = keep.tile([P, PACK, POOL_COLS], I32, name="hi_rows", tag="x_right", align_bytes=64)
         nc.vector.tensor_scalar(hi_rows[:], wt_pool[:].bitcast(I32), HI_MASK, None, ALU.bitwise_and)
         first_tier(1, J_HALF, x_last[:, :, J_HALF : J - P], x_bf_third[:])
         first_tier(1, J - P, x_last[:, :, J - P :], x_bf_fourth[:])
+        quantize(xr_w[0], xr_s[0], J_HALF, rest_right[:])
 
         rest_last = woven("rest_last", J, "x_second")
         late = woven("late", N, "rest_left")
-        lo_rows = late[:, :POOL_COLS, :].rearrange("p n t -> p (n t)").rearrange("p (t n) -> p t n", t=PACK)
         upper = late[:, POOL_COLS:, :]
-        nc.gpsimd.tensor_tensor(lo_rows, wt_pool[:], hi_rows[:].bitcast(F32), ALU.subtract)
+        lo_rows = []
+        for cols in (slice(0, P), slice(P, POOL_COLS)):
+            rows = late[:, cols, :].rearrange("p n t -> p (n t)").rearrange("p (t n) -> p t n", t=PACK)
+            nc.gpsimd.tensor_tensor(rows, wt_pool[:, :, cols], hi_rows[:, :, cols].bitcast(F32), ALU.subtract)
+            lo_rows.append(rows)
         for j0 in range(0, J, P):
             left_over(1, j0, x_last[:, :, j0 : j0 + P], rest_last[:, j0 : j0 + P, :])
         v_w = keep.tile([P, J], U32, name="v_w", tag="ramp", align_bytes=64)
@@ -210,17 +213,16 @@ def tile_list_tiert_xhl_gate_kernel(
         nc.scalar.copy(paired_words(hi[:, :POOL_COLS, :]), paired_rows(hi_rows[:].bitcast(F32)))
         halves = wt_rest[:].bitcast(BF16).rearrange("p t (n e) -> p t n e", e=2)
         nc.scalar.copy(paired_words(upper), paired_rows(halves[:, :, :, 1]))
-        for first in range(0, POOL_COLS, P):
-            nc.scalar.copy(paired_words(lo[:, first : first + P, :]), paired_rows(lo_rows[:, :, first : first + P]))
+        nc.scalar.copy(paired_words(lo[:, :P, :]), paired_rows(lo_rows[0]))
+        nc.scalar.copy(paired_words(lo[:, P:POOL_COLS, :]), paired_rows(lo_rows[1]))
 
         hi_w = keep.tile([P, N], U32, name="hi_w", tag="x_last", align_bytes=64)
         hi_s = keep.tile([P, N], U8, name="hi_s", align_bytes=64)
         lo_w = keep.tile([P, N], U32, name="lo_w", align_bytes=64)
         lo_s = keep.tile([P, N], U8, name="lo_s", align_bytes=64)
 
+        quantize(hi_w, hi_s, 0, hi[:, :N_HALF, :])
         quantize(xr_w[1], xr_s[1], 0, rest_last[:, :J_HALF, :])
-        quantize(hi_w, hi_s, 0, hi[:, :POOL_COLS, :])
-        quantize(xr_w[1], xr_s[1], J_HALF, rest_last[:, J_HALF:, :])
         quantize(lo_w, lo_s, 0, lo[:, :P, :])
         nc.vector.tensor_scalar(
             hi[:, POOL_COLS:, :].rearrange("p n t -> p (n t)").bitcast(I32),
@@ -229,22 +231,18 @@ def tile_list_tiert_xhl_gate_kernel(
             None,
             ALU.bitwise_and,
         )
-        quantize(lo_w, lo_s, P, lo[:, P:POOL_COLS, :])
-        for first in range(POOL_COLS, N, P):
-            cols = slice(first, first + P)
-            nc.vector.tensor_tensor(
-                paired_words(lo[:, cols, :]),
-                paired_rows(wt_rest[:, :, first - POOL_COLS : first - POOL_COLS + P]),
-                paired_words(hi[:, cols, :]),
-                ALU.subtract,
-            )
-        quantize(hi_w, hi_s, POOL_COLS, hi[:, POOL_COLS:, :])
-        quantize(lo_w, lo_s, POOL_COLS, lo[:, POOL_COLS:, :])
+        quantize(xr_w[1], xr_s[1], J_HALF, rest_last[:, J_HALF:, :])
+        nc.vector.tensor_tensor(
+            paired_words(lo[:, POOL_COLS:, :]), paired_rows(wt_rest[:]), paired_words(hi[:, POOL_COLS:, :]), ALU.subtract
+        )
+        quantize(lo_w, lo_s, P, lo[:, P:N_HALF, :])
+        quantize(hi_w, hi_s, N_HALF, hi[:, N_HALF:, :])
+        quantize(lo_w, lo_s, N_HALF, lo[:, N_HALF:, :])
 
         y = [y_psum.tile([P, J], F32, name=f"y{nt}", tag=f"y{nt}") for nt in range(N_TILES)]
         x_operands = ((1, xq_w, xq_s), (0, xq_w, xq_s), (0, xr_w, xr_s), (1, xr_w, xr_s))
 
-        def wx_pass(i, nt):
+        def wx_pass(i, nt, stop=False):
             a, words, scales = x_operands[i]
             nc.tensor.matmul_mx(
                 out=y[nt][:],
@@ -253,7 +251,7 @@ def tile_list_tiert_xhl_gate_kernel(
                 rhs=words[a][:].bitcast(FP8X4),
                 rhs_scale=scales[a][:],
                 start=(i == 0),
-                stop=False,
+                stop=stop,
             )
 
         for nt in range(N_TILES):
@@ -262,7 +260,8 @@ def tile_list_tiert_xhl_gate_kernel(
 
         sums = {}
         for nt in range(N_TILES):
-            wx_pass(len(x_operands) - 1, nt)
+            if nt > 0:
+                wx_pass(len(x_operands) - 1, nt)
             for words, scales in ((hi_w, hi_s), (lo_w, lo_s)):
                 nc.tensor.matmul_mx(
                     out=y[nt][:],
@@ -271,8 +270,10 @@ def tile_list_tiert_xhl_gate_kernel(
                     rhs=v_w[:].bitcast(FP8X4),
                     rhs_scale=v_s[:],
                     start=False,
-                    stop=(words is lo_w),
+                    stop=(words is lo_w and nt > 0),
                 )
+            if nt == 0:
+                wx_pass(len(x_operands) - 1, nt, stop=True)
             sums[nt] = keep.tile([P, J], F32, name=f"sums{nt}")
             nc.scalar.copy(sums[nt][:], y[nt][:])
 

@@ -27,7 +27,7 @@ LIST_ROWS = 16
 
 FLOPS = 2 * J * (2 * K * N + 2 * L * N + L * K_PASS)
 
-POOL_COLS = 320
+POOL_COLS = 288
 WARM_PASSES = 4
 
 HI_MASK = -1048576
@@ -49,6 +49,7 @@ def tile_list_tiert_xhl_gate_kernel(
     nc = tc.nc
     with ExitStack() as ctx:
         keep = ctx.enter_context(tc.tile_pool(name="keep", bufs=1))
+        relay = ctx.enter_context(tc.tile_pool(name="relay", bufs=1))
         y_psum = ctx.enter_context(tc.psum_pool(name="y_psum", bufs=1))
         back_psum = ctx.enter_context(tc.psum_pool(name="back_psum", bufs=4))
 
@@ -59,7 +60,7 @@ def tile_list_tiert_xhl_gate_kernel(
         wx_s = keep.tile([P, X_PASSES, N], U8, name="wx_s", align_bytes=64)
         nc.vector.memset(wx_s[:].rearrange("p a n -> p (a n)").bitcast(I32), 0)
 
-        ramp = keep.tile([P, 2 * P], BF16, name="ramp", tag="ramp", align_bytes=64)
+        ramp = relay.tile([P, 2 * P], BF16, name="ramp", offset=768, align_bytes=64)
         nc.gpsimd.iota(
             ramp[:], pattern=[[1, 2 * P]], base=0, channel_multiplier=-2, allow_small_or_imprecise_dtypes=True
         )
@@ -130,8 +131,11 @@ def tile_list_tiert_xhl_gate_kernel(
                 out=words[:, cols].bitcast(FP8X4), scales=scales[:, cols], in_=values.rearrange("p j t -> p (j t)")
             )
 
-        def first_tier(a, first, rows, x_bf):
-            nc.scalar.copy(paired_words(x_bf), paired_rows(rows))
+        def first_tier(a, first, rows, x_bf, on_pool=False):
+            if on_pool:
+                nc.gpsimd.tensor_scalar(x_bf, rows.rearrange("p t j -> p j t"), 1.0, 0.0, ALU.mult, ALU.add)
+            else:
+                nc.scalar.copy(paired_words(x_bf), paired_rows(rows))
             quantize(xq_w[a], xq_s[a], first, x_bf)
             for j0 in range(first, first + x_bf.shape[1], P):
                 back[a, j0] = back_psum.tile([P, PACK, P], F32, name="back")
@@ -154,18 +158,15 @@ def tile_list_tiert_xhl_gate_kernel(
         def woven(name, width, tag):
             return keep.tile([P, width, PACK], BF16, name=name, tag=tag, align_bytes=64)
 
-        v_rows = keep.tile([P, J], U8, name="v_rows", tag="ident1", align_bytes=64)
-        nc.vector.tensor_copy(v_rows[:], tab_s[:].indirect(offsets[:]))
-        for q in range(QUADRANTS):
-            gathered = slice(P - SCALE_ROWS + 4 * q, P - SCALE_ROWS + 4 * q + 4)
-            nc.sync.dma_start(v_s[32 * q : 32 * q + 4, :].bitcast(I32), v_rows[gathered, :].bitcast(I32))
-        gates = []
-        for nt in range(N_TILES):
-            g = keep.tile([P, T], F32, name=f"gate{nt}")
-            nc.sync.dma_start(g[:], gT[nt * P : (nt + 1) * P, :])
-            gates.append(g)
+        def gather_scales(h, rows):
+            picks = offsets[:, h * J_HALF // LIST_ROWS : (h + 1) * J_HALF // LIST_ROWS]
+            nc.vector.tensor_copy(rows[:], tab_s[:].indirect(picks))
+            return rows
 
-        x_bf_first = woven("x_bf_first", J, "ramp")
+        v_rows = [gather_scales(0, keep.tile([P, J_HALF], U8, name="v_rows0", tag="ident1", align_bytes=64))]
+
+        x_bf_head = relay.tile([P, P, PACK], BF16, name="x_bf_head", offset=0, align_bytes=64)
+        x_bf_first = relay.tile([P, J - P, PACK], BF16, name="x_bf_first", offset=1024, align_bytes=64)
         rest_left = woven("rest_left", J_HALF, "rest_left")
         rest_right = woven("rest_right", J_HALF, "rest_right")
 
@@ -178,20 +179,36 @@ def tile_list_tiert_xhl_gate_kernel(
             half = rest_left if j0 < J_HALF else rest_right
             return half[:, j0 % J_HALF : j0 % J_HALF + P, :]
 
-        first_tier(0, 0, first_rows(0), x_bf_first[:, :P, :])
-        for j0 in range(0, J - P, P):
-            first_tier(0, j0 + P, first_rows(j0 + P), x_bf_first[:, j0 + P : j0 + 2 * P, :])
+        first_tier(0, 0, first_rows(0), x_bf_head[:])
+        v_rows.append(gather_scales(1, relay.tile([P, J_HALF], U8, name="v_rows1", offset=0, align_bytes=64)))
+        for h in range(2):
+            for q in range(QUADRANTS):
+                gathered = slice(P - SCALE_ROWS + 4 * q, P - SCALE_ROWS + 4 * q + 4)
+                nc.sync.dma_start(
+                    v_s[32 * q : 32 * q + 4, h * J_HALF : (h + 1) * J_HALF].bitcast(I32),
+                    v_rows[h][gathered, :].bitcast(I32),
+                )
+        gates = []
+        for nt in range(N_TILES):
+            g = keep.tile([P, T], F32, name=f"gate{nt}")
+            nc.sync.dma_start(g[:], gT[nt * P : (nt + 1) * P, :])
+            gates.append(g)
+
+        first_tier(0, P, first_rows(P), x_bf_first[:, :P, :])
+        for j0 in range(0, J_HALF, P):
             left_over(0, j0, first_rows(j0), first_rest(j0))
+            first_tier(0, j0 + J_HALF, first_rows(j0 + J_HALF), x_bf_first[:, j0 + P : j0 + J_HALF, :])
         quantize(xr_w[0], xr_s[0], 0, rest_left[:])
-        left_over(0, J - P, first_rows(J - P), first_rest(J - P))
+        for j0 in range(J_HALF, J, P):
+            left_over(0, j0, first_rows(j0), first_rest(j0))
 
         x_bf_left = woven("x_bf_left", J_HALF, "x_second")
-        x_bf_third = woven("x_bf_third", P, "ramp")
+        x_bf_third = relay.tile([P, P, PACK], BF16, name="x_bf_third", offset=1024, align_bytes=64)
         x_bf_fourth = woven("x_bf_fourth", P, "rest_left")
         first_tier(1, 0, x_last[:, :, :J_HALF], x_bf_left[:])
+        first_tier(1, J_HALF, x_last[:, :, J_HALF : J - P], x_bf_third[:], on_pool=True)
         hi_rows = keep.tile([P, PACK, POOL_COLS], I32, name="hi_rows", tag="x_right", align_bytes=64)
         nc.vector.tensor_scalar(hi_rows[:], wt_pool[:].bitcast(I32), HI_MASK, None, ALU.bitwise_and)
-        first_tier(1, J_HALF, x_last[:, :, J_HALF : J - P], x_bf_third[:])
         first_tier(1, J - P, x_last[:, :, J - P :], x_bf_fourth[:])
         quantize(xr_w[0], xr_s[0], J_HALF, rest_right[:])
 
@@ -205,7 +222,7 @@ def tile_list_tiert_xhl_gate_kernel(
             lo_rows.append(rows)
         for j0 in range(0, J, P):
             left_over(1, j0, x_last[:, :, j0 : j0 + P], rest_last[:, j0 : j0 + P, :])
-        v_w = keep.tile([P, J], U32, name="v_w", tag="ramp", align_bytes=64)
+        v_w = relay.tile([P, J], U32, name="v_w", offset=1024, align_bytes=64)
         nc.vector.tensor_copy(v_w[:], tab_w[:].bitcast(U32).indirect(offsets[:]))
 
         hi = woven("hi", N, "hi")
@@ -242,7 +259,7 @@ def tile_list_tiert_xhl_gate_kernel(
         y = [y_psum.tile([P, J], F32, name=f"y{nt}", tag=f"y{nt}") for nt in range(N_TILES)]
         x_operands = ((1, xq_w, xq_s), (0, xq_w, xq_s), (0, xr_w, xr_s), (1, xr_w, xr_s))
 
-        def wx_pass(i, nt, stop=False):
+        def wx_pass(i, nt, start=False, stop=False):
             a, words, scales = x_operands[i]
             nc.tensor.matmul_mx(
                 out=y[nt][:],
@@ -250,32 +267,43 @@ def tile_list_tiert_xhl_gate_kernel(
                 lhsT_scale=wx_s[:, a, P * nt : P * (nt + 1)],
                 rhs=words[a][:].bitcast(FP8X4),
                 rhs_scale=scales[a][:],
-                start=(i == 0),
+                start=start,
                 stop=stop,
             )
 
-        for nt in range(N_TILES):
-            for i in range(len(x_operands) - 1):
-                wx_pass(i, nt)
+        def table_pass(words, scales, nt, start=False, stop=False):
+            nc.tensor.matmul_mx(
+                out=y[nt][:],
+                lhsT=words[:, P * nt : P * (nt + 1)].bitcast(FP8X4),
+                lhsT_scale=scales[:, P * nt : P * (nt + 1)],
+                rhs=v_w[:].bitcast(FP8X4),
+                rhs_scale=v_s[:],
+                start=start,
+                stop=stop,
+            )
 
         sums = {}
-        for nt in range(N_TILES):
-            if nt > 0:
-                wx_pass(len(x_operands) - 1, nt)
-            for words, scales in ((hi_w, hi_s), (lo_w, lo_s)):
-                nc.tensor.matmul_mx(
-                    out=y[nt][:],
-                    lhsT=words[:, P * nt : P * (nt + 1)].bitcast(FP8X4),
-                    lhsT_scale=scales[:, P * nt : P * (nt + 1)],
-                    rhs=v_w[:].bitcast(FP8X4),
-                    rhs_scale=v_s[:],
-                    start=False,
-                    stop=(words is lo_w and nt > 0),
-                )
-            if nt == 0:
-                wx_pass(len(x_operands) - 1, nt, stop=True)
+
+        def empty(nt):
             sums[nt] = keep.tile([P, J], F32, name=f"sums{nt}")
             nc.scalar.copy(sums[nt][:], y[nt][:])
+
+        last = len(x_operands) - 1
+        for nt in range(N_TILES - 1):
+            for i in range(last):
+                wx_pass(i, nt, start=(i == 0))
+        table_pass(hi_w, hi_s, 0)
+        table_pass(lo_w, lo_s, 0)
+        wx_pass(last, 0, stop=True)
+        empty(0)
+        for nt in range(1, N_TILES):
+            wx_pass(last, nt, start=(nt == N_TILES - 1))
+            if nt == N_TILES - 1:
+                for i in range(last):
+                    wx_pass(i, nt)
+            table_pass(hi_w, hi_s, nt)
+            table_pass(lo_w, lo_s, nt, stop=True)
+            empty(nt)
 
         def gate_and_store(nt, first, width):
             result = keep.tile([P, width], F32, name=f"result{nt}_{first}")

@@ -27,7 +27,7 @@ LIST_ROWS = 16
 
 FLOPS = 2 * J * (2 * K * N + 2 * L * N + L * K_PASS)
 
-POOL_COLS = 288
+POOL_COLS = N_HALF
 WARM_PASSES = 4
 
 HI_MASK = -1048576
@@ -83,7 +83,7 @@ def tile_list_tiert_xhl_gate_kernel(
                 in_=ident[h][:].rearrange("p t f -> p (t f)").bitcast(BF16),
             )
 
-        warm_sum = y_psum.tile([P, 2 * P], F32, name="warm_sum", tag=f"y{N_TILES - 1}")
+        warm_sum = y_psum.tile([P, 2 * P], F32, name="warm_sum", tag="y0")
         for i in range(WARM_PASSES):
             nc.tensor.matmul_mx(
                 out=warm_sum[:],
@@ -105,7 +105,8 @@ def tile_list_tiert_xhl_gate_kernel(
         nc.sync.dma_start(offsets[:], offs)
         nc.sync.dma_start(tab_s[P - SCALE_ROWS :, :].bitcast(I32), tab_scales[0].bitcast(I32))
         x_second = load_rows("x_second", x[:K_PASS, :], P, P)
-        x_right = load_rows("x_right", x[:K_PASS, :], J_HALF, J_HALF)
+        x_right = relay.tile([P, PACK, J_HALF], F32, name="x_right", offset=8704, align_bytes=64)
+        nc.sync.dma_start(x_right[:], x[:K_PASS, J_HALF:].rearrange("(p t) j -> p t j", t=PACK))
         x_last = load_rows("x_last", x[K_PASS:, :], 0, J)
         wt_pool = load_rows("wt_pool", wt, 0, POOL_COLS)
         for q in range(QUADRANTS):
@@ -167,7 +168,7 @@ def tile_list_tiert_xhl_gate_kernel(
 
         x_bf_head = relay.tile([P, P, PACK], BF16, name="x_bf_head", offset=0, align_bytes=64)
         x_bf_first = relay.tile([P, J - P, PACK], BF16, name="x_bf_first", offset=1024, align_bytes=64)
-        rest_left = woven("rest_left", J_HALF, "rest_left")
+        rest_left = relay.tile([P, J_HALF, PACK], BF16, name="rest_left", offset=4608, align_bytes=64)
         rest_right = woven("rest_right", J_HALF, "rest_right")
 
         def first_rows(j0):
@@ -204,59 +205,64 @@ def tile_list_tiert_xhl_gate_kernel(
 
         x_bf_left = woven("x_bf_left", J_HALF, "x_second")
         x_bf_third = relay.tile([P, P, PACK], BF16, name="x_bf_third", offset=1024, align_bytes=64)
-        x_bf_fourth = woven("x_bf_fourth", P, "rest_left")
+        x_bf_fourth = relay.tile([P, P, PACK], BF16, name="x_bf_fourth", offset=5376, align_bytes=64)
         first_tier(1, 0, x_last[:, :, :J_HALF], x_bf_left[:])
         first_tier(1, J_HALF, x_last[:, :, J_HALF : J - P], x_bf_third[:], on_pool=True)
-        hi_rows = keep.tile([P, PACK, POOL_COLS], I32, name="hi_rows", tag="x_right", align_bytes=64)
+        hi_rows = relay.tile([P, PACK, POOL_COLS], I32, name="hi_rows", offset=8704, align_bytes=64)
         nc.vector.tensor_scalar(hi_rows[:], wt_pool[:].bitcast(I32), HI_MASK, None, ALU.bitwise_and)
         first_tier(1, J - P, x_last[:, :, J - P :], x_bf_fourth[:])
         quantize(xr_w[0], xr_s[0], J_HALF, rest_right[:])
 
         rest_last = woven("rest_last", J, "x_second")
-        late = woven("late", N, "rest_left")
-        upper = late[:, POOL_COLS:, :]
         lo_rows = []
-        for cols in (slice(0, P), slice(P, POOL_COLS)):
-            rows = late[:, cols, :].rearrange("p n t -> p (n t)").rearrange("p (t n) -> p t n", t=PACK)
-            nc.gpsimd.tensor_tensor(rows, wt_pool[:, :, cols], hi_rows[:, :, cols].bitcast(F32), ALU.subtract)
-            lo_rows.append(rows)
+        for cols, offset in ((slice(0, P), 4608), (slice(P, POOL_COLS), 6144)):
+            rows = relay.tile(
+                [P, PACK, cols.stop - cols.start], BF16, name=f"lo_rows{cols.start}", offset=offset, align_bytes=64
+            )
+            nc.gpsimd.tensor_tensor(rows[:], wt_pool[:, :, cols], hi_rows[:, :, cols].bitcast(F32), ALU.subtract)
+            lo_rows.append(rows[:])
         for j0 in range(0, J, P):
             left_over(1, j0, x_last[:, :, j0 : j0 + P], rest_last[:, j0 : j0 + P, :])
         v_w = relay.tile([P, J], U32, name="v_w", offset=1024, align_bytes=64)
         nc.vector.tensor_copy(v_w[:], tab_w[:].bitcast(U32).indirect(offsets[:]))
 
         hi = woven("hi", N, "hi")
-        lo = woven("lo", N, "lo")
+        lo = [woven("lo0", P, "lo0"), relay.tile([P, P, PACK], BF16, name="lo1", offset=5120, align_bytes=64)]
         nc.scalar.copy(paired_words(hi[:, :POOL_COLS, :]), paired_rows(hi_rows[:].bitcast(F32)))
+        nc.scalar.copy(paired_words(lo[0][:]), paired_rows(lo_rows[0]))
+        upper = relay.tile([P, N_HALF, PACK], BF16, name="upper", offset=3072, align_bytes=64)[:]
         halves = wt_rest[:].bitcast(BF16).rearrange("p t (n e) -> p t n e", e=2)
         nc.scalar.copy(paired_words(upper), paired_rows(halves[:, :, :, 1]))
-        nc.scalar.copy(paired_words(lo[:, :P, :]), paired_rows(lo_rows[0]))
-        nc.scalar.copy(paired_words(lo[:, P:POOL_COLS, :]), paired_rows(lo_rows[1]))
+        nc.scalar.copy(paired_words(lo[1][:]), paired_rows(lo_rows[1]))
 
-        hi_w = keep.tile([P, N], U32, name="hi_w", tag="x_last", align_bytes=64)
-        hi_s = keep.tile([P, N], U8, name="hi_s", align_bytes=64)
-        lo_w = keep.tile([P, N], U32, name="lo_w", align_bytes=64)
-        lo_s = keep.tile([P, N], U8, name="lo_s", align_bytes=64)
+        hi_w = [
+            keep.tile([P, N_HALF], U32, name="hi_w0", tag="x_last", align_bytes=64),
+            relay.tile([P, N_HALF], U32, name="hi_w1", offset=5632, align_bytes=64),
+        ]
+        lo_w = [keep.tile([P, N_HALF], U32, name=f"lo_w{h}", align_bytes=64) for h in range(2)]
+        hi_s = [keep.tile([P, N_HALF], U8, name=f"hi_s{h}", align_bytes=64) for h in range(2)]
+        lo_s = [keep.tile([P, N_HALF], U8, name=f"lo_s{h}", align_bytes=64) for h in range(2)]
 
-        quantize(hi_w, hi_s, 0, hi[:, :N_HALF, :])
+        quantize(hi_w[0], hi_s[0], 0, hi[:, :N_HALF, :])
         quantize(xr_w[1], xr_s[1], 0, rest_last[:, :J_HALF, :])
-        quantize(lo_w, lo_s, 0, lo[:, :P, :])
+        quantize(lo_w[0], lo_s[0], 0, lo[0][:])
+        quantize(xr_w[1], xr_s[1], J_HALF, rest_last[:, J_HALF:, :])
         nc.vector.tensor_scalar(
-            hi[:, POOL_COLS:, :].rearrange("p n t -> p (n t)").bitcast(I32),
+            hi[:, N_HALF:, :].rearrange("p n t -> p (n t)").bitcast(I32),
             upper.rearrange("p n t -> p (n t)").bitcast(I32),
             HI_MASK_PAIR,
             None,
             ALU.bitwise_and,
         )
-        quantize(xr_w[1], xr_s[1], J_HALF, rest_last[:, J_HALF:, :])
+        quantize(lo_w[0], lo_s[0], P, lo[1][:])
+        lo_rest = relay.tile([P, N_HALF, PACK], BF16, name="lo_rest", offset=6656, align_bytes=64)
         nc.vector.tensor_tensor(
-            paired_words(lo[:, POOL_COLS:, :]), paired_rows(wt_rest[:]), paired_words(hi[:, POOL_COLS:, :]), ALU.subtract
+            paired_words(lo_rest[:]), paired_rows(wt_rest[:]), paired_words(hi[:, N_HALF:, :]), ALU.subtract
         )
-        quantize(lo_w, lo_s, P, lo[:, P:N_HALF, :])
-        quantize(hi_w, hi_s, N_HALF, hi[:, N_HALF:, :])
-        quantize(lo_w, lo_s, N_HALF, lo[:, N_HALF:, :])
+        quantize(hi_w[1], hi_s[1], 0, hi[:, N_HALF:, :])
+        quantize(lo_w[1], lo_s[1], 0, lo_rest[:])
 
-        y = [y_psum.tile([P, J], F32, name=f"y{nt}", tag=f"y{nt}") for nt in range(N_TILES)]
+        y = [y_psum.tile([P, J], F32, name=f"y{nt}", tag=f"y{nt}") for nt in range(N_TILES - 1)]
         x_operands = ((1, xq_w, xq_s), (0, xq_w, xq_s), (0, xr_w, xr_s), (1, xr_w, xr_s))
 
         def wx_pass(i, nt, start=False, stop=False):
@@ -274,8 +280,8 @@ def tile_list_tiert_xhl_gate_kernel(
         def table_pass(words, scales, nt, start=False, stop=False):
             nc.tensor.matmul_mx(
                 out=y[nt][:],
-                lhsT=words[:, P * nt : P * (nt + 1)].bitcast(FP8X4),
-                lhsT_scale=scales[:, P * nt : P * (nt + 1)],
+                lhsT=words[nt // 2][:, P * (nt % 2) : P * (nt % 2 + 1)].bitcast(FP8X4),
+                lhsT_scale=scales[nt // 2][:, P * (nt % 2) : P * (nt % 2 + 1)],
                 rhs=v_w[:].bitcast(FP8X4),
                 rhs_scale=v_s[:],
                 start=start,
@@ -296,14 +302,20 @@ def tile_list_tiert_xhl_gate_kernel(
         table_pass(lo_w, lo_s, 0)
         wx_pass(last, 0, stop=True)
         empty(0)
-        for nt in range(1, N_TILES):
-            wx_pass(last, nt, start=(nt == N_TILES - 1))
-            if nt == N_TILES - 1:
-                for i in range(last):
-                    wx_pass(i, nt)
-            table_pass(hi_w, hi_s, nt)
-            table_pass(lo_w, lo_s, nt, stop=True)
-            empty(nt)
+        table_pass(lo_w, lo_s, 1)
+        table_pass(hi_w, hi_s, 1)
+        wx_pass(last, 1, stop=True)
+        empty(1)
+        table_pass(hi_w, hi_s, 2)
+        wx_pass(last, 2)
+        table_pass(lo_w, lo_s, 2, stop=True)
+        empty(2)
+        y.append(y_psum.tile([P, J], F32, name="y3", tag="y0"))
+        for i in range(len(x_operands)):
+            wx_pass(i, 3, start=(i == 0))
+        table_pass(hi_w, hi_s, 3)
+        table_pass(lo_w, lo_s, 3, stop=True)
+        empty(3)
 
         def gate_and_store(nt, first, width):
             result = keep.tile([P, width], F32, name=f"result{nt}_{first}")

@@ -105,7 +105,7 @@ def tile_list_tiert_xhl_gate_kernel(
         nc.sync.dma_start(offsets[:], offs)
         nc.sync.dma_start(tab_s[P - SCALE_ROWS :, :].bitcast(I32), tab_scales[0].bitcast(I32))
         x_second = load_rows("x_second", x[:K_PASS, :], P, P)
-        x_right = relay.tile([P, PACK, J_HALF], F32, name="x_right", offset=8704, align_bytes=64)
+        x_right = relay.tile([P, PACK, J_HALF], F32, name="x_right", offset=8192, align_bytes=64)
         nc.sync.dma_start(x_right[:], x[:K_PASS, J_HALF:].rearrange("(p t) j -> p t j", t=PACK))
         x_last = load_rows("x_last", x[K_PASS:, :], 0, J)
         wt_pool = load_rows("wt_pool", wt, 0, POOL_COLS)
@@ -120,7 +120,7 @@ def tile_list_tiert_xhl_gate_kernel(
         nc.sync.dma_start(tab_w[:], tab_words[0].rearrange("p t i -> p (t i)").bitcast(I32))
         wt_rest = load_rows("wt_rest", wt, POOL_COLS, N - POOL_COLS)
 
-        xq_w = [keep.tile([P, J], U32, name=f"xq_w{a}", align_bytes=64) for a in range(X_PASSES)]
+        xq_w = [keep.tile([P, J], U32, name="xq_w0", align_bytes=64)]
         xq_s = [keep.tile([P, J], U8, name=f"xq_s{a}", align_bytes=64) for a in range(X_PASSES)]
         xr_w = [keep.tile([P, J], U32, name=f"xr_w{a}", align_bytes=64) for a in range(X_PASSES)]
         xr_s = [keep.tile([P, J], U8, name=f"xr_s{a}", align_bytes=64) for a in range(X_PASSES)]
@@ -132,11 +132,8 @@ def tile_list_tiert_xhl_gate_kernel(
                 out=words[:, cols].bitcast(FP8X4), scales=scales[:, cols], in_=values.rearrange("p j t -> p (j t)")
             )
 
-        def first_tier(a, first, rows, x_bf, on_pool=False):
-            if on_pool:
-                nc.gpsimd.tensor_scalar(x_bf, rows.rearrange("p t j -> p j t"), 1.0, 0.0, ALU.mult, ALU.add)
-            else:
-                nc.scalar.copy(paired_words(x_bf), paired_rows(rows))
+        def first_tier(a, first, rows, x_bf):
+            nc.scalar.copy(paired_words(x_bf), paired_rows(rows))
             quantize(xq_w[a], xq_s[a], first, x_bf)
             for j0 in range(first, first + x_bf.shape[1], P):
                 back[a, j0] = back_psum.tile([P, PACK, P], F32, name="back")
@@ -167,8 +164,8 @@ def tile_list_tiert_xhl_gate_kernel(
         v_rows = [gather_scales(0, keep.tile([P, J_HALF], U8, name="v_rows0", tag="ident1", align_bytes=64))]
 
         x_bf_head = relay.tile([P, P, PACK], BF16, name="x_bf_head", offset=0, align_bytes=64)
-        x_bf_first = relay.tile([P, J - P, PACK], BF16, name="x_bf_first", offset=1024, align_bytes=64)
-        rest_left = relay.tile([P, J_HALF, PACK], BF16, name="rest_left", offset=4608, align_bytes=64)
+        x_bf_first = relay.tile([P, J, PACK], BF16, name="x_bf_first", offset=1024, align_bytes=64)
+        rest_left = woven("rest_left", J_HALF, "rest_left")
         rest_right = woven("rest_right", J_HALF, "rest_right")
 
         def first_rows(j0):
@@ -199,23 +196,25 @@ def tile_list_tiert_xhl_gate_kernel(
         for j0 in range(0, J_HALF, P):
             left_over(0, j0, first_rows(j0), first_rest(j0))
             first_tier(0, j0 + J_HALF, first_rows(j0 + J_HALF), x_bf_first[:, j0 + P : j0 + J_HALF, :])
+        left_over(0, J_HALF, first_rows(J_HALF), first_rest(J_HALF))
         quantize(xr_w[0], xr_s[0], 0, rest_left[:])
-        for j0 in range(J_HALF, J, P):
-            left_over(0, j0, first_rows(j0), first_rest(j0))
+        left_over(0, J - P, first_rows(J - P), first_rest(J - P))
 
         x_bf_left = woven("x_bf_left", J_HALF, "x_second")
         x_bf_third = relay.tile([P, P, PACK], BF16, name="x_bf_third", offset=1024, align_bytes=64)
-        x_bf_fourth = relay.tile([P, P, PACK], BF16, name="x_bf_fourth", offset=5376, align_bytes=64)
-        first_tier(1, 0, x_last[:, :, :J_HALF], x_bf_left[:])
-        first_tier(1, J_HALF, x_last[:, :, J_HALF : J - P], x_bf_third[:], on_pool=True)
-        hi_rows = relay.tile([P, PACK, POOL_COLS], I32, name="hi_rows", offset=8704, align_bytes=64)
-        nc.vector.tensor_scalar(hi_rows[:], wt_pool[:].bitcast(I32), HI_MASK, None, ALU.bitwise_and)
-        first_tier(1, J - P, x_last[:, :, J - P :], x_bf_fourth[:])
+        x_bf_fourth = relay.tile([P, P, PACK], BF16, name="x_bf_fourth", offset=4864, align_bytes=64)
+        xq_w.append(keep.tile([P, J], U32, name="xq_w1", tag="rest_left", align_bytes=64))
+        first_tier(1, 0, x_last[:, :, :P], x_bf_left[:, :P, :])
         quantize(xr_w[0], xr_s[0], J_HALF, rest_right[:])
+        first_tier(1, P, x_last[:, :, P:J_HALF], x_bf_left[:, P:, :])
+        hi_rows = relay.tile([P, PACK, POOL_COLS], I32, name="hi_rows", offset=8192, align_bytes=64)
+        nc.vector.tensor_scalar(hi_rows[:], wt_pool[:].bitcast(I32), HI_MASK, None, ALU.bitwise_and)
+        first_tier(1, J_HALF, x_last[:, :, J_HALF : J - P], x_bf_third[:])
+        first_tier(1, J - P, x_last[:, :, J - P :], x_bf_fourth[:])
 
         rest_last = woven("rest_last", J, "x_second")
         lo_rows = []
-        for cols, offset in ((slice(0, P), 4608), (slice(P, POOL_COLS), 6144)):
+        for cols, offset in ((slice(0, P), 4096), (slice(P, POOL_COLS), 5632)):
             rows = relay.tile(
                 [P, PACK, cols.stop - cols.start], BF16, name=f"lo_rows{cols.start}", offset=offset, align_bytes=64
             )
@@ -223,21 +222,21 @@ def tile_list_tiert_xhl_gate_kernel(
             lo_rows.append(rows[:])
         for j0 in range(0, J, P):
             left_over(1, j0, x_last[:, :, j0 : j0 + P], rest_last[:, j0 : j0 + P, :])
-        v_w = relay.tile([P, J], U32, name="v_w", offset=1024, align_bytes=64)
+        v_w = relay.tile([P, J], U32, name="v_w", offset=512, align_bytes=64)
         nc.vector.tensor_copy(v_w[:], tab_w[:].bitcast(U32).indirect(offsets[:]))
 
         hi = woven("hi", N, "hi")
-        lo = [woven("lo0", P, "lo0"), relay.tile([P, P, PACK], BF16, name="lo1", offset=5120, align_bytes=64)]
+        lo = [woven("lo0", P, "lo0"), relay.tile([P, P, PACK], BF16, name="lo1", offset=4608, align_bytes=64)]
         nc.scalar.copy(paired_words(hi[:, :POOL_COLS, :]), paired_rows(hi_rows[:].bitcast(F32)))
         nc.scalar.copy(paired_words(lo[0][:]), paired_rows(lo_rows[0]))
-        upper = relay.tile([P, N_HALF, PACK], BF16, name="upper", offset=3072, align_bytes=64)[:]
+        upper = relay.tile([P, N_HALF, PACK], BF16, name="upper", offset=2560, align_bytes=64)[:]
         halves = wt_rest[:].bitcast(BF16).rearrange("p t (n e) -> p t n e", e=2)
         nc.scalar.copy(paired_words(upper), paired_rows(halves[:, :, :, 1]))
         nc.scalar.copy(paired_words(lo[1][:]), paired_rows(lo_rows[1]))
 
         hi_w = [
             keep.tile([P, N_HALF], U32, name="hi_w0", tag="x_last", align_bytes=64),
-            relay.tile([P, N_HALF], U32, name="hi_w1", offset=5632, align_bytes=64),
+            relay.tile([P, N_HALF], U32, name="hi_w1", offset=5120, align_bytes=64),
         ]
         lo_w = [keep.tile([P, N_HALF], U32, name=f"lo_w{h}", align_bytes=64) for h in range(2)]
         hi_s = [keep.tile([P, N_HALF], U8, name=f"hi_s{h}", align_bytes=64) for h in range(2)]
@@ -255,7 +254,7 @@ def tile_list_tiert_xhl_gate_kernel(
             ALU.bitwise_and,
         )
         quantize(lo_w[0], lo_s[0], P, lo[1][:])
-        lo_rest = relay.tile([P, N_HALF, PACK], BF16, name="lo_rest", offset=6656, align_bytes=64)
+        lo_rest = relay.tile([P, N_HALF, PACK], BF16, name="lo_rest", offset=6144, align_bytes=64)
         nc.vector.tensor_tensor(
             paired_words(lo_rest[:]), paired_rows(wt_rest[:]), paired_words(hi[:, N_HALF:, :]), ALU.subtract
         )

@@ -234,17 +234,18 @@ def tile_list_tiert_xhl_gate_kernel(
         nc.scalar.copy(paired_words(upper), paired_rows(halves[:, :, :, 1]))
         nc.scalar.copy(paired_words(lo[1][:]), paired_rows(lo_rows[1]))
 
-        hi_w = [
-            keep.tile([P, N_HALF], U32, name="hi_w0", tag="x_last", align_bytes=64),
-            relay.tile([P, N_HALF], U32, name="hi_w1", offset=5120, align_bytes=64),
-        ]
-        lo_w = [keep.tile([P, N_HALF], U32, name=f"lo_w{h}", align_bytes=64) for h in range(2)]
-        hi_s = [keep.tile([P, N_HALF], U8, name=f"hi_s{h}", align_bytes=64) for h in range(2)]
-        lo_s = [keep.tile([P, N_HALF], U8, name=f"lo_s{h}", align_bytes=64) for h in range(2)]
+        hi_first = keep.tile([P, P], U32, name="hi_first", tag="x_last", align_bytes=64)
+        hi_second = relay.tile([P, P], U32, name="hi_second", offset=5888, align_bytes=64)
+        hi_rest = relay.tile([P, N_HALF], U32, name="hi_rest", offset=4864, align_bytes=64)
+        hi_w = [hi_first[:], hi_second[:], hi_rest[:, :P], hi_rest[:, P:]]
+        hi_s = keep.tile([P, N], U8, name="hi_s", align_bytes=64)
+        lo_all = keep.tile([P, N], U32, name="lo_all", align_bytes=64)
+        lo_w = [lo_all[:, P * nt : P * (nt + 1)] for nt in range(N_TILES)]
+        lo_s = keep.tile([P, N], U8, name="lo_s", align_bytes=64)
 
-        quantize(hi_w[0], hi_s[0], 0, hi[:, :N_HALF, :])
+        quantize(hi_first, hi_s[:, :P], 0, hi[:, :P, :])
         quantize(xr_w[1], xr_s[1], 0, rest_last[:, :J_HALF, :])
-        quantize(lo_w[0], lo_s[0], 0, lo[0][:])
+        quantize(lo_all, lo_s, 0, lo[0][:])
         quantize(xr_w[1], xr_s[1], J_HALF, rest_last[:, J_HALF:, :])
         nc.vector.tensor_scalar(
             hi[:, N_HALF:, :].rearrange("p n t -> p (n t)").bitcast(I32),
@@ -253,13 +254,14 @@ def tile_list_tiert_xhl_gate_kernel(
             None,
             ALU.bitwise_and,
         )
-        quantize(lo_w[0], lo_s[0], P, lo[1][:])
-        lo_rest = relay.tile([P, N_HALF, PACK], BF16, name="lo_rest", offset=6144, align_bytes=64)
+        quantize(lo_all, lo_s, P, lo[1][:])
+        quantize(hi_second, hi_s[:, P:N_HALF], 0, hi[:, P:N_HALF, :])
+        lo_rest = relay.tile([P, N_HALF, PACK], BF16, name="lo_rest", offset=6400, align_bytes=64)
         nc.vector.tensor_tensor(
             paired_words(lo_rest[:]), paired_rows(wt_rest[:]), paired_words(hi[:, N_HALF:, :]), ALU.subtract
         )
-        quantize(hi_w[1], hi_s[1], 0, hi[:, N_HALF:, :])
-        quantize(lo_w[1], lo_s[1], 0, lo_rest[:])
+        quantize(hi_rest, hi_s[:, N_HALF:], 0, hi[:, N_HALF:, :])
+        quantize(lo_all, lo_s, N_HALF, lo_rest[:])
 
         y = [y_psum.tile([P, J], F32, name=f"y{nt}", tag=f"y{nt}") for nt in range(N_TILES - 1)]
         x_operands = ((1, xq_w, xq_s), (0, xq_w, xq_s), (0, xr_w, xr_s), (1, xr_w, xr_s))
@@ -279,8 +281,8 @@ def tile_list_tiert_xhl_gate_kernel(
         def table_pass(words, scales, nt, start=False, stop=False):
             nc.tensor.matmul_mx(
                 out=y[nt][:],
-                lhsT=words[nt // 2][:, P * (nt % 2) : P * (nt % 2 + 1)].bitcast(FP8X4),
-                lhsT_scale=scales[nt // 2][:, P * (nt % 2) : P * (nt % 2 + 1)],
+                lhsT=words[nt].bitcast(FP8X4),
+                lhsT_scale=scales[:, P * nt : P * (nt + 1)],
                 rhs=v_w[:].bitcast(FP8X4),
                 rhs_scale=v_s[:],
                 start=start,
@@ -326,5 +328,6 @@ def tile_list_tiert_xhl_gate_kernel(
 
         for nt in range(N_TILES - 1):
             gate_and_store(nt, 0, J)
-        gate_and_store(N_TILES - 1, 0, J - P)
+        gate_and_store(N_TILES - 1, 0, J_HALF)
+        gate_and_store(N_TILES - 1, J_HALF, P)
         gate_and_store(N_TILES - 1, J - P, P)

@@ -24,15 +24,32 @@ J_HALF = J // 2
 N_HALF = N // 2
 SCALE_ROWS = K_PASS // 32
 LIST_ROWS = 16
+BACK_BANKS = 4
 
 FLOPS = 2 * J * (2 * K * N + 2 * L * N + L * K_PASS)
 
-POOL_COLS = N_HALF
 WARM_PASSES = 4
 
 HI_MASK = -1048576
 HI_MASK_PAIR = -983056
 BF16_ONE = 0x3F80
+
+ALIGN = 64
+PIECE = P * PACK * 2
+AT_V_ROWS = 0
+AT_X_BF_HEAD = PIECE // 4 - ALIGN
+AT_RAMP = AT_X_BF_HEAD + PIECE - ALIGN
+AT_X_BF_FIRST = AT_RAMP + PIECE // 2 - ALIGN
+AT_X_BF_THIRD = AT_X_BF_FIRST
+AT_X_BF_FOURTH = AT_X_BF_FIRST + 3 * PIECE - ALIGN
+AT_V_W = PIECE // 4
+AT_UPPER = AT_V_W + 2 * PIECE
+AT_LO_SECOND = AT_UPPER + 2 * PIECE
+AT_LO_ROWS = (AT_LO_SECOND - PIECE // 2, AT_LO_SECOND + PIECE)
+AT_HI_REST = AT_X_BF_FOURTH
+AT_HI_SECOND = AT_HI_REST + PIECE
+AT_LO_REST = AT_HI_SECOND + PIECE // 2
+AT_X_RIGHT = AT_LO_REST + 2 * PIECE
 
 
 def paired_rows(ap):
@@ -51,25 +68,28 @@ def tile_list_tiert_xhl_gate_kernel(
         keep = ctx.enter_context(tc.tile_pool(name="keep", bufs=1))
         relay = ctx.enter_context(tc.tile_pool(name="relay", bufs=1))
         y_psum = ctx.enter_context(tc.psum_pool(name="y_psum", bufs=1))
-        back_psum = ctx.enter_context(tc.psum_pool(name="back_psum", bufs=4))
+        back_psum = ctx.enter_context(tc.psum_pool(name="back_psum", bufs=BACK_BANKS))
 
-        tab_s = keep.tile([P, T], U8, name="tab_s", align_bytes=64)
+        def woven(name, width, tag):
+            return keep.tile([P, width, PACK], BF16, name=name, tag=tag, align_bytes=ALIGN)
+
+        def relayed(name, shape, dtype, offset):
+            return relay.tile(shape, dtype, name=name, offset=offset, align_bytes=ALIGN)
+
+        tab_s = keep.tile([P, T], U8, name="tab_s", align_bytes=ALIGN)
         nc.vector.memset(tab_s[: P - SCALE_ROWS, :].bitcast(I32), 0)
-        v_s = keep.tile([P, J], U8, name="v_s", align_bytes=64)
+        v_s = keep.tile([P, J], U8, name="v_s", align_bytes=ALIGN)
         nc.vector.memset(v_s[:].bitcast(I32), 0)
-        wx_s = keep.tile([P, X_PASSES, N], U8, name="wx_s", align_bytes=64)
+        wx_s = keep.tile([P, X_PASSES, N], U8, name="wx_s", align_bytes=ALIGN)
         nc.vector.memset(wx_s[:].rearrange("p a n -> p (a n)").bitcast(I32), 0)
 
-        ramp = relay.tile([P, 2 * P], BF16, name="ramp", offset=768, align_bytes=64)
+        ramp = relayed("ramp", [P, 2 * P], BF16, AT_RAMP)
         nc.gpsimd.iota(
             ramp[:], pattern=[[1, 2 * P]], base=0, channel_multiplier=-2, allow_small_or_imprecise_dtypes=True
         )
-        id_w = keep.tile([P, K_PASS], U32, name="id_w", align_bytes=64)
-        id_s = keep.tile([P, K_PASS], U8, name="id_s", align_bytes=64)
-        ident = [
-            keep.tile([P, 2, 2 * P], I32, name="ident0", tag="ident0", align_bytes=64),
-            keep.tile([P, 2, 2 * P], I32, name="ident1", tag="ident1", align_bytes=64),
-        ]
+        id_w = keep.tile([P, K_PASS], U32, name="id_w", align_bytes=ALIGN)
+        id_s = keep.tile([P, K_PASS], U8, name="id_s", align_bytes=ALIGN)
+        ident = [keep.tile([P, 2, 2 * P], I32, name=f"ident{h}", tag=f"ident{h}", align_bytes=ALIGN) for h in range(2)]
         for t in range(PACK):
             one = float(BF16_ONE << (16 * (t % 2)))
             nc.vector.tensor_scalar(ident[t // 2][:, t % 2, :], ramp[:], float(t // 2), one, ALU.is_equal, ALU.mult)
@@ -96,7 +116,7 @@ def tile_list_tiert_xhl_gate_kernel(
             )
 
         def load_rows(name, source, first, width):
-            raw = keep.tile([P, PACK, width], F32, name=name, tag=name, align_bytes=64)
+            raw = keep.tile([P, PACK, width], F32, name=name, tag=name, align_bytes=ALIGN)
             nc.sync.dma_start(raw[:], source[:, first : first + width].rearrange("(p t) j -> p t j", t=PACK))
             return raw
 
@@ -105,25 +125,25 @@ def tile_list_tiert_xhl_gate_kernel(
         nc.sync.dma_start(offsets[:], offs)
         nc.sync.dma_start(tab_s[P - SCALE_ROWS :, :].bitcast(I32), tab_scales[0].bitcast(I32))
         x_second = load_rows("x_second", x[:K_PASS, :], P, P)
-        x_right = relay.tile([P, PACK, J_HALF], F32, name="x_right", offset=8192, align_bytes=64)
+        x_right = relayed("x_right", [P, PACK, J_HALF], F32, AT_X_RIGHT)
         nc.sync.dma_start(x_right[:], x[:K_PASS, J_HALF:].rearrange("(p t) j -> p t j", t=PACK))
         x_last = load_rows("x_last", x[K_PASS:, :], 0, J)
-        wt_pool = load_rows("wt_pool", wt, 0, POOL_COLS)
+        wt_left = load_rows("wt_left", wt, 0, N_HALF)
         for q in range(QUADRANTS):
             nc.sync.dma_start(
                 wx_s[32 * q : 32 * q + 4, :, :].bitcast(I32),
                 wx_scales[:, 4 * q : 4 * q + 4, :].rearrange("a r n -> r a n").bitcast(I32),
             )
-        wx_w = keep.tile([P, X_PASSES, 2 * N], U8, name="wx_w", align_bytes=64)
+        wx_w = keep.tile([P, X_PASSES, 2 * N], U8, name="wx_w", align_bytes=ALIGN)
         nc.sync.dma_start(wx_w[:].bitcast(I32), wx_words.rearrange("a p b -> p a b").bitcast(I32))
-        tab_w = keep.tile([P, T], I32, name="tab_w", align_bytes=64)
+        tab_w = keep.tile([P, T], I32, name="tab_w", align_bytes=ALIGN)
         nc.sync.dma_start(tab_w[:], tab_words[0].rearrange("p t i -> p (t i)").bitcast(I32))
-        wt_rest = load_rows("wt_rest", wt, POOL_COLS, N - POOL_COLS)
+        wt_right = load_rows("wt_right", wt, N_HALF, N_HALF)
 
-        xq_w = [keep.tile([P, J], U32, name="xq_w0", align_bytes=64)]
-        xq_s = [keep.tile([P, J], U8, name=f"xq_s{a}", align_bytes=64) for a in range(X_PASSES)]
-        xr_w = [keep.tile([P, J], U32, name=f"xr_w{a}", align_bytes=64) for a in range(X_PASSES)]
-        xr_s = [keep.tile([P, J], U8, name=f"xr_s{a}", align_bytes=64) for a in range(X_PASSES)]
+        xq_w = [keep.tile([P, J], U32, name="xq_w0", align_bytes=ALIGN)]
+        xq_s = [keep.tile([P, J], U8, name=f"xq_s{a}", align_bytes=ALIGN) for a in range(X_PASSES)]
+        xr_w = [keep.tile([P, J], U32, name=f"xr_w{a}", align_bytes=ALIGN) for a in range(X_PASSES)]
+        xr_s = [keep.tile([P, J], U8, name=f"xr_s{a}", align_bytes=ALIGN) for a in range(X_PASSES)]
         back = {}
 
         def quantize(words, scales, first, values):
@@ -132,39 +152,33 @@ def tile_list_tiert_xhl_gate_kernel(
                 out=words[:, cols].bitcast(FP8X4), scales=scales[:, cols], in_=values.rearrange("p j t -> p (j t)")
             )
 
-        def first_tier(a, first, rows, x_bf):
+        def first_tier(a, j0, rows, x_bf):
             nc.scalar.copy(paired_words(x_bf), paired_rows(rows))
-            quantize(xq_w[a], xq_s[a], first, x_bf)
-            for j0 in range(first, first + x_bf.shape[1], P):
-                back[a, j0] = back_psum.tile([P, PACK, P], F32, name="back")
-                for t in range(PACK):
-                    nc.tensor.matmul_mx(
-                        out=back[a, j0][:, t, :],
-                        lhsT=id_w[:, t * P : (t + 1) * P].bitcast(FP8X4),
-                        lhsT_scale=id_s[:, t * P : (t + 1) * P],
-                        rhs=xq_w[a][:, j0 : j0 + P].bitcast(FP8X4),
-                        rhs_scale=xq_s[a][:, j0 : j0 + P],
-                        start=True,
-                        stop=True,
-                    )
+            quantize(xq_w[a], xq_s[a], j0, x_bf)
+            back[a, j0] = back_psum.tile([P, PACK, P], F32, name="back")
+            for t in range(PACK):
+                nc.tensor.matmul_mx(
+                    out=back[a, j0][:, t, :],
+                    lhsT=id_w[:, t * P : (t + 1) * P].bitcast(FP8X4),
+                    lhsT_scale=id_s[:, t * P : (t + 1) * P],
+                    rhs=xq_w[a][:, j0 : j0 + P].bitcast(FP8X4),
+                    rhs_scale=xq_s[a][:, j0 : j0 + P],
+                    start=True,
+                    stop=True,
+                )
 
         def left_over(a, j0, rows, rest):
-            nc.vector.tensor_tensor(
-                paired_words(rest), paired_rows(rows), paired_rows(back[a, j0][:]), ALU.subtract
-            )
+            nc.vector.tensor_tensor(paired_words(rest), paired_rows(rows), paired_rows(back[a, j0][:]), ALU.subtract)
 
-        def woven(name, width, tag):
-            return keep.tile([P, width, PACK], BF16, name=name, tag=tag, align_bytes=64)
-
-        def gather_scales(h, rows):
+        def gather_scales(h, gathered):
             picks = offsets[:, h * J_HALF // LIST_ROWS : (h + 1) * J_HALF // LIST_ROWS]
-            nc.vector.tensor_copy(rows[:], tab_s[:].indirect(picks))
-            return rows
+            nc.vector.tensor_copy(gathered[:], tab_s[:].indirect(picks))
+            return gathered
 
-        v_rows = [gather_scales(0, keep.tile([P, J_HALF], U8, name="v_rows0", tag="ident1", align_bytes=64))]
+        v_rows = [gather_scales(0, keep.tile([P, J_HALF], U8, name="v_rows0", tag="ident1", align_bytes=ALIGN))]
 
-        x_bf_head = relay.tile([P, P, PACK], BF16, name="x_bf_head", offset=0, align_bytes=64)
-        x_bf_first = relay.tile([P, J, PACK], BF16, name="x_bf_first", offset=1024, align_bytes=64)
+        x_bf_head = relayed("x_bf_head", [P, P, PACK], BF16, AT_X_BF_HEAD)
+        x_bf_first = relayed("x_bf_first", [P, J - P, PACK], BF16, AT_X_BF_FIRST)
         rest_left = woven("rest_left", J_HALF, "rest_left")
         rest_right = woven("rest_right", J_HALF, "rest_right")
 
@@ -178,13 +192,13 @@ def tile_list_tiert_xhl_gate_kernel(
             return half[:, j0 % J_HALF : j0 % J_HALF + P, :]
 
         first_tier(0, 0, first_rows(0), x_bf_head[:])
-        v_rows.append(gather_scales(1, relay.tile([P, J_HALF], U8, name="v_rows1", offset=0, align_bytes=64)))
+        v_rows.append(gather_scales(1, relayed("v_rows1", [P, J_HALF], U8, AT_V_ROWS)))
         for h in range(2):
             for q in range(QUADRANTS):
-                gathered = slice(P - SCALE_ROWS + 4 * q, P - SCALE_ROWS + 4 * q + 4)
+                rows_q = slice(P - SCALE_ROWS + 4 * q, P - SCALE_ROWS + 4 * q + 4)
                 nc.sync.dma_start(
                     v_s[32 * q : 32 * q + 4, h * J_HALF : (h + 1) * J_HALF].bitcast(I32),
-                    v_rows[h][gathered, :].bitcast(I32),
+                    v_rows[h][rows_q, :].bitcast(I32),
                 )
         gates = []
         for nt in range(N_TILES):
@@ -201,70 +215,71 @@ def tile_list_tiert_xhl_gate_kernel(
         left_over(0, J - P, first_rows(J - P), first_rest(J - P))
 
         x_bf_left = woven("x_bf_left", J_HALF, "x_second")
-        x_bf_third = relay.tile([P, P, PACK], BF16, name="x_bf_third", offset=1024, align_bytes=64)
-        x_bf_fourth = relay.tile([P, P, PACK], BF16, name="x_bf_fourth", offset=4864, align_bytes=64)
-        xq_w.append(keep.tile([P, J], U32, name="xq_w1", tag="rest_left", align_bytes=64))
+        x_bf_third = relayed("x_bf_third", [P, P, PACK], BF16, AT_X_BF_THIRD)
+        x_bf_fourth = relayed("x_bf_fourth", [P, P, PACK], BF16, AT_X_BF_FOURTH)
+        xq_w.append(keep.tile([P, J], U32, name="xq_w1", tag="rest_left", align_bytes=ALIGN))
         first_tier(1, 0, x_last[:, :, :P], x_bf_left[:, :P, :])
         quantize(xr_w[0], xr_s[0], J_HALF, rest_right[:])
         first_tier(1, P, x_last[:, :, P:J_HALF], x_bf_left[:, P:, :])
-        hi_rows = relay.tile([P, PACK, POOL_COLS], I32, name="hi_rows", offset=8192, align_bytes=64)
-        nc.vector.tensor_scalar(hi_rows[:], wt_pool[:].bitcast(I32), HI_MASK, None, ALU.bitwise_and)
+        hi_rows = relayed("hi_rows", [P, PACK, N_HALF], I32, AT_X_RIGHT)
+        nc.vector.tensor_scalar(hi_rows[:], wt_left[:].bitcast(I32), HI_MASK, None, ALU.bitwise_and)
         first_tier(1, J_HALF, x_last[:, :, J_HALF : J - P], x_bf_third[:])
         first_tier(1, J - P, x_last[:, :, J - P :], x_bf_fourth[:])
 
         rest_last = woven("rest_last", J, "x_second")
         lo_rows = []
-        for cols, offset in ((slice(0, P), 4096), (slice(P, POOL_COLS), 5632)):
-            rows = relay.tile(
-                [P, PACK, cols.stop - cols.start], BF16, name=f"lo_rows{cols.start}", offset=offset, align_bytes=64
-            )
-            nc.gpsimd.tensor_tensor(rows[:], wt_pool[:, :, cols], hi_rows[:, :, cols].bitcast(F32), ALU.subtract)
-            lo_rows.append(rows[:])
+        for nt in range(2):
+            cols = slice(nt * P, (nt + 1) * P)
+            rows = relayed(f"lo_rows{nt}", [P, PACK, P], BF16, AT_LO_ROWS[nt])
+            nc.gpsimd.tensor_tensor(rows[:], wt_left[:, :, cols], hi_rows[:, :, cols].bitcast(F32), ALU.subtract)
+            lo_rows.append(rows)
         for j0 in range(0, J, P):
             left_over(1, j0, x_last[:, :, j0 : j0 + P], rest_last[:, j0 : j0 + P, :])
-        v_w = relay.tile([P, J], U32, name="v_w", offset=512, align_bytes=64)
+        v_w = relayed("v_w", [P, J], U32, AT_V_W)
         nc.vector.tensor_copy(v_w[:], tab_w[:].bitcast(U32).indirect(offsets[:]))
 
         hi = woven("hi", N, "hi")
-        lo = [woven("lo0", P, "lo0"), relay.tile([P, P, PACK], BF16, name="lo1", offset=4608, align_bytes=64)]
-        nc.scalar.copy(paired_words(hi[:, :POOL_COLS, :]), paired_rows(hi_rows[:].bitcast(F32)))
-        nc.scalar.copy(paired_words(lo[0][:]), paired_rows(lo_rows[0]))
-        upper = relay.tile([P, N_HALF, PACK], BF16, name="upper", offset=2560, align_bytes=64)[:]
-        halves = wt_rest[:].bitcast(BF16).rearrange("p t (n e) -> p t n e", e=2)
-        nc.scalar.copy(paired_words(upper), paired_rows(halves[:, :, :, 1]))
-        nc.scalar.copy(paired_words(lo[1][:]), paired_rows(lo_rows[1]))
+        lo_first = woven("lo_first", P, "lo_first")
+        lo_second = relayed("lo_second", [P, P, PACK], BF16, AT_LO_SECOND)
+        nc.scalar.copy(paired_words(hi[:, :N_HALF, :]), paired_rows(hi_rows[:].bitcast(F32)))
+        nc.scalar.copy(paired_words(lo_first[:]), paired_rows(lo_rows[0][:]))
+        upper = relayed("upper", [P, N_HALF, PACK], BF16, AT_UPPER)
+        halves = wt_right[:].bitcast(BF16).rearrange("p t (n e) -> p t n e", e=2)
+        nc.scalar.copy(paired_words(upper[:]), paired_rows(halves[:, :, :, 1]))
+        nc.scalar.copy(paired_words(lo_second[:]), paired_rows(lo_rows[1][:]))
 
-        hi_first = keep.tile([P, P], U32, name="hi_first", tag="x_last", align_bytes=64)
-        hi_second = relay.tile([P, P], U32, name="hi_second", offset=5888, align_bytes=64)
-        hi_rest = relay.tile([P, N_HALF], U32, name="hi_rest", offset=4864, align_bytes=64)
+        hi_first = keep.tile([P, P], U32, name="hi_first", tag="x_last", align_bytes=ALIGN)
+        hi_second = relayed("hi_second", [P, P], U32, AT_HI_SECOND)
+        hi_rest = relayed("hi_rest", [P, N_HALF], U32, AT_HI_REST)
         hi_w = [hi_first[:], hi_second[:], hi_rest[:, :P], hi_rest[:, P:]]
-        hi_s = keep.tile([P, N], U8, name="hi_s", align_bytes=64)
-        lo_all = keep.tile([P, N], U32, name="lo_all", align_bytes=64)
+        hi_s = keep.tile([P, N], U8, name="hi_s", align_bytes=ALIGN)
+        lo_all = keep.tile([P, N], U32, name="lo_all", align_bytes=ALIGN)
         lo_w = [lo_all[:, P * nt : P * (nt + 1)] for nt in range(N_TILES)]
-        lo_s = keep.tile([P, N], U8, name="lo_s", align_bytes=64)
+        lo_s = keep.tile([P, N], U8, name="lo_s", align_bytes=ALIGN)
 
         quantize(hi_first, hi_s[:, :P], 0, hi[:, :P, :])
         quantize(xr_w[1], xr_s[1], 0, rest_last[:, :J_HALF, :])
-        quantize(lo_all, lo_s, 0, lo[0][:])
+        quantize(lo_all, lo_s, 0, lo_first[:])
         quantize(xr_w[1], xr_s[1], J_HALF, rest_last[:, J_HALF:, :])
         nc.vector.tensor_scalar(
             hi[:, N_HALF:, :].rearrange("p n t -> p (n t)").bitcast(I32),
-            upper.rearrange("p n t -> p (n t)").bitcast(I32),
+            upper[:].rearrange("p n t -> p (n t)").bitcast(I32),
             HI_MASK_PAIR,
             None,
             ALU.bitwise_and,
         )
-        quantize(lo_all, lo_s, P, lo[1][:])
+        quantize(lo_all, lo_s, P, lo_second[:])
         quantize(hi_second, hi_s[:, P:N_HALF], 0, hi[:, P:N_HALF, :])
-        lo_rest = relay.tile([P, N_HALF, PACK], BF16, name="lo_rest", offset=6400, align_bytes=64)
+        lo_rest = relayed("lo_rest", [P, N_HALF, PACK], BF16, AT_LO_REST)
         nc.vector.tensor_tensor(
-            paired_words(lo_rest[:]), paired_rows(wt_rest[:]), paired_words(hi[:, N_HALF:, :]), ALU.subtract
+            paired_words(lo_rest[:]), paired_rows(wt_right[:]), paired_words(hi[:, N_HALF:, :]), ALU.subtract
         )
         quantize(hi_rest, hi_s[:, N_HALF:], 0, hi[:, N_HALF:, :])
         quantize(lo_all, lo_s, N_HALF, lo_rest[:])
 
         y = [y_psum.tile([P, J], F32, name=f"y{nt}", tag=f"y{nt}") for nt in range(N_TILES - 1)]
         x_operands = ((1, xq_w, xq_s), (0, xq_w, xq_s), (0, xr_w, xr_s), (1, xr_w, xr_s))
+        last = len(x_operands) - 1
 
         def wx_pass(i, nt, start=False, stop=False):
             a, words, scales = x_operands[i]
@@ -278,14 +293,14 @@ def tile_list_tiert_xhl_gate_kernel(
                 stop=stop,
             )
 
-        def table_pass(words, scales, nt, start=False, stop=False):
+        def table_pass(words, scales, nt, stop=False):
             nc.tensor.matmul_mx(
                 out=y[nt][:],
                 lhsT=words[nt].bitcast(FP8X4),
                 lhsT_scale=scales[:, P * nt : P * (nt + 1)],
                 rhs=v_w[:].bitcast(FP8X4),
                 rhs_scale=v_s[:],
-                start=start,
+                start=False,
                 stop=stop,
             )
 
@@ -295,7 +310,6 @@ def tile_list_tiert_xhl_gate_kernel(
             sums[nt] = keep.tile([P, J], F32, name=f"sums{nt}")
             nc.scalar.copy(sums[nt][:], y[nt][:])
 
-        last = len(x_operands) - 1
         for nt in range(N_TILES - 1):
             for i in range(last):
                 wx_pass(i, nt, start=(i == 0))
@@ -311,12 +325,13 @@ def tile_list_tiert_xhl_gate_kernel(
         wx_pass(last, 2)
         table_pass(lo_w, lo_s, 2, stop=True)
         empty(2)
-        y.append(y_psum.tile([P, J], F32, name="y3", tag="y0"))
+        final = N_TILES - 1
+        y.append(y_psum.tile([P, J], F32, name=f"y{final}", tag="y0"))
         for i in range(len(x_operands)):
-            wx_pass(i, 3, start=(i == 0))
-        table_pass(hi_w, hi_s, 3)
-        table_pass(lo_w, lo_s, 3, stop=True)
-        empty(3)
+            wx_pass(i, final, start=(i == 0))
+        table_pass(hi_w, hi_s, final)
+        table_pass(lo_w, lo_s, final, stop=True)
+        empty(final)
 
         def gate_and_store(nt, first, width):
             result = keep.tile([P, width], F32, name=f"result{nt}_{first}")
@@ -326,8 +341,8 @@ def tile_list_tiert_xhl_gate_kernel(
             )
             nc.sync.dma_start(out[nt * P : (nt + 1) * P, first : first + width], result[:])
 
-        for nt in range(N_TILES - 1):
+        for nt in range(final):
             gate_and_store(nt, 0, J)
-        gate_and_store(N_TILES - 1, 0, J_HALF)
-        gate_and_store(N_TILES - 1, J_HALF, P)
-        gate_and_store(N_TILES - 1, J - P, P)
+        gate_and_store(final, 0, J_HALF)
+        gate_and_store(final, J_HALF, P)
+        gate_and_store(final, J - P, P)

from contextlib import ExitStack

import concourse.mybir as mybir

K, L, N, T, J = 512, 1024, 512, 1024, 512

F32 = mybir.dt.float32
BF16 = mybir.dt.bfloat16
I32 = mybir.dt.int32
U32 = mybir.dt.uint32
U16 = mybir.dt.uint16
U8 = mybir.dt.uint8
FP8X4 = mybir.dt.float8_e4m3fn_x4
FP4X4 = mybir.dt.float4_e2m1fn_x4
ALU = mybir.AluOpType

P = 128
PACK = 4
K_PASS = P * PACK
QUADRANTS = 4
X_PASSES = L // K_PASS
N_TILES = N // P
J_HALF = J // 2
N_HALF = N // 2
SCALE_ROWS = K_PASS // 32
LIST_ROWS = 16
BACK_BANKS = 4

FLOPS = 2 * J * (2 * K * N + 2 * L * N + L * K_PASS)

WARM_PASSES = 4

HI_MASK = -1048576
HI_MASK_PAIR = -983056
BF16_ONE = 0x3F80

ALIGN = 64
PIECE = P * PACK * 2
AT_V_ROWS = 0
AT_X_BF_HEAD = PIECE // 4 - ALIGN
AT_RAMP = AT_X_BF_HEAD + PIECE - ALIGN
AT_X_BF_FIRST = AT_RAMP + PIECE // 2 - ALIGN
AT_X_BF_THIRD = AT_X_BF_FIRST
AT_X_BF_FOURTH = AT_X_BF_FIRST + 3 * PIECE - ALIGN
AT_V_W = PIECE // 4
AT_UPPER = AT_V_W + 2 * PIECE
AT_LO_SECOND = AT_UPPER + 2 * PIECE
AT_LO_ROWS = (AT_LO_SECOND - PIECE // 2, AT_LO_SECOND + PIECE)
AT_HI_REST = AT_X_BF_FOURTH
AT_HI_SECOND = AT_HI_REST + PIECE
AT_LO_REST = AT_HI_SECOND + PIECE // 2
AT_X_RIGHT = AT_LO_REST + 2 * PIECE


def paired_rows(ap):
    return ap.rearrange("p t (c i) -> p c t i", i=2)


def paired_words(ap):
    return ap.rearrange("p (c i) t -> p c t i", i=2)


def tile_list_tiert_xhl_gate_kernel(
    tc, tab_words, tab_scales, wt, x, wx_words, wx_scales, gT, offs, out
):
    nc = tc.nc
    with ExitStack() as ctx:
        keep = ctx.enter_context(tc.tile_pool(name="keep", bufs=1))
        relay = ctx.enter_context(tc.tile_pool(name="relay", bufs=1))
        y_psum = ctx.enter_context(tc.psum_pool(name="y_psum", bufs=1))
        back_psum = ctx.enter_context(tc.psum_pool(name="back_psum", bufs=BACK_BANKS))

        def woven(name, width, tag):
            return keep.tile([P, width, PACK], BF16, name=name, tag=tag, align_bytes=ALIGN)

        def relayed(name, shape, dtype, offset):
            return relay.tile(shape, dtype, name=name, offset=offset, align_bytes=ALIGN)

        tab_s = keep.tile([P, T], U8, name="tab_s", align_bytes=ALIGN)
        nc.vector.memset(tab_s[: P - SCALE_ROWS, :].bitcast(I32), 0)
        v_s = keep.tile([P, J], U8, name="v_s", align_bytes=ALIGN)
        nc.vector.memset(v_s[:].bitcast(I32), 0)
        wx_s = keep.tile([P, X_PASSES, N], U8, name="wx_s", align_bytes=ALIGN)
        nc.vector.memset(wx_s[:].rearrange("p a n -> p (a n)").bitcast(I32), 0)

        ramp = relayed("ramp", [P, 2 * P], BF16, AT_RAMP)
        nc.gpsimd.iota(
            ramp[:], pattern=[[1, 2 * P]], base=0, channel_multiplier=-2, allow_small_or_imprecise_dtypes=True
        )
        id_w = keep.tile([P, K_PASS], U32, name="id_w", align_bytes=ALIGN)
        id_s = keep.tile([P, K_PASS], U8, name="id_s", align_bytes=ALIGN)
        ident = [keep.tile([P, 2, 2 * P], I32, name=f"ident{h}", tag=f"ident{h}", align_bytes=ALIGN) for h in range(2)]
        for t in range(PACK):
            one = float(BF16_ONE << (16 * (t % 2)))
            nc.vector.tensor_scalar(ident[t // 2][:, t % 2, :], ramp[:], float(t // 2), one, ALU.is_equal, ALU.mult)
        warm = keep.tile([P, 2], BF16, name="warm")
        nc.scalar.copy(warm[:], ramp[:, 0:2])
        for h in range(2):
            cols = slice(h * 2 * P, (h + 1) * 2 * P)
            nc.vector.quantize_mx(
                out=id_w[:, cols].bitcast(FP8X4),
                scales=id_s[:, cols],
                in_=ident[h][:].rearrange("p t f -> p (t f)").bitcast(BF16),
            )

        warm_sum = y_psum.tile([P, 2 * P], F32, name="warm_sum", tag="y0")
        for i in range(WARM_PASSES):
            nc.tensor.matmul_mx(
                out=warm_sum[:],
                lhsT=id_w[:, :P].bitcast(FP8X4),
                lhsT_scale=id_s[:, :P],
                rhs=id_w[:, : 2 * P].bitcast(FP8X4),
                rhs_scale=id_s[:, : 2 * P],
                start=True,
                stop=True,
            )

        def load_rows(name, source, first, width):
            raw = keep.tile([P, PACK, width], F32, name=name, tag=name, align_bytes=ALIGN)
            nc.sync.dma_start(raw[:], source[:, first : first + width].rearrange("(p t) j -> p t j", t=PACK))
            return raw

        x_first = load_rows("x_first", x[:K_PASS, :], 0, P)
        offsets = keep.tile([P, J // LIST_ROWS], U16, name="offsets")
        nc.sync.dma_start(offsets[:], offs)
        nc.sync.dma_start(tab_s[P - SCALE_ROWS :, :].bitcast(I32), tab_scales[0].bitcast(I32))
        x_second = load_rows("x_second", x[:K_PASS, :], P, P)
        x_right = relayed("x_right", [P, PACK, J_HALF], F32, AT_X_RIGHT)
        nc.sync.dma_start(x_right[:], x[:K_PASS, J_HALF:].rearrange("(p t) j -> p t j", t=PACK))
        x_last = load_rows("x_last", x[K_PASS:, :], 0, J)
        wt_left = load_rows("wt_left", wt, 0, N_HALF)
        for q in range(QUADRANTS):
            nc.sync.dma_start(
                wx_s[32 * q : 32 * q + 4, :, :].bitcast(I32),
                wx_scales[:, 4 * q : 4 * q + 4, :].rearrange("a r n -> r a n").bitcast(I32),
            )
        wx_w = keep.tile([P, X_PASSES, 2 * N], U8, name="wx_w", align_bytes=ALIGN)
        nc.sync.dma_start(wx_w[:].bitcast(I32), wx_words.rearrange("a p b -> p a b").bitcast(I32))
        tab_w = keep.tile([P, T], I32, name="tab_w", align_bytes=ALIGN)
        nc.sync.dma_start(tab_w[:], tab_words[0].rearrange("p t i -> p (t i)").bitcast(I32))
        wt_right = load_rows("wt_right", wt, N_HALF, N_HALF)

        xq_w = [keep.tile([P, J], U32, name="xq_w0", align_bytes=ALIGN)]
        xq_s = [keep.tile([P, J], U8, name=f"xq_s{a}", align_bytes=ALIGN) for a in range(X_PASSES)]
        xr_w = [keep.tile([P, J], U32, name=f"xr_w{a}", align_bytes=ALIGN) for a in range(X_PASSES)]
        xr_s = [keep.tile([P, J], U8, name=f"xr_s{a}", align_bytes=ALIGN) for a in range(X_PASSES)]
        back = {}

        def quantize(words, scales, first, values):
            cols = slice(first, first + values.shape[1])
            nc.vector.quantize_mx(
                out=words[:, cols].bitcast(FP8X4), scales=scales[:, cols], in_=values.rearrange("p j t -> p (j t)")
            )

        def first_tier(a, j0, rows, x_bf):
            nc.scalar.copy(paired_words(x_bf), paired_rows(rows))
            quantize(xq_w[a], xq_s[a], j0, x_bf)
            back[a, j0] = back_psum.tile([P, PACK, P], F32, name="back")
            for t in range(PACK):
                nc.tensor.matmul_mx(
                    out=back[a, j0][:, t, :],
                    lhsT=id_w[:, t * P : (t + 1) * P].bitcast(FP8X4),
                    lhsT_scale=id_s[:, t * P : (t + 1) * P],
                    rhs=xq_w[a][:, j0 : j0 + P].bitcast(FP8X4),
                    rhs_scale=xq_s[a][:, j0 : j0 + P],
                    start=True,
                    stop=True,
                )

        def left_over(a, j0, rows, rest):
            nc.vector.tensor_tensor(paired_words(rest), paired_rows(rows), paired_rows(back[a, j0][:]), ALU.subtract)

        def gather_scales(h, gathered):
            picks = offsets[:, h * J_HALF // LIST_ROWS : (h + 1) * J_HALF // LIST_ROWS]
            nc.vector.tensor_copy(gathered[:], tab_s[:].indirect(picks))
            return gathered

        v_rows = [gather_scales(0, keep.tile([P, J_HALF], U8, name="v_rows0", tag="ident1", align_bytes=ALIGN))]

        x_bf_head = relayed("x_bf_head", [P, P, PACK], BF16, AT_X_BF_HEAD)
        x_bf_first = relayed("x_bf_first", [P, J - P, PACK], BF16, AT_X_BF_FIRST)
        rest_left = woven("rest_left", J_HALF, "rest_left")
        rest_right = woven("rest_right", J_HALF, "rest_right")

        def first_rows(j0):
            if j0 < J_HALF:
                return (x_first, x_second)[j0 // P][:]
            return x_right[:, :, j0 - J_HALF : j0 - J_HALF + P]

        def first_rest(j0):
            half = rest_left if j0 < J_HALF else rest_right
            return half[:, j0 % J_HALF : j0 % J_HALF + P, :]

        first_tier(0, 0, first_rows(0), x_bf_head[:])
        v_rows.append(gather_scales(1, relayed("v_rows1", [P, J_HALF], U8, AT_V_ROWS)))
        for h in range(2):
            for q in range(QUADRANTS):
                rows_q = slice(P - SCALE_ROWS + 4 * q, P - SCALE_ROWS + 4 * q + 4)
                nc.sync.dma_start(
                    v_s[32 * q : 32 * q + 4, h * J_HALF : (h + 1) * J_HALF].bitcast(I32),
                    v_rows[h][rows_q, :].bitcast(I32),
                )
        gates = []
        for nt in range(N_TILES):
            g = keep.tile([P, T], F32, name=f"gate{nt}")
            nc.sync.dma_start(g[:], gT[nt * P : (nt + 1) * P, :])
            gates.append(g)

        first_tier(0, P, first_rows(P), x_bf_first[:, :P, :])
        for j0 in range(0, J_HALF, P):
            left_over(0, j0, first_rows(j0), first_rest(j0))
            first_tier(0, j0 + J_HALF, first_rows(j0 + J_HALF), x_bf_first[:, j0 + P : j0 + J_HALF, :])
        left_over(0, J_HALF, first_rows(J_HALF), first_rest(J_HALF))
        quantize(xr_w[0], xr_s[0], 0, rest_left[:])
        left_over(0, J - P, first_rows(J - P), first_rest(J - P))

        x_bf_left = woven("x_bf_left", J_HALF, "x_second")
        x_bf_third = relayed("x_bf_third", [P, P, PACK], BF16, AT_X_BF_THIRD)
        x_bf_fourth = relayed("x_bf_fourth", [P, P, PACK], BF16, AT_X_BF_FOURTH)
        xq_w.append(keep.tile([P, J], U32, name="xq_w1", tag="rest_left", align_bytes=ALIGN))
        first_tier(1, 0, x_last[:, :, :P], x_bf_left[:, :P, :])
        quantize(xr_w[0], xr_s[0], J_HALF, rest_right[:])
        first_tier(1, P, x_last[:, :, P:J_HALF], x_bf_left[:, P:, :])
        hi_rows = relayed("hi_rows", [P, PACK, N_HALF], I32, AT_X_RIGHT)
        nc.vector.tensor_scalar(hi_rows[:], wt_left[:].bitcast(I32), HI_MASK, None, ALU.bitwise_and)
        first_tier(1, J_HALF, x_last[:, :, J_HALF : J - P], x_bf_third[:])
        first_tier(1, J - P, x_last[:, :, J - P :], x_bf_fourth[:])

        rest_last = woven("rest_last", J, "x_second")
        lo_rows = []
        for nt in range(2):
            cols = slice(nt * P, (nt + 1) * P)
            rows = relayed(f"lo_rows{nt}", [P, PACK, P], BF16, AT_LO_ROWS[nt])
            nc.gpsimd.tensor_tensor(rows[:], wt_left[:, :, cols], hi_rows[:, :, cols].bitcast(F32), ALU.subtract)
            lo_rows.append(rows)
        for j0 in range(0, J, P):
            left_over(1, j0, x_last[:, :, j0 : j0 + P], rest_last[:, j0 : j0 + P, :])
        v_w = relayed("v_w", [P, J], U32, AT_V_W)
        nc.vector.tensor_copy(v_w[:], tab_w[:].bitcast(U32).indirect(offsets[:]))

        hi = woven("hi", N, "hi")
        lo_first = woven("lo_first", P, "lo_first")
        lo_second = relayed("lo_second", [P, P, PACK], BF16, AT_LO_SECOND)
        nc.scalar.copy(paired_words(hi[:, :N_HALF, :]), paired_rows(hi_rows[:].bitcast(F32)))
        nc.scalar.copy(paired_words(lo_first[:]), paired_rows(lo_rows[0][:]))
        upper = relayed("upper", [P, N_HALF, PACK], BF16, AT_UPPER)
        halves = wt_right[:].bitcast(BF16).rearrange("p t (n e) -> p t n e", e=2)
        nc.scalar.copy(paired_words(upper[:]), paired_rows(halves[:, :, :, 1]))
        nc.scalar.copy(paired_words(lo_second[:]), paired_rows(lo_rows[1][:]))

        hi_first = keep.tile([P, P], U32, name="hi_first", tag="x_last", align_bytes=ALIGN)
        hi_second = relayed("hi_second", [P, P], U32, AT_HI_SECOND)
        hi_rest = relayed("hi_rest", [P, N_HALF], U32, AT_HI_REST)
        hi_w = [hi_first[:], hi_second[:], hi_rest[:, :P], hi_rest[:, P:]]
        hi_s = keep.tile([P, N], U8, name="hi_s", align_bytes=ALIGN)
        lo_all = keep.tile([P, N], U32, name="lo_all", align_bytes=ALIGN)
        lo_w = [lo_all[:, P * nt : P * (nt + 1)] for nt in range(N_TILES)]
        lo_s = keep.tile([P, N], U8, name="lo_s", align_bytes=ALIGN)

        quantize(hi_first, hi_s[:, :P], 0, hi[:, :P, :])
        quantize(xr_w[1], xr_s[1], 0, rest_last[:, :J_HALF, :])
        quantize(lo_all, lo_s, 0, lo_first[:])
        quantize(xr_w[1], xr_s[1], J_HALF, rest_last[:, J_HALF:, :])
        nc.vector.tensor_scalar(
            hi[:, N_HALF:, :].rearrange("p n t -> p (n t)").bitcast(I32),
            upper[:].rearrange("p n t -> p (n t)").bitcast(I32),
            HI_MASK_PAIR,
            None,
            ALU.bitwise_and,
        )
        quantize(lo_all, lo_s, P, lo_second[:])
        quantize(hi_second, hi_s[:, P:N_HALF], 0, hi[:, P:N_HALF, :])
        lo_rest = relayed("lo_rest", [P, N_HALF, PACK], BF16, AT_LO_REST)
        nc.vector.tensor_tensor(
            paired_words(lo_rest[:]), paired_rows(wt_right[:]), paired_words(hi[:, N_HALF:, :]), ALU.subtract
        )
        quantize(hi_rest, hi_s[:, N_HALF:], 0, hi[:, N_HALF:, :])
        quantize(lo_all, lo_s, N_HALF, lo_rest[:])

        y = [y_psum.tile([P, J], F32, name=f"y{nt}", tag=f"y{nt}") for nt in range(N_TILES - 1)]
        x_operands = ((1, xq_w, xq_s), (0, xq_w, xq_s), (0, xr_w, xr_s), (1, xr_w, xr_s))
        last = len(x_operands) - 1

        def wx_pass(i, nt, start=False, stop=False):
            a, words, scales = x_operands[i]
            nc.tensor.matmul_mx(
                out=y[nt][:],
                lhsT=wx_w[:, a, 2 * P * nt : 2 * P * (nt + 1)].bitcast(FP4X4),
                lhsT_scale=wx_s[:, a, P * nt : P * (nt + 1)],
                rhs=words[a][:].bitcast(FP8X4),
                rhs_scale=scales[a][:],
                start=start,
                stop=stop,
            )

        def table_pass(words, scales, nt, stop=False):
            nc.tensor.matmul_mx(
                out=y[nt][:],
                lhsT=words[nt].bitcast(FP8X4),
                lhsT_scale=scales[:, P * nt : P * (nt + 1)],
                rhs=v_w[:].bitcast(FP8X4),
                rhs_scale=v_s[:],
                start=False,
                stop=stop,
            )

        sums = {}

        def empty(nt):
            sums[nt] = keep.tile([P, J], F32, name=f"sums{nt}")
            nc.scalar.copy(sums[nt][:], y[nt][:])

        for nt in range(N_TILES - 1):
            for i in range(last):
                wx_pass(i, nt, start=(i == 0))
        table_pass(hi_w, hi_s, 0)
        table_pass(lo_w, lo_s, 0)
        wx_pass(last, 0, stop=True)
        empty(0)
        table_pass(lo_w, lo_s, 1)
        table_pass(hi_w, hi_s, 1)
        wx_pass(last, 1, stop=True)
        empty(1)
        table_pass(hi_w, hi_s, 2)
        wx_pass(last, 2)
        table_pass(lo_w, lo_s, 2, stop=True)
        empty(2)
        final = N_TILES - 1
        y.append(y_psum.tile([P, J], F32, name=f"y{final}", tag="y0"))
        for i in range(len(x_operands)):
            wx_pass(i, final, start=(i == 0))
        table_pass(hi_w, hi_s, final)
        table_pass(lo_w, lo_s, final, stop=True)
        empty(final)

        def gate_and_store(nt, first, width):
            result = keep.tile([P, width], F32, name=f"result{nt}_{first}")
            picks = offsets[:, first // LIST_ROWS : (first + width) // LIST_ROWS]
            nc.vector.tensor_tensor(
                result[:], gates[nt][:].indirect(picks), sums[nt][:, first : first + width], ALU.mult
            )
            nc.sync.dma_start(out[nt * P : (nt + 1) * P, first : first + width], result[:])

        for nt in range(final):
            gate_and_store(nt, 0, J)
        gate_and_store(final, 0, J_HALF)
        gate_and_store(final, J_HALF, P)
        gate_and_store(final, J - P, P)
